import numpy as np
import ml_dtypes


def mxq(x, axis, fmt="e4m3"):
    dtype, down = {"e4m3": (ml_dtypes.float8_e4m3fn, 7), "e5m2": (ml_dtypes.float8_e5m2, 14)}[fmt]
    v = np.moveaxis(np.asarray(x, np.float32).astype(ml_dtypes.bfloat16).astype(np.float64), axis, -1)
    blocks = v.reshape(v.shape[:-1] + (-1, 32))
    amax = np.abs(blocks).max(-1, keepdims=True)
    byte = np.maximum(np.where(amax > 0, np.frexp(amax)[1] - 1 + 127, 0) - down, 1)
    scale = np.exp2(byte - 127.0)
    codes = (blocks / scale).astype(np.float32).astype(dtype).astype(np.float64)
    return np.moveaxis((codes * scale).reshape(v.shape), -1, axis)


WIDE = False


def mx_kscale(k):
    if not WIDE:
        return np.ones(k)
    levels = np.array([10, -10, 5, -5, 0])
    if k % 512:
        return np.exp2(np.random.permutation(np.resize(levels, k // 32))).repeat(32)
    a = np.empty((k // 512, 16))
    for p in range(k // 512):
        a[p, :8] = np.random.permutation(np.resize(levels, 8))
        for g in range(8):
            far = levels[np.abs(levels - a[p, g]) >= 10]
            a[p, g + 8] = far[np.random.randint(len(far))]
    return np.exp2(a.ravel()).repeat(32)


def f64(x):
    return np.asarray(x).astype(np.float64)


def striped(idx):
    return np.tile(idx.reshape(-1, 16).T, (8, 1)).astype(np.uint16)


def unstriped(offs):
    return offs[:16].T.reshape(-1).astype(np.int64)


E2M1 = np.array([0.0, 0.5, 1.0, 1.5, 2.0, 3.0, 4.0, 6.0, -0.0, -0.5, -1.0, -1.5, -2.0, -3.0, -4.0, -6.0])


def pack_weight(w, fmt):
    k, n = w.shape
    w = f64(np.asarray(w, np.float32).astype(ml_dtypes.bfloat16)).reshape(k // 32, 32, n)
    amax = np.abs(w).max(1)
    if fmt == "e4m3":
        byte = np.frexp(amax)[1] - 1 + 127 - 7
    else:
        mant, ex = np.frexp(amax / 6.0)
        byte = np.where(mant > 0.5, ex, ex - 1) + 127
    byte = np.clip(np.where(amax > 0, byte, 1), 1, 254)
    scaled = (w * np.exp2(127.0 - byte)[:, None, :]).reshape(k, n).astype(np.float32)
    by_word = np.ascontiguousarray(scaled.reshape(k // 512, 128, 4, n).transpose(0, 1, 3, 2))
    if fmt == "e4m3":
        words = by_word.astype(ml_dtypes.float8_e4m3fn).view(np.uint8)
    else:
        c = by_word.astype(ml_dtypes.float4_e2m1fn).view(np.uint8) & 0xF
        words = (c[..., 0::2] | (c[..., 1::2] << 4)).reshape(k // 512, 128, 2 * n)
    return np.ascontiguousarray(words), np.ascontiguousarray(byte.astype(np.uint8).reshape(k // 512, 16, n))


def unpack_weight(words, scales, fmt):
    g, _, n = scales.shape
    words = np.ascontiguousarray(words).reshape(g, 128, n, -1)
    if fmt == "e4m3":
        vals = words.view(ml_dtypes.float8_e4m3fn).astype(np.float64)
    else:
        nib = np.empty((g, 128, n, 4), np.uint8)
        nib[..., 0::2] = words & 0xF
        nib[..., 1::2] = words >> 4
        vals = E2M1[nib]
    vals = vals * np.repeat(np.exp2(scales.astype(np.float64) - 127.0), 8, axis=1)[..., None]
    return vals.transpose(0, 1, 3, 2).reshape(g * 512, n)


def gelu(v):
    return 0.5 * v * (1.0 + np.tanh(np.sqrt(2.0 / np.pi) * (v + 0.044715 * v**3)))


def bf(x):
    return np.asarray(x, np.float32).astype(ml_dtypes.bfloat16)


def planes(Y):
    n, m = Y.shape
    b = f64(bf(Y)).reshape(n // 32, 32, m)
    amax = np.abs(b).max(1)
    byte = np.clip(np.where(amax > 0, np.frexp(amax)[1] - 1 + 127 - 7, 1), 1, 254)
    codes = (b * np.exp2(127.0 - byte)[:, None, :]).reshape(n, m).astype(np.float32).astype(ml_dtypes.float8_e4m3fn).view(np.uint8)
    words = codes.reshape(n // 512, 128, 4, m).transpose(0, 1, 3, 2)
    return np.ascontiguousarray(words), np.ascontiguousarray(byte.astype(np.uint8).reshape(n // 512, 16, m))


K, T, S, T2, H, N = 1536, 2048, 512, 1024, 1024, 512


def setup_inputs():
    n = np.random.standard_normal
    s = mx_kscale(K)[:, None]
    u = mx_kscale(H)[:, None]
    tab_words, tab_scales = pack_weight(n((K, T)) * s, "e4m3")
    w1 = n((K, H)) / np.sqrt(K) / s
    amp = 1.5 * np.exp(0.3 * n(H)) * np.sign(n(H)) * u[:, 0]
    w2 = n((H, N)) / np.sqrt(H) / u
    w3_words, w3_scales = pack_weight(n((H, N)) / np.sqrt(H) / u, "e2m1")
    return {
        "tab_words": tab_words, "tab_scales": tab_scales,
        "offs": striped(np.random.permutation(T)[:S]),
        "offs2": striped(np.random.permutation(T2)[:S]),
        "w1": w1.astype(np.float32),
        "amp": amp.astype(np.float32),
        "wgs": np.exp(0.3 * n((128, S))).astype(np.float32),
        "page0": (n((H, T2)) * u).astype(np.float32),
        "w2": w2.astype(np.float32),
        "w3_words": w3_words, "w3_scales": w3_scales,
        "base": (0.5 * n((N, T2))).astype(np.float32),
    }


def reference(tab_words, tab_scales, offs, offs2, w1, amp, wgs, page0, w2, w3_words, w3_scales, base):
    v = unpack_weight(tab_words, tab_scales, "e4m3")[:, unstriped(offs)]
    a = mxq(f64(w1), 0, "e4m3").T @ v
    h = f64(amp)[:, None] / (1.0 + np.square(a))
    page = f64(page0).copy()
    page[:, unstriped(offs2)] = np.tile(f64(wgs), (H // 128, 1)) * h
    words, scales = planes(page)
    pq = mxq(page, 0, "e4m3")
    b = mxq(f64(w2), 0, "e4m3").T @ pq
    d = unpack_weight(w3_words, w3_scales, "e2m1").T @ pq
    y = b * np.tanh(d) + f64(base)
    return y, page, words, scales

@@ -1,0 +1,326 @@
+from contextlib import ExitStack
+
+import concourse.mybir as mybir
+from concourse.masks import make_identity
+
+K, T, S, T2, H, N = 1536, 2048, 512, 1024, 1024, 512
+FLOPS = 2 * K * H * S + 2 * 2 * H * N * T2
+
+F32 = mybir.dt.float32
+BF16 = mybir.dt.bfloat16
+I32 = mybir.dt.int32
+U32 = mybir.dt.uint32
+U16 = mybir.dt.uint16
+U8 = mybir.dt.uint8
+FP8X4 = mybir.dt.float8_e4m3fn_x4
+FP4X4 = mybir.dt.float4_e2m1fn_x4
+ACT = mybir.ActivationFunctionType
+MULT = mybir.AluOpType.mult
+ADD = mybir.AluOpType.add
+
+P = 128
+PACK = 4
+K_PASS = P * PACK
+KP = K // K_PASS
+HG = H // K_PASS
+HALF = T2 // 2
+NT = N // P
+
+
+def tile_list_furnace_zone_checkpoint_kernel(
+    tc, tab_words, tab_scales, offs, offs2, w1, amp, wgs, page0, w2, w3_words, w3_scales, base,
+    out_0, out_1, out_2, out_3,
+):
+    nc = tc.nc
+    with ExitStack() as ctx:
+        lists = ctx.enter_context(tc.tile_pool(name="lists", bufs=1))
+        keep = ctx.enter_context(tc.tile_pool(name="keep", bufs=1))
+        psum = ctx.enter_context(tc.psum_pool(name="psum", bufs=1))
+
+        def bank(b):
+            return psum.tile([P, 512], F32, name="bank%d" % b, tag="bank%d" % b)
+
+        def raw_tile(slot, shape, dtype, name):
+            return keep.tile(shape, dtype, name=name, tag="raw%d" % slot, align_bytes=64)
+
+        tab_sc = keep.tile([P, T], U8, name="tab_sc", align_bytes=64)
+        nc.vector.memset(tab_sc[:].bitcast(I32), 0)
+        ident = keep.tile([P, P], F32, name="ident")
+        make_identity(nc, ident[:])
+        amp_t = keep.tile([P, HG, PACK], F32, name="amp_t")
+        w3_sc = keep.tile([P, HG, N], U8, name="w3_sc", align_bytes=64)
+        nc.vector.memset(w3_sc[:].bitcast(I32), 0)
+        idx = lists.tile([P, S // 16], U16, name="idx")
+        idx2 = lists.tile([P, S // 16], U16, name="idx2")
+        wgs_t = keep.tile([P, S], F32, name="wgs_t")
+
+        w1_raw = {}
+        tab = []
+        page = {}
+        w2_raw = {}
+
+        def load_w1(g, a):
+            t = raw_tile(KP * g + a, [P, PACK, K_PASS], F32, "w1_raw%d%d" % (g, a))
+            rows = w1[a * K_PASS : (a + 1) * K_PASS, g * K_PASS : (g + 1) * K_PASS]
+            nc.sync.dma_start(out=t[:], in_=rows.rearrange("(p j) c -> p j c", j=PACK))
+            w1_raw[(g, a)] = t
+
+        def load_tab(a):
+            t = keep.tile([P, T], U32, name="tab%d" % a, align_bytes=64)
+            nc.sync.dma_start(out=t[:].bitcast(I32), in_=tab_words[a].rearrange("p n t -> p (n t)").bitcast(I32))
+            tab.append(t)
+
+        page0_v = page0.rearrange("(g p t) m -> g t p m", g=HG, t=PACK)
+        out1_v = out_1.rearrange("(g p t) m -> g t p m", g=HG, t=PACK)
+
+        def load_page(g, t):
+            tl = keep.tile([P, T2], F32, name="page%d%d" % (g, t))
+            nc.sync.dma_start(out=tl[:], in_=page0_v[g, t])
+            page[(g, t)] = tl
+
+        def load_w2(g, slot):
+            t = raw_tile(slot, [P, PACK, N], F32, "w2_raw%d" % g)
+            nc.sync.dma_start(out=t[:], in_=w2[g * K_PASS : (g + 1) * K_PASS, :].rearrange("(p j) c -> p j c", j=PACK))
+            w2_raw[g] = t
+
+        nc.sync.dma_start(out=wgs_t[:], in_=wgs)
+        nc.sync.dma_start(idx[:], offs)
+        load_w1(0, 0)
+        nc.sync.dma_start(out=amp_t[:], in_=amp.rearrange("(g p t) -> p g t", g=HG, t=PACK))
+        load_tab(0)
+        for q in range(4):
+            nc.sync.dma_start(
+                out=tab_sc[32 * q : 32 * q + 4 * KP, :].bitcast(I32),
+                in_=tab_scales[:, 4 * q : 4 * q + 4, :].bitcast(I32),
+            )
+        nc.sync.dma_start(idx2[:], offs2)
+        for a in range(1, KP):
+            load_w1(0, a)
+            load_tab(a)
+        for a in range(KP):
+            load_page(0, a)
+            load_w1(1, a)
+
+        warm = keep.tile([P, 1], F32, name="warm")
+        nc.scalar.activation(out=warm[:], in_=ident[:, 0:1], func=ACT.Abs_reciprocal_sqrt, bias=1.0)
+
+        wgs_T = bank(4)
+        for jb in range(4):
+            nc.tensor.transpose(wgs_T[:, jb * P : (jb + 1) * P], wgs_t[:, jb * P : (jb + 1) * P], ident[:])
+        dealt = raw_tile(6, [P, 4, PACK, 4, 32], F32, "dealt")
+        for q in range(4):
+            nc.scalar.copy(out=dealt[:, :, :, q, :], in_=wgs_T[:].rearrange("j (b p t) -> j b t p", b=4, t=PACK))
+        wa = {}
+        for t in range(PACK):
+            back = bank(4 + (t + 1) % 4)
+            for jb in range(4):
+                nc.tensor.transpose(
+                    back[:, jb * P : (jb + 1) * P], dealt[:, jb, t, :, :].rearrange("j q p -> j (q p)"), ident[:]
+                )
+            for g in range(HG):
+                wa[(g, t)] = keep.tile([P, S], F32, name="wa%d%d" % (g, t))
+                nc.scalar.activation(out=wa[(g, t)][:], in_=back[:], func=ACT.Copy, scale=amp_t[:, g, t : t + 1])
+
+        def copy_on(eng, out, in_):
+            if eng == "v":
+                nc.vector.tensor_copy(out=out, in_=in_)
+            else:
+                nc.scalar.copy(out=out, in_=in_)
+
+        def grouped_tile():
+            return keep.tile([P, 4 * 512], BF16, name="grouped", tag="grouped", bufs=3, align_bytes=64)
+
+        def cast_w1(g, a, mv):
+            gr = grouped_tile()
+            dst = gr[:].rearrange("p (t m j) -> p m j t", t=PACK, j=PACK)
+            src = w1_raw[(g, a)][:].rearrange("p j (m t) -> p m j t", t=PACK)
+            if mv > 0:
+                copy_on("v", dst[:, 0:mv], src[:, 0:mv])
+            if mv < P:
+                copy_on("s", dst[:, mv:P], src[:, mv:P])
+            return gr
+
+        def cast_w2(g, cv):
+            gr = grouped_tile()
+            dst = gr[:].rearrange("p (c i j) -> p c j i", i=4, j=PACK)
+            src = w2_raw[g][:].rearrange("p j (c i) -> p c j i", i=4)
+            if cv > 0:
+                copy_on("v", dst[:, 0:cv], src[:, 0:cv])
+            if cv < P:
+                copy_on("s", dst[:, cv:P], src[:, cv:P])
+            return gr
+
+        def quant(gr, name):
+            codes = keep.tile([P, 512], U32, name=name + "_c", align_bytes=64)
+            scales = keep.tile([P, 512], U8, name=name + "_s", align_bytes=64)
+            nc.vector.quantize_mx(out=codes[:].bitcast(FP8X4), scales=scales[:], in_=gr[:])
+            return codes, scales
+
+        v_sc = keep.tile([P, S], U8, name="v_sc", align_bytes=64)
+        v_w = []
+        acc = {}
+
+        def stage1_pass(g, a, wq):
+            for t in range(PACK):
+                if a == 0:
+                    acc[(g, t)] = bank(PACK * g + t)
+                nc.tensor.matmul_mx(
+                    out=acc[(g, t)][:],
+                    lhsT=wq[0][:, t * P : (t + 1) * P].bitcast(FP8X4),
+                    lhsT_scale=wq[1][:, t * P : (t + 1) * P],
+                    rhs=v_w[a][:].bitcast(FP8X4),
+                    rhs_scale=v_sc[4 * a : P, :],
+                    start=(a == 0),
+                    stop=(a == KP - 1),
+                )
+
+        for a in range(KP):
+            wq = quant(cast_w1(0, a, P), "w1q0%d" % a)
+            if a == 0:
+                nc.vector.tensor_copy(out=v_sc[:], in_=tab_sc[:].indirect(idx[:]))
+            vw = keep.tile([P, S], U32, name="v_w%d" % a, align_bytes=64)
+            nc.vector.tensor_copy(out=vw[:], in_=tab[a][:].indirect(idx[:]))
+            v_w.append(vw)
+            stage1_pass(0, a, wq)
+
+        load_w2(0, 6)
+        load_page(0, 3)
+        load_w2(1, 0)
+        w3_w = keep.tile([P, HG, 2 * N], U8, name="w3_w", align_bytes=64)
+        nc.sync.dma_start(out=w3_w[:].bitcast(I32), in_=w3_words.bitcast(I32).rearrange("g p c -> p g c"))
+        for q in range(4):
+            nc.sync.dma_start(
+                out=w3_sc[32 * q : 32 * q + 4, :, :].bitcast(I32),
+                in_=w3_scales[:, 4 * q : 4 * q + 4, :].bitcast(I32).rearrange("g r c -> r g c"),
+            )
+        for t in range(PACK - 1):
+            load_page(1, t)
+        base_t = []
+        for nt in range(NT):
+            bt = keep.tile([P, T2], F32, name="base%d" % nt)
+            nc.sync.dma_start(out=bt[:], in_=base[nt * P : (nt + 1) * P, :])
+            base_t.append(bt)
+        load_page(1, PACK - 1)
+
+        def respond(g, t):
+            us = keep.tile([P, S], F32, name="us", tag="us", bufs=2)
+            nc.scalar.activation(out=us[:], in_=acc[(g, t)][:], func=ACT.Square)
+            nc.scalar.activation(out=us[:], in_=us[:], func=ACT.Abs_reciprocal_sqrt, bias=1.0)
+            h = keep.tile([P, S], F32, name="h", tag="h", bufs=4)
+            nc.scalar.activation(out=h[:], in_=us[:], func=ACT.Square)
+            nc.vector.tensor_tensor(page[(g, t)][:].indirect(idx2[:]), h[:], wa[(g, t)][:], MULT)
+            nc.sync.dma_start(out=out1_v[g, t], in_=page[(g, t)][:])
+
+        respond(0, 0)
+        respond(0, 1)
+        stage1_pass(1, 0, quant(cast_w1(1, 0, 0), "w1q10"))
+        respond(0, 2)
+        stage1_pass(1, 1, quant(cast_w1(1, 1, 0), "w1q11"))
+        stage1_pass(1, 2, quant(cast_w1(1, 2, 64), "w1q12"))
+        respond(0, 3)
+
+        pairs0 = raw_tile(5, [P, 2, T2, 2], BF16, "pairs0")
+        pairs1 = [raw_tile(1 + hf, [P, 2, HALF, 2], BF16, "pairs1%d" % hf) for hf in range(2)]
+        pq_c = [keep.tile([P, T2], U32, name="pq_c%d" % g, align_bytes=64) for g in range(HG)]
+        pq_s = keep.tile([P, HG, T2], U8, name="pq_s", align_bytes=64)
+
+        def round0(t):
+            copy_on("s", pairs0[:, t // 2, :, t % 2], page[(0, t)][:])
+
+        def round1(eng, t, hf):
+            copy_on(eng, pairs1[hf][:, t // 2, :, t % 2], page[(1, t)][:, hf * HALF : (hf + 1) * HALF])
+
+        def weave(words):
+            gr = grouped_tile()
+            nc.vector.tensor_copy(
+                out=gr[:].bitcast(F32).rearrange("p (m u) -> p m u", u=2), in_=words.rearrange("p u m -> p m u")
+            )
+            return gr
+
+        def quant_page(g, hf, gr):
+            cols = slice(hf * HALF, (hf + 1) * HALF)
+            nc.vector.quantize_mx(out=pq_c[g][:, cols].bitcast(FP8X4), scales=pq_s[:, g, cols], in_=gr[:])
+
+        respond(1, 0)
+        respond(1, 1)
+        round0(0)
+        round0(1)
+        respond(1, 2)
+        round0(2)
+        round0(3)
+        words0 = pairs0[:].rearrange("p u m e -> p u (m e)").bitcast(F32)
+        g00 = weave(words0[:, :, 0:HALF])
+        g01 = weave(words0[:, :, HALF:T2])
+        quant_page(0, 0, g00)
+        quant_page(0, 1, g01)
+        nc.sync.dma_start(
+            out=out_2[0].rearrange("p m t -> p (m t)").bitcast(I32), in_=pq_c[0][:].bitcast(I32)
+        )
+        round1("v", 2, 0)
+        round1("v", 2, 1)
+        respond(1, 3)
+        w2q = [quant(cast_w2(g, 0), "w2q%d" % g) for g in range(HG)]
+        for t in range(2):
+            for hf in range(2):
+                round1("s", t, hf)
+
+        acc2 = {}
+
+        def stage2_pass(g, hf, nt):
+            cols = slice(hf * HALF, (hf + 1) * HALF)
+            if g == 0:
+                acc2[(hf, nt)] = (bank(2 * nt), bank(2 * nt + 1))
+            d_acc, b_acc = acc2[(hf, nt)]
+            nc.tensor.matmul_mx(
+                out=d_acc[:],
+                lhsT=w3_w[:, g, 2 * nt * P : 2 * (nt + 1) * P].bitcast(FP4X4),
+                lhsT_scale=w3_sc[:, g, nt * P : (nt + 1) * P],
+                rhs=pq_c[g][:, cols].bitcast(FP8X4),
+                rhs_scale=pq_s[:, g, cols],
+                start=(g == 0),
+                stop=(g == HG - 1),
+            )
+            nc.tensor.matmul_mx(
+                out=b_acc[:],
+                lhsT=w2q[g][0][:, nt * P : (nt + 1) * P].bitcast(FP8X4),
+                lhsT_scale=w2q[g][1][:, nt * P : (nt + 1) * P],
+                rhs=pq_c[g][:, cols].bitcast(FP8X4),
+                rhs_scale=pq_s[:, g, cols],
+                start=(g == 0),
+                stop=(g == HG - 1),
+            )
+
+        def finish(hf, nt):
+            cols = slice(hf * HALF, (hf + 1) * HALF)
+            d_acc, b_acc = acc2[(hf, nt)]
+            th = keep.tile([P, HALF], F32, name="th", tag="th", bufs=3)
+            nc.scalar.activation(out=th[:], in_=d_acc[:], func=ACT.Tanh)
+            nc.vector.tensor_tensor(th[:], b_acc[:], th[:], MULT)
+            nc.vector.tensor_tensor(base_t[nt][:, cols], th[:], base_t[nt][:, cols], ADD)
+            nc.sync.dma_start(out=out_0[nt * P : (nt + 1) * P, cols], in_=base_t[nt][:, cols])
+
+        for nt in range(NT):
+            stage2_pass(0, 0, nt)
+        grs = []
+        for hf in range(2):
+            round1("v", 3, hf)
+        for hf in range(2):
+            grs.append(weave(pairs1[hf][:].rearrange("p u m e -> p u (m e)").bitcast(F32)))
+        for hf in range(2):
+            quant_page(1, hf, grs[hf])
+        nc.sync.dma_start(
+            out=out_2[1].rearrange("p m t -> p (m t)").bitcast(I32), in_=pq_c[1][:].bitcast(I32)
+        )
+        for q in range(4):
+            nc.sync.dma_start(
+                out=out_3[:, 4 * q : 4 * q + 4, :].bitcast(I32).rearrange("g r m -> r g m"),
+                in_=pq_s[32 * q : 32 * q + 4, :, :].bitcast(I32),
+            )
+        for nt in range(NT):
+            stage2_pass(1, 0, nt)
+        for nt in range(NT):
+            finish(0, nt)
+            stage2_pass(0, 1, nt)
+            stage2_pass(1, 1, nt)
+        for nt in range(NT):
+            finish(1, nt)

@@ -44,7 +44,7 @@ def tile_list_furnace_zone_checkpoint_kernel(
             return keep.tile(shape, dtype, name=name, tag="raw%d" % slot, align_bytes=64)
 
         tab_sc = keep.tile([P, T], U8, name="tab_sc", align_bytes=64)
-        nc.vector.memset(tab_sc[:].bitcast(I32), 0)
+        nc.gpsimd.memset(tab_sc[:].bitcast(I32), 0)
         ident = keep.tile([P, P], F32, name="ident")
         make_identity(nc, ident[:])
         amp_t = keep.tile([P, HG, PACK], F32, name="amp_t")
@@ -59,15 +59,20 @@ def tile_list_furnace_zone_checkpoint_kernel(
         page = {}
         w2_raw = {}
 
-        def load_w1(g, a):
+        def load_w1(g, a, parts=1):
             t = raw_tile(KP * g + a, [P, PACK, K_PASS], F32, "w1_raw%d%d" % (g, a))
             rows = w1[a * K_PASS : (a + 1) * K_PASS, g * K_PASS : (g + 1) * K_PASS]
-            nc.sync.dma_start(out=t[:], in_=rows.rearrange("(p j) c -> p j c", j=PACK))
+            step = PACK // parts
+            for j in range(0, PACK, step):
+                nc.sync.dma_start(out=t[:, j : j + step, :], in_=rows.rearrange("(p j) c -> p j c", j=PACK)[:, j : j + step, :])
             w1_raw[(g, a)] = t
 
-        def load_tab(a):
+        def load_tab(a, parts=1):
             t = keep.tile([P, T], U32, name="tab%d" % a, align_bytes=64)
-            nc.sync.dma_start(out=t[:].bitcast(I32), in_=tab_words[a].rearrange("p n t -> p (n t)").bitcast(I32))
+            words = tab_words[a].rearrange("p n t -> p (n t)").bitcast(I32)
+            step = T // parts
+            for c in range(0, T, step):
+                nc.sync.dma_start(out=t[:, c : c + step].bitcast(I32), in_=words[:, c : c + step])
             tab.append(t)
 
         page0_v = page0.rearrange("(g p t) m -> g t p m", g=HG, t=PACK)
@@ -85,21 +90,24 @@ def tile_list_furnace_zone_checkpoint_kernel(
 
         nc.sync.dma_start(out=wgs_t[:], in_=wgs)
         nc.sync.dma_start(idx[:], offs)
-        load_w1(0, 0)
+        nc.sync.dma_start(idx2[:], offs2)
         nc.sync.dma_start(out=amp_t[:], in_=amp.rearrange("(g p t) -> p g t", g=HG, t=PACK))
-        load_tab(0)
         for q in range(4):
-            nc.sync.dma_start(
+            nc.scalar.dma_start(
                 out=tab_sc[32 * q : 32 * q + 4 * KP, :].bitcast(I32),
                 in_=tab_scales[:, 4 * q : 4 * q + 4, :].bitcast(I32),
             )
-        nc.sync.dma_start(idx2[:], offs2)
+        load_w1(0, 0, 2)
+        load_tab(0, 2)
         for a in range(1, KP):
             load_w1(0, a)
             load_tab(a)
-        for a in range(KP):
-            load_page(0, a)
-            load_w1(1, a)
+        load_page(0, 0)
+        load_w1(1, 0)
+        load_page(0, 1)
+        load_w1(1, 1)
+        load_w1(1, 2)
+        load_page(0, 2)
 
         warm = keep.tile([P, 1], F32, name="warm")
         nc.scalar.activation(out=warm[:], in_=ident[:, 0:1], func=ACT.Abs_reciprocal_sqrt, bias=1.0)
@@ -130,8 +138,7 @@ def tile_list_furnace_zone_checkpoint_kernel(
         def grouped_tile():
             return keep.tile([P, 4 * 512], BF16, name="grouped", tag="grouped", bufs=3, align_bytes=64)
 
-        def cast_w1(g, a, mv):
-            gr = grouped_tile()
+        def cast_w1(g, a, mv, gr):
             dst = gr[:].rearrange("p (t m j) -> p m j t", t=PACK, j=PACK)
             src = w1_raw[(g, a)][:].rearrange("p j (m t) -> p m j t", t=PACK)
             if mv > 0:
@@ -140,8 +147,7 @@ def tile_list_furnace_zone_checkpoint_kernel(
                 copy_on("s", dst[:, mv:P], src[:, mv:P])
             return gr
 
-        def cast_w2(g, cv):
-            gr = grouped_tile()
+        def cast_w2(g, cv, gr):
             dst = gr[:].rearrange("p (c i j) -> p c j i", i=4, j=PACK)
             src = w2_raw[g][:].rearrange("p j (c i) -> p c j i", i=4)
             if cv > 0:
@@ -160,22 +166,25 @@ def tile_list_furnace_zone_checkpoint_kernel(
         v_w = []
         acc = {}
 
+        def stage1_one(g, a, t, wq):
+            if a == 0:
+                acc[(g, t)] = bank(PACK * g + t)
+            nc.tensor.matmul_mx(
+                out=acc[(g, t)][:],
+                lhsT=wq[0][:, t * P : (t + 1) * P].bitcast(FP8X4),
+                lhsT_scale=wq[1][:, t * P : (t + 1) * P],
+                rhs=v_w[a][:].bitcast(FP8X4),
+                rhs_scale=v_sc[4 * a : P, :],
+                start=(a == 0),
+                stop=(a == KP - 1),
+            )
+
         def stage1_pass(g, a, wq):
             for t in range(PACK):
-                if a == 0:
-                    acc[(g, t)] = bank(PACK * g + t)
-                nc.tensor.matmul_mx(
-                    out=acc[(g, t)][:],
-                    lhsT=wq[0][:, t * P : (t + 1) * P].bitcast(FP8X4),
-                    lhsT_scale=wq[1][:, t * P : (t + 1) * P],
-                    rhs=v_w[a][:].bitcast(FP8X4),
-                    rhs_scale=v_sc[4 * a : P, :],
-                    start=(a == 0),
-                    stop=(a == KP - 1),
-                )
+                stage1_one(g, a, t, wq)
 
         for a in range(KP):
-            wq = quant(cast_w1(0, a, P), "w1q0%d" % a)
+            wq = quant(cast_w1(0, a, P, grouped_tile()), "w1q0%d" % a)
             if a == 0:
                 nc.vector.tensor_copy(out=v_sc[:], in_=tab_sc[:].indirect(idx[:]))
             vw = keep.tile([P, S], U32, name="v_w%d" % a, align_bytes=64)
@@ -202,24 +211,38 @@ def tile_list_furnace_zone_checkpoint_kernel(
             base_t.append(bt)
         load_page(1, PACK - 1)
 
-        def respond(g, t):
-            us = keep.tile([P, S], F32, name="us", tag="us", bufs=2)
-            nc.scalar.activation(out=us[:], in_=acc[(g, t)][:], func=ACT.Square)
-            nc.scalar.activation(out=us[:], in_=us[:], func=ACT.Abs_reciprocal_sqrt, bias=1.0)
-            h = keep.tile([P, S], F32, name="h", tag="h", bufs=4)
-            nc.scalar.activation(out=h[:], in_=us[:], func=ACT.Square)
-            nc.vector.tensor_tensor(page[(g, t)][:].indirect(idx2[:]), h[:], wa[(g, t)][:], MULT)
-            nc.sync.dma_start(out=out1_v[g, t], in_=page[(g, t)][:])
+        def scratch():
+            return keep.tile([P, S], F32, name="us", tag="us", bufs=2)
 
-        respond(0, 0)
-        respond(0, 1)
-        stage1_pass(1, 0, quant(cast_w1(1, 0, 0), "w1q10"))
-        respond(0, 2)
-        stage1_pass(1, 1, quant(cast_w1(1, 1, 0), "w1q11"))
-        stage1_pass(1, 2, quant(cast_w1(1, 2, 64), "w1q12"))
-        respond(0, 3)
+        def respond(g, t, us_t, h=None, parts=1):
+            if h is None:
+                h = keep.tile([P, S], F32, name="h", tag="h", bufs=4)
+            w = S // parts
+            for c in range(0, S, w):
+                us = us_t[:, c : c + w]
+                nc.scalar.activation(out=us, in_=acc[(g, t)][:, c : c + w], func=ACT.Square)
+                nc.scalar.activation(out=us, in_=us, func=ACT.Abs_reciprocal_sqrt, bias=1.0)
+                nc.scalar.activation(out=h[:, c : c + w], in_=us, func=ACT.Square)
+                nc.vector.tensor_tensor(
+                    page[(g, t)][:].indirect(idx2[:, c // 16 : (c + w) // 16]), h[:, c : c + w], wa[(g, t)][:, c : c + w], MULT
+                )
+            queue = nc.sync if (g, t) == (1, 3) else nc.gpsimd
+            queue.dma_start(out=out1_v[g, t], in_=page[(g, t)][:])
 
-        pairs0 = raw_tile(5, [P, 2, T2, 2], BF16, "pairs0")
+        respond(0, 0, scratch(), None, 2)
+        respond(0, 1, raw_tile(7, [P, S], F32, "us01"))
+        stage1_pass(1, 0, quant(cast_w1(1, 0, 0, raw_tile(7, [P, 2048], BF16, "gr10")), "w1q10"))
+        gr11 = cast_w1(1, 1, 0, grouped_tile())
+        gr12 = cast_w1(1, 2, P, grouped_tile())
+        late = [quant(gr11, "w1q11"), quant(gr12, "w1q12")]
+        for t in range(PACK):
+            stage1_one(1, 1, t, late[0])
+            stage1_one(1, 2, t, late[1])
+        respond(0, 2, scratch(), raw_tile(5, [P, S], F32, "h02"))
+        respond(0, 3, scratch())
+
+        pairs0 = raw_tile(4, [P, 2, T2, 2], BF16, "pairs0")
+        words0 = pairs0[:].rearrange("p u m e -> p u (m e)").bitcast(F32)
         pairs1 = [raw_tile(1 + hf, [P, 2, HALF, 2], BF16, "pairs1%d" % hf) for hf in range(2)]
         pq_c = [keep.tile([P, T2], U32, name="pq_c%d" % g, align_bytes=64) for g in range(HG)]
         pq_s = keep.tile([P, HG, T2], U8, name="pq_s", align_bytes=64)
@@ -241,14 +264,15 @@ def tile_list_furnace_zone_checkpoint_kernel(
             cols = slice(hf * HALF, (hf + 1) * HALF)
             nc.vector.quantize_mx(out=pq_c[g][:, cols].bitcast(FP8X4), scales=pq_s[:, g, cols], in_=gr[:])
 
-        respond(1, 0)
-        respond(1, 1)
         round0(0)
         round0(1)
-        respond(1, 2)
+        respond(1, 0, words0[:, 1, 0:S])
+        respond(1, 1, raw_tile(8, [P, S], F32, "us11"))
+        respond(1, 2, scratch())
+        w2q = [quant(cast_w2(0, 0, raw_tile(8, [P, 2048], BF16, "grw20")), "w2q0")]
         round0(2)
         round0(3)
-        words0 = pairs0[:].rearrange("p u m e -> p u (m e)").bitcast(F32)
+        round1("v", 2, 0)
         g00 = weave(words0[:, :, 0:HALF])
         g01 = weave(words0[:, :, HALF:T2])
         quant_page(0, 0, g00)
@@ -256,13 +280,12 @@ def tile_list_furnace_zone_checkpoint_kernel(
         nc.sync.dma_start(
             out=out_2[0].rearrange("p m t -> p (m t)").bitcast(I32), in_=pq_c[0][:].bitcast(I32)
         )
-        round1("v", 2, 0)
-        round1("v", 2, 1)
-        respond(1, 3)
-        w2q = [quant(cast_w2(g, 0), "w2q%d" % g) for g in range(HG)]
+        w2q.append(quant(cast_w2(1, 0, grouped_tile()), "w2q1"))
+        respond(1, 3, scratch(), raw_tile(4, [P, S], F32, "h13"))
         for t in range(2):
             for hf in range(2):
                 round1("s", t, hf)
+        round1("s", 2, 1)
 
         acc2 = {}
 
@@ -293,17 +316,18 @@ def tile_list_furnace_zone_checkpoint_kernel(
         def finish(hf, nt):
             cols = slice(hf * HALF, (hf + 1) * HALF)
             d_acc, b_acc = acc2[(hf, nt)]
-            th = keep.tile([P, HALF], F32, name="th", tag="th", bufs=3)
+            th = keep.tile([P, HALF], F32, name="th", tag="th", bufs=4)
             nc.scalar.activation(out=th[:], in_=d_acc[:], func=ACT.Tanh)
             nc.vector.tensor_tensor(th[:], b_acc[:], th[:], MULT)
-            nc.vector.tensor_tensor(base_t[nt][:, cols], th[:], base_t[nt][:, cols], ADD)
+            adder = nc.gpsimd if (NT * hf + nt) in (0, 1, 3, 4, 6) else nc.vector
+            adder.tensor_tensor(base_t[nt][:, cols], th[:], base_t[nt][:, cols], ADD)
             nc.sync.dma_start(out=out_0[nt * P : (nt + 1) * P, cols], in_=base_t[nt][:, cols])
 
         for nt in range(NT):
             stage2_pass(0, 0, nt)
         grs = []
-        for hf in range(2):
-            round1("v", 3, hf)
+        round1("v", 3, 0)
+        round1("s", 3, 1)
         for hf in range(2):
             grs.append(weave(pairs1[hf][:].rearrange("p u m e -> p u (m e)").bitcast(F32)))
         for hf in range(2):

@@ -112,7 +112,7 @@ def tile_list_furnace_zone_checkpoint_kernel(
         warm = keep.tile([P, 1], F32, name="warm")
         nc.scalar.activation(out=warm[:], in_=ident[:, 0:1], func=ACT.Abs_reciprocal_sqrt, bias=1.0)
 
-        wgs_T = bank(4)
+        wgs_T = bank(5)
         for jb in range(4):
             nc.tensor.transpose(wgs_T[:, jb * P : (jb + 1) * P], wgs_t[:, jb * P : (jb + 1) * P], ident[:])
         dealt = raw_tile(6, [P, 4, PACK, 4, 32], F32, "dealt")
@@ -120,7 +120,7 @@ def tile_list_furnace_zone_checkpoint_kernel(
             nc.scalar.copy(out=dealt[:, :, :, q, :], in_=wgs_T[:].rearrange("j (b p t) -> j b t p", b=4, t=PACK))
         wa = {}
         for t in range(PACK):
-            back = bank(4 + (t + 1) % 4)
+            back = bank(5 + (t + 1) % 3)
             for jb in range(4):
                 nc.tensor.transpose(
                     back[:, jb * P : (jb + 1) * P], dealt[:, jb, t, :, :].rearrange("j q p -> j (q p)"), ident[:]
@@ -166,18 +166,29 @@ def tile_list_furnace_zone_checkpoint_kernel(
         v_w = []
         acc = {}
 
-        def stage1_one(g, a, t, wq):
-            if a == 0:
-                acc[(g, t)] = bank(PACK * g + t)
+        def stage1_mm(out, a, t, wq, cols):
             nc.tensor.matmul_mx(
-                out=acc[(g, t)][:],
+                out=out,
                 lhsT=wq[0][:, t * P : (t + 1) * P].bitcast(FP8X4),
                 lhsT_scale=wq[1][:, t * P : (t + 1) * P],
-                rhs=v_w[a][:].bitcast(FP8X4),
-                rhs_scale=v_sc[4 * a : P, :],
+                rhs=v_w[a][:, cols].bitcast(FP8X4),
+                rhs_scale=v_sc[4 * a : P, cols],
                 start=(a == 0),
                 stop=(a == KP - 1),
             )
+
+        halves = [slice(0, S // 2), slice(S // 2, S)]
+        offs_halves = [slice(0, S // 32), slice(S // 32, S // 16)]
+        acc00 = [bank(0), bank(4)]
+
+        def stage1_one(g, a, t, wq):
+            if (g, t) == (0, 0):
+                for hf in range(2):
+                    stage1_mm(acc00[hf][:, 0 : S // 2], a, t, wq, halves[hf])
+                return
+            if a == 0:
+                acc[(g, t)] = bank(PACK * g + t)
+            stage1_mm(acc[(g, t)][:], a, t, wq, slice(0, S))
 
         def stage1_pass(g, a, wq):
             for t in range(PACK):
@@ -188,7 +199,11 @@ def tile_list_furnace_zone_checkpoint_kernel(
             if a == 0:
                 nc.vector.tensor_copy(out=v_sc[:], in_=tab_sc[:].indirect(idx[:]))
             vw = keep.tile([P, S], U32, name="v_w%d" % a, align_bytes=64)
-            nc.vector.tensor_copy(out=vw[:], in_=tab[a][:].indirect(idx[:]))
+            if a < KP - 1:
+                nc.vector.tensor_copy(out=vw[:], in_=tab[a][:].indirect(idx[:]))
+            else:
+                for hf in range(2):
+                    nc.vector.tensor_copy(out=vw[:, halves[hf]], in_=tab[a][:].indirect(idx[:, offs_halves[hf]]))
             v_w.append(vw)
             stage1_pass(0, a, wq)
 
@@ -214,26 +229,40 @@ def tile_list_furnace_zone_checkpoint_kernel(
         def scratch():
             return keep.tile([P, S], F32, name="us", tag="us", bufs=2)
 
-        def respond(g, t, us_t, h=None, parts=1):
-            if h is None:
-                h = keep.tile([P, S], F32, name="h", tag="h", bufs=4)
-            w = S // parts
-            for c in range(0, S, w):
-                us = us_t[:, c : c + w]
-                nc.scalar.activation(out=us, in_=acc[(g, t)][:, c : c + w], func=ACT.Square)
-                nc.scalar.activation(out=us, in_=us, func=ACT.Abs_reciprocal_sqrt, bias=1.0)
-                nc.scalar.activation(out=h[:, c : c + w], in_=us, func=ACT.Square)
-                nc.vector.tensor_tensor(
-                    page[(g, t)][:].indirect(idx2[:, c // 16 : (c + w) // 16]), h[:, c : c + w], wa[(g, t)][:, c : c + w], MULT
-                )
+        def resonance(src, us, h):
+            nc.scalar.activation(out=us, in_=src, func=ACT.Square)
+            nc.scalar.activation(out=us, in_=us, func=ACT.Abs_reciprocal_sqrt, bias=1.0)
+            nc.scalar.activation(out=h, in_=us, func=ACT.Square)
+
+        def store_page(g, t):
             queue = nc.sync if (g, t) == (1, 3) else nc.gpsimd
             queue.dma_start(out=out1_v[g, t], in_=page[(g, t)][:])
 
-        respond(0, 0, scratch(), None, 2)
-        respond(0, 1, raw_tile(7, [P, S], F32, "us01"))
+        def h_tile():
+            return keep.tile([P, S], F32, name="h", tag="h", bufs=4)
+
+        def scatter_half(g, t, hf, h):
+            nc.vector.tensor_tensor(
+                page[(g, t)][:].indirect(idx2[:, offs_halves[hf]]), h, wa[(g, t)][:, halves[hf]], MULT
+            )
+
+        def respond(g, t, us, h=None):
+            if h is None:
+                h = h_tile()
+            resonance(acc[(g, t)][:], us[:, :], h[:])
+            nc.vector.tensor_tensor(page[(g, t)][:].indirect(idx2[:]), h[:], wa[(g, t)][:], MULT)
+            store_page(g, t)
+
+        us00 = scratch()
+        h00 = h_tile()
+        for hf in range(2):
+            resonance(acc00[hf][:, 0 : S // 2], us00[:, halves[hf]], h00[:, halves[hf]])
+            scatter_half(0, 0, hf, h00[:, halves[hf]])
+        store_page(0, 0)
+        respond(0, 1, raw_tile(7, [P, S], F32, "us01"), raw_tile(9, [P, S], F32, "h01"))
         stage1_pass(1, 0, quant(cast_w1(1, 0, 0, raw_tile(7, [P, 2048], BF16, "gr10")), "w1q10"))
         gr11 = cast_w1(1, 1, 0, grouped_tile())
-        gr12 = cast_w1(1, 2, P, grouped_tile())
+        gr12 = cast_w1(1, 2, P, raw_tile(9, [P, 2048], BF16, "gr12"))
         late = [quant(gr11, "w1q11"), quant(gr12, "w1q12")]
         for t in range(PACK):
             stage1_one(1, 1, t, late[0])
@@ -253,8 +282,7 @@ def tile_list_furnace_zone_checkpoint_kernel(
         def round1(eng, t, hf):
             copy_on(eng, pairs1[hf][:, t // 2, :, t % 2], page[(1, t)][:, hf * HALF : (hf + 1) * HALF])
 
-        def weave(words):
-            gr = grouped_tile()
+        def weave(words, gr):
             nc.vector.tensor_copy(
                 out=gr[:].bitcast(F32).rearrange("p (m u) -> p m u", u=2), in_=words.rearrange("p u m -> p m u")
             )
@@ -273,8 +301,8 @@ def tile_list_furnace_zone_checkpoint_kernel(
         round0(2)
         round0(3)
         round1("v", 2, 0)
-        g00 = weave(words0[:, :, 0:HALF])
-        g01 = weave(words0[:, :, HALF:T2])
+        g00 = weave(words0[:, :, 0:HALF], grouped_tile())
+        g01 = weave(words0[:, :, HALF:T2], grouped_tile())
         quant_page(0, 0, g00)
         quant_page(0, 1, g01)
         nc.sync.dma_start(
@@ -329,7 +357,7 @@ def tile_list_furnace_zone_checkpoint_kernel(
         round1("v", 3, 0)
         round1("s", 3, 1)
         for hf in range(2):
-            grs.append(weave(pairs1[hf][:].rearrange("p u m e -> p u (m e)").bitcast(F32)))
+            grs.append(weave(pairs1[hf][:].rearrange("p u m e -> p u (m e)").bitcast(F32), grouped_tile()))
         for hf in range(2):
             quant_page(1, hf, grs[hf])
         nc.sync.dma_start(

@@ -40,40 +40,45 @@ def tile_list_furnace_zone_checkpoint_kernel(
         def bank(b):
             return psum.tile([P, 512], F32, name="bank%d" % b, tag="bank%d" % b)
 
-        def raw_tile(slot, shape, dtype, name):
-            return keep.tile(shape, dtype, name=name, tag="raw%d" % slot, align_bytes=64)
+        def slot_tile(slot, shape, dtype, name):
+            return keep.tile(shape, dtype, name=name, tag=slot, align_bytes=64)
 
         tab_sc = keep.tile([P, T], U8, name="tab_sc", align_bytes=64)
-        nc.gpsimd.memset(tab_sc[:].bitcast(I32), 0)
+        nc.vector.memset(tab_sc[:].bitcast(I32), 0)
+        w3_sc = keep.tile([P, HG, N], U8, name="w3_sc", align_bytes=64)
+        nc.vector.memset(w3_sc[:].bitcast(I32), 0)
+        for q in range(4):
+            nc.gpsimd.dma_start(
+                out=tab_sc[32 * q : 32 * q + 4 * KP, :].bitcast(I32),
+                in_=tab_scales[:, 4 * q : 4 * q + 4, :].bitcast(I32),
+            )
         ident = keep.tile([P, P], F32, name="ident")
         make_identity(nc, ident[:])
         amp_t = keep.tile([P, HG, PACK], F32, name="amp_t")
-        w3_sc = keep.tile([P, HG, N], U8, name="w3_sc", align_bytes=64)
-        nc.vector.memset(w3_sc[:].bitcast(I32), 0)
+        for q in range(4):
+            nc.gpsimd.dma_start(
+                out=w3_sc[32 * q : 32 * q + 4, :, :].bitcast(I32),
+                in_=w3_scales[:, 4 * q : 4 * q + 4, :].bitcast(I32).rearrange("g r c -> r g c"),
+            )
+
         idx = lists.tile([P, S // 16], U16, name="idx")
         idx2 = lists.tile([P, S // 16], U16, name="idx2")
-        wgs_t = keep.tile([P, S], F32, name="wgs_t")
-
         w1_raw = {}
-        tab = []
+        tab = {}
         page = {}
         w2_raw = {}
+        base_t = {}
 
-        def load_w1(g, a, parts=1):
-            t = raw_tile(KP * g + a, [P, PACK, K_PASS], F32, "w1_raw%d%d" % (g, a))
+        def load_w1(g, a):
+            t = slot_tile("w1raw%d%d" % (g, a), [P, PACK, K_PASS], F32, "w1_raw%d%d" % (g, a))
             rows = w1[a * K_PASS : (a + 1) * K_PASS, g * K_PASS : (g + 1) * K_PASS]
-            step = PACK // parts
-            for j in range(0, PACK, step):
-                nc.sync.dma_start(out=t[:, j : j + step, :], in_=rows.rearrange("(p j) c -> p j c", j=PACK)[:, j : j + step, :])
+            nc.sync.dma_start(out=t[:], in_=rows.rearrange("(p j) c -> p j c", j=PACK))
             w1_raw[(g, a)] = t
 
-        def load_tab(a, parts=1):
-            t = keep.tile([P, T], U32, name="tab%d" % a, align_bytes=64)
-            words = tab_words[a].rearrange("p n t -> p (n t)").bitcast(I32)
-            step = T // parts
-            for c in range(0, T, step):
-                nc.sync.dma_start(out=t[:, c : c + step].bitcast(I32), in_=words[:, c : c + step])
-            tab.append(t)
+        def load_tab(a):
+            t = slot_tile("tab%d" % a, [P, T], U32, "tab%d" % a)
+            nc.sync.dma_start(out=t[:].bitcast(I32), in_=tab_words[a].rearrange("p n t -> p (n t)").bitcast(I32))
+            tab[a] = t
 
         page0_v = page0.rearrange("(g p t) m -> g t p m", g=HG, t=PACK)
         out1_v = out_1.rearrange("(g p t) m -> g t p m", g=HG, t=PACK)
@@ -83,31 +88,40 @@ def tile_list_furnace_zone_checkpoint_kernel(
             nc.sync.dma_start(out=tl[:], in_=page0_v[g, t])
             page[(g, t)] = tl
 
-        def load_w2(g, slot):
-            t = raw_tile(slot, [P, PACK, N], F32, "w2_raw%d" % g)
+        def load_w2(g):
+            t = keep.tile([P, PACK, N], F32, name="w2_raw%d" % g)
             nc.sync.dma_start(out=t[:], in_=w2[g * K_PASS : (g + 1) * K_PASS, :].rearrange("(p j) c -> p j c", j=PACK))
             w2_raw[g] = t
 
-        nc.sync.dma_start(out=wgs_t[:], in_=wgs)
+        load_w1(0, 0)
         nc.sync.dma_start(idx[:], offs)
-        nc.sync.dma_start(idx2[:], offs2)
         nc.sync.dma_start(out=amp_t[:], in_=amp.rearrange("(g p t) -> p g t", g=HG, t=PACK))
-        for q in range(4):
-            nc.scalar.dma_start(
-                out=tab_sc[32 * q : 32 * q + 4 * KP, :].bitcast(I32),
-                in_=tab_scales[:, 4 * q : 4 * q + 4, :].bitcast(I32),
-            )
-        load_w1(0, 0, 2)
-        load_tab(0, 2)
-        for a in range(1, KP):
-            load_w1(0, a)
-            load_tab(a)
+        load_tab(0)
+        wgs_t = keep.tile([P, S], F32, name="wgs_t")
+        nc.sync.dma_start(out=wgs_t[:], in_=wgs)
+        load_w1(0, 1)
+        load_tab(1)
+        nc.sync.dma_start(idx2[:], offs2)
+        load_w1(0, 2)
+        load_tab(2)
         load_page(0, 0)
         load_w1(1, 0)
         load_page(0, 1)
         load_w1(1, 1)
-        load_w1(1, 2)
         load_page(0, 2)
+        load_w1(1, 2)
+        load_page(0, 3)
+        load_page(1, 0)
+        load_w2(0)
+        load_page(1, 1)
+        load_w2(1)
+        load_page(1, 2)
+        load_page(1, 3)
+        w3_w = keep.tile([P, HG, 2 * N], U8, name="w3_w", align_bytes=64)
+        nc.sync.dma_start(out=w3_w[:].bitcast(I32), in_=w3_words.bitcast(I32).rearrange("g p c -> p g c"))
+        for nt in range(NT):
+            base_t[nt] = keep.tile([P, T2], F32, name="base%d" % nt)
+            nc.sync.dma_start(out=base_t[nt][:], in_=base[nt * P : (nt + 1) * P, :])
 
         warm = keep.tile([P, 1], F32, name="warm")
         nc.scalar.activation(out=warm[:], in_=ident[:, 0:1], func=ACT.Abs_reciprocal_sqrt, bias=1.0)
@@ -115,7 +129,7 @@ def tile_list_furnace_zone_checkpoint_kernel(
         wgs_T = bank(5)
         for jb in range(4):
             nc.tensor.transpose(wgs_T[:, jb * P : (jb + 1) * P], wgs_t[:, jb * P : (jb + 1) * P], ident[:])
-        dealt = raw_tile(6, [P, 4, PACK, 4, 32], F32, "dealt")
+        dealt = slot_tile("dealt", [P, 4, PACK, 4, 32], F32, "dealt")
         for q in range(4):
             nc.scalar.copy(out=dealt[:, :, :, q, :], in_=wgs_T[:].rearrange("j (b p t) -> j b t p", b=4, t=PACK))
         wa = {}
@@ -138,22 +152,16 @@ def tile_list_furnace_zone_checkpoint_kernel(
         def grouped_tile():
             return keep.tile([P, 4 * 512], BF16, name="grouped", tag="grouped", bufs=3, align_bytes=64)
 
-        def cast_w1(g, a, mv, gr):
+        def cast_w1(eng, g, a, gr):
             dst = gr[:].rearrange("p (t m j) -> p m j t", t=PACK, j=PACK)
             src = w1_raw[(g, a)][:].rearrange("p j (m t) -> p m j t", t=PACK)
-            if mv > 0:
-                copy_on("v", dst[:, 0:mv], src[:, 0:mv])
-            if mv < P:
-                copy_on("s", dst[:, mv:P], src[:, mv:P])
+            copy_on(eng, dst, src)
             return gr
 
-        def cast_w2(g, cv, gr):
+        def cast_w2(eng, g, gr):
             dst = gr[:].rearrange("p (c i j) -> p c j i", i=4, j=PACK)
             src = w2_raw[g][:].rearrange("p j (c i) -> p c j i", i=4)
-            if cv > 0:
-                copy_on("v", dst[:, 0:cv], src[:, 0:cv])
-            if cv < P:
-                copy_on("s", dst[:, cv:P], src[:, cv:P])
+            copy_on(eng, dst, src)
             return gr
 
         def quant(gr, name):
@@ -162,7 +170,6 @@ def tile_list_furnace_zone_checkpoint_kernel(
             nc.vector.quantize_mx(out=codes[:].bitcast(FP8X4), scales=scales[:], in_=gr[:])
             return codes, scales
 
-        v_sc = keep.tile([P, S], U8, name="v_sc", align_bytes=64)
         v_w = []
         acc = {}
 
@@ -194,185 +201,181 @@ def tile_list_furnace_zone_checkpoint_kernel(
             for t in range(PACK):
                 stage1_one(g, a, t, wq)
 
-        for a in range(KP):
-            wq = quant(cast_w1(0, a, P, grouped_tile()), "w1q0%d" % a)
-            if a == 0:
+        w1q0 = []
+        for a in range(KP - 1):
+            w1q0.append(quant(cast_w1("v", 0, a, grouped_tile()), "w1q0%d" % a))
+            if a == 1:
+                v_sc = slot_tile("w1raw01", [P, S], U8, "v_sc")
                 nc.vector.tensor_copy(out=v_sc[:], in_=tab_sc[:].indirect(idx[:]))
-            vw = keep.tile([P, S], U32, name="v_w%d" % a, align_bytes=64)
-            if a < KP - 1:
-                nc.vector.tensor_copy(out=vw[:], in_=tab[a][:].indirect(idx[:]))
-            else:
-                for hf in range(2):
-                    nc.vector.tensor_copy(out=vw[:, halves[hf]], in_=tab[a][:].indirect(idx[:, offs_halves[hf]]))
-            v_w.append(vw)
-            stage1_pass(0, a, wq)
-
-        load_w2(0, 6)
-        load_page(0, 3)
-        load_w2(1, 0)
-        w3_w = keep.tile([P, HG, 2 * N], U8, name="w3_w", align_bytes=64)
-        nc.sync.dma_start(out=w3_w[:].bitcast(I32), in_=w3_words.bitcast(I32).rearrange("g p c -> p g c"))
-        for q in range(4):
-            nc.sync.dma_start(
-                out=w3_sc[32 * q : 32 * q + 4, :, :].bitcast(I32),
-                in_=w3_scales[:, 4 * q : 4 * q + 4, :].bitcast(I32).rearrange("g r c -> r g c"),
-            )
-        for t in range(PACK - 1):
-            load_page(1, t)
-        base_t = []
-        for nt in range(NT):
-            bt = keep.tile([P, T2], F32, name="base%d" % nt)
-            nc.sync.dma_start(out=bt[:], in_=base[nt * P : (nt + 1) * P, :])
-            base_t.append(bt)
-        load_page(1, PACK - 1)
+            v_w.append(keep.tile([P, S], U32, name="v_w%d" % a, align_bytes=64))
+            nc.vector.tensor_copy(out=v_w[a][:], in_=tab[a][:].indirect(idx[:]))
+        for a in range(KP - 1):
+            stage1_pass(0, a, w1q0[a])
+        a = KP - 1
+        wq = quant(cast_w1("v", 0, a, slot_tile("w1raw00", [P, 4 * 512], BF16, "gr02")), "w1q0%d" % a)
+        v_w.append(slot_tile("w1raw00", [P, S], U32, "v_w2"))
+        for hf in range(2):
+            nc.vector.tensor_copy(out=v_w[a][:, halves[hf]], in_=tab[a][:].indirect(idx[:, offs_halves[hf]]))
+        stage1_pass(0, a, wq)
 
         def scratch():
-            return keep.tile([P, S], F32, name="us", tag="us", bufs=2)
+            return keep.tile([P, S], F32, name="us", tag="us", bufs=1)
 
-        def resonance(src, us, h):
+        def resonance(src, us, us2, h):
             nc.scalar.activation(out=us, in_=src, func=ACT.Square)
-            nc.scalar.activation(out=us, in_=us, func=ACT.Abs_reciprocal_sqrt, bias=1.0)
-            nc.scalar.activation(out=h, in_=us, func=ACT.Square)
+            nc.scalar.activation(out=us2, in_=us, func=ACT.Abs_reciprocal_sqrt, bias=1.0)
+            nc.scalar.activation(out=h, in_=us2, func=ACT.Square)
 
         def store_page(g, t):
-            queue = nc.sync if (g, t) == (1, 3) else nc.gpsimd
-            queue.dma_start(out=out1_v[g, t], in_=page[(g, t)][:])
+            nc.sync.dma_start(out=out1_v[g, t], in_=page[(g, t)][:])
 
-        def h_tile():
-            return keep.tile([P, S], F32, name="h", tag="h", bufs=4)
+        def scatter(g, t, h):
+            nc.vector.tensor_tensor(page[(g, t)][:].indirect(idx2[:]), h, wa[(g, t)][:], MULT)
+            store_page(g, t)
 
         def scatter_half(g, t, hf, h):
             nc.vector.tensor_tensor(
                 page[(g, t)][:].indirect(idx2[:, offs_halves[hf]]), h, wa[(g, t)][:, halves[hf]], MULT
             )
 
-        def respond(g, t, us, h=None):
-            if h is None:
-                h = h_tile()
-            resonance(acc[(g, t)][:], us[:, :], h[:])
-            nc.vector.tensor_tensor(page[(g, t)][:].indirect(idx2[:]), h[:], wa[(g, t)][:], MULT)
-            store_page(g, t)
+        h0 = slot_tile("w1raw02", [P, PACK * S], F32, "h0")
+        h1 = slot_tile("dealt", [P, PACK * S], F32, "h1")
+
+        def respond(g, t, us, us2):
+            h = (h0, h1)[g][:, t * S : (t + 1) * S]
+            resonance(acc[(g, t)][:], us, us2, h)
+            scatter(g, t, h)
 
         us00 = scratch()
-        h00 = h_tile()
         for hf in range(2):
-            resonance(acc00[hf][:, 0 : S // 2], us00[:, halves[hf]], h00[:, halves[hf]])
-            scatter_half(0, 0, hf, h00[:, halves[hf]])
+            resonance(acc00[hf][:, 0 : S // 2], us00[:, halves[hf]], us00[:, halves[hf]], h0[:, halves[hf]])
+            scatter_half(0, 0, hf, h0[:, halves[hf]])
         store_page(0, 0)
-        respond(0, 1, raw_tile(7, [P, S], F32, "us01"), raw_tile(9, [P, S], F32, "h01"))
-        stage1_pass(1, 0, quant(cast_w1(1, 0, 0, raw_tile(7, [P, 2048], BF16, "gr10")), "w1q10"))
-        gr11 = cast_w1(1, 1, 0, grouped_tile())
-        gr12 = cast_w1(1, 2, P, raw_tile(9, [P, 2048], BF16, "gr12"))
-        late = [quant(gr11, "w1q11"), quant(gr12, "w1q12")]
+        gr1 = [grouped_tile() for a in range(KP)]
+        gr1_f = [gr[:].bitcast(F32)[:, 0:S] for gr in gr1]
+        respond(0, 1, gr1_f[0], gr1_f[0])
+        stage1_pass(1, 0, quant(cast_w1("s", 1, 0, gr1[0]), "w1q10"))
+        respond(0, 2, gr1_f[1], gr1_f[2])
+        late = [quant(cast_w1("s", 1, a, gr1[a]), "w1q1%d" % a) for a in (1, 2)]
         for t in range(PACK):
             stage1_one(1, 1, t, late[0])
             stage1_one(1, 2, t, late[1])
-        respond(0, 2, scratch(), raw_tile(5, [P, S], F32, "h02"))
-        respond(0, 3, scratch())
+        us03 = slot_tile("w1raw12", [P, S], F32, "us03")
+        respond(0, 3, us03[:], us03[:])
 
-        pairs0 = raw_tile(4, [P, 2, T2, 2], BF16, "pairs0")
-        words0 = pairs0[:].rearrange("p u m e -> p u (m e)").bitcast(F32)
-        pairs1 = [raw_tile(1 + hf, [P, 2, HALF, 2], BF16, "pairs1%d" % hf) for hf in range(2)]
+        pairs = {}
+        for g in range(HG):
+            for hf in range(2):
+                pairs[(g, hf)] = keep.tile([P, 2 * HALF], F32, name="pairs%d%d" % (g, hf))
         pq_c = [keep.tile([P, T2], U32, name="pq_c%d" % g, align_bytes=64) for g in range(HG)]
         pq_s = keep.tile([P, HG, T2], U8, name="pq_s", align_bytes=64)
 
-        def round0(t):
-            copy_on("s", pairs0[:, t // 2, :, t % 2], page[(0, t)][:])
+        def words(g, u, hf):
+            return pairs[(g, hf)][:, u * HALF : (u + 1) * HALF]
 
-        def round1(eng, t, hf):
-            copy_on(eng, pairs1[hf][:, t // 2, :, t % 2], page[(1, t)][:, hf * HALF : (hf + 1) * HALF])
+        def round_page(eng, g, t, hf):
+            dst = words(g, t // 2, hf).bitcast(BF16).rearrange("p (m e) -> p m e", e=2)
+            copy_on(eng, dst[:, :, t % 2], page[(g, t)][:, hf * HALF : (hf + 1) * HALF])
 
-        def weave(words, gr):
+        def weave(g, hf, gr):
             nc.vector.tensor_copy(
-                out=gr[:].bitcast(F32).rearrange("p (m u) -> p m u", u=2), in_=words.rearrange("p u m -> p m u")
+                out=gr[:].bitcast(F32).rearrange("p (m u) -> p m u", u=2),
+                in_=pairs[(g, hf)][:].rearrange("p (u m) -> p m u", u=2),
             )
             return gr
 
         def quant_page(g, hf, gr):
             cols = slice(hf * HALF, (hf + 1) * HALF)
             nc.vector.quantize_mx(out=pq_c[g][:, cols].bitcast(FP8X4), scales=pq_s[:, g, cols], in_=gr[:])
+            nc.sync.dma_start(
+                out=out_2[g].rearrange("p m t -> p (m t)").bitcast(I32)[:, cols], in_=pq_c[g][:, cols].bitcast(I32)
+            )
 
-        round0(0)
-        round0(1)
-        respond(1, 0, words0[:, 1, 0:S])
-        respond(1, 1, raw_tile(8, [P, S], F32, "us11"))
-        respond(1, 2, scratch())
-        w2q = [quant(cast_w2(0, 0, raw_tile(8, [P, 2048], BF16, "grw20")), "w2q0")]
-        round0(2)
-        round0(3)
-        round1("v", 2, 0)
-        g00 = weave(words0[:, :, 0:HALF], grouped_tile())
-        g01 = weave(words0[:, :, HALF:T2], grouped_tile())
-        quant_page(0, 0, g00)
-        quant_page(0, 1, g01)
-        nc.sync.dma_start(
-            out=out_2[0].rearrange("p m t -> p (m t)").bitcast(I32), in_=pq_c[0][:].bitcast(I32)
-        )
-        w2q.append(quant(cast_w2(1, 0, grouped_tile()), "w2q1"))
-        respond(1, 3, scratch(), raw_tile(4, [P, S], F32, "h13"))
+        round_page("s", 0, 0, 1)
+        round_page("s", 0, 1, 1)
+        respond(1, 0, words(0, 0, 0), words(0, 0, 0))
+        respond(1, 1, words(0, 1, 1), words(0, 1, 1))
+        round_page("s", 0, 0, 0)
+        round_page("s", 0, 1, 0)
+        round_page("s", 0, 2, 1)
+        round_page("s", 0, 3, 1)
+        quant_page(0, 1, weave(0, 1, grouped_tile()))
+        grw = [slot_tile("tab%d" % g, [P, 4 * 512], BF16, "grw%d" % g) for g in range(HG)]
+        respond(1, 2, words(0, 1, 0), grw[0][:].bitcast(F32)[:, 0:S])
+        round_page("s", 0, 2, 0)
+        round_page("s", 0, 3, 0)
+        w2q = [quant(cast_w2("s", 0, grw[0]), "w2q0")]
+        round_page("v", 1, 2, 0)
+        h13a = slot_tile("tab2", [P, S // 2], F32, "h13a")
+        us13 = grw[1][:].bitcast(F32)[:, 0:S]
+        nc.scalar.activation(out=us13, in_=acc[(1, 3)][:], func=ACT.Square)
+        r13 = h1[:, 3 * S : 4 * S]
+        nc.scalar.activation(out=r13, in_=us13, func=ACT.Abs_reciprocal_sqrt, bias=1.0)
+        nc.scalar.activation(out=h13a[:], in_=r13[:, halves[0]], func=ACT.Square)
+        scatter_half(1, 3, 0, h13a[:])
+        quant_page(0, 0, weave(0, 0, slot_tile("tab2", [P, 4 * 512], BF16, "gr00")))
+        w2q.append(quant(cast_w2("s", 1, grw[1]), "w2q1"))
         for t in range(2):
-            for hf in range(2):
-                round1("s", t, hf)
-        round1("s", 2, 1)
+            round_page("s", 1, t, 0)
+        h13b = slot_tile("tab2", [P, S // 2], F32, "h13b")
+        nc.scalar.activation(out=h13b[:], in_=r13[:, halves[1]], func=ACT.Square)
+        scatter_half(1, 3, 1, h13b[:])
+        store_page(1, 3)
+        for t in range(3):
+            round_page("s", 1, t, 1)
 
         acc2 = {}
 
-        def stage2_pass(g, hf, nt):
+        def stage2_pass(g, hf, nt, which):
             cols = slice(hf * HALF, (hf + 1) * HALF)
             if g == 0:
-                acc2[(hf, nt)] = (bank(2 * nt), bank(2 * nt + 1))
-            d_acc, b_acc = acc2[(hf, nt)]
+                acc2[(hf, nt, which)] = bank(2 * nt + which)
+            if which == 0:
+                lhsT = w3_w[:, g, 2 * nt * P : 2 * (nt + 1) * P].bitcast(FP4X4)
+                lhsT_scale = w3_sc[:, g, nt * P : (nt + 1) * P]
+            else:
+                lhsT = w2q[g][0][:, nt * P : (nt + 1) * P].bitcast(FP8X4)
+                lhsT_scale = w2q[g][1][:, nt * P : (nt + 1) * P]
             nc.tensor.matmul_mx(
-                out=d_acc[:],
-                lhsT=w3_w[:, g, 2 * nt * P : 2 * (nt + 1) * P].bitcast(FP4X4),
-                lhsT_scale=w3_sc[:, g, nt * P : (nt + 1) * P],
+                out=acc2[(hf, nt, which)][:],
+                lhsT=lhsT,
+                lhsT_scale=lhsT_scale,
                 rhs=pq_c[g][:, cols].bitcast(FP8X4),
                 rhs_scale=pq_s[:, g, cols],
                 start=(g == 0),
                 stop=(g == HG - 1),
             )
-            nc.tensor.matmul_mx(
-                out=b_acc[:],
-                lhsT=w2q[g][0][:, nt * P : (nt + 1) * P].bitcast(FP8X4),
-                lhsT_scale=w2q[g][1][:, nt * P : (nt + 1) * P],
-                rhs=pq_c[g][:, cols].bitcast(FP8X4),
-                rhs_scale=pq_s[:, g, cols],
-                start=(g == 0),
-                stop=(g == HG - 1),
-            )
+
+        th_all = [slot_tile("w1raw1%d" % hf, [P, NT * HALF], F32, "th%d" % hf) for hf in range(2)]
 
         def finish(hf, nt):
             cols = slice(hf * HALF, (hf + 1) * HALF)
-            d_acc, b_acc = acc2[(hf, nt)]
-            th = keep.tile([P, HALF], F32, name="th", tag="th", bufs=4)
-            nc.scalar.activation(out=th[:], in_=d_acc[:], func=ACT.Tanh)
-            nc.vector.tensor_tensor(th[:], b_acc[:], th[:], MULT)
-            adder = nc.gpsimd if (NT * hf + nt) in (0, 1, 3, 4, 6) else nc.vector
-            adder.tensor_tensor(base_t[nt][:, cols], th[:], base_t[nt][:, cols], ADD)
+            th = th_all[hf][:, nt * HALF : (nt + 1) * HALF]
+            nc.scalar.activation(out=th, in_=acc2[(hf, nt, 0)][:], func=ACT.Tanh)
+            nc.vector.tensor_tensor(th, acc2[(hf, nt, 1)][:], th, MULT)
+            adder = nc.gpsimd if (NT * hf + nt) in (0, 1, 2, 4) else nc.vector
+            adder.tensor_tensor(base_t[nt][:, cols], th, base_t[nt][:, cols], ADD)
             nc.sync.dma_start(out=out_0[nt * P : (nt + 1) * P, cols], in_=base_t[nt][:, cols])
 
         for nt in range(NT):
-            stage2_pass(0, 0, nt)
-        grs = []
-        round1("v", 3, 0)
-        round1("s", 3, 1)
+            for which in range(2):
+                stage2_pass(0, 0, nt, which)
+        round_page("v", 1, 3, 0)
+        round_page("s", 1, 3, 1)
         for hf in range(2):
-            grs.append(weave(pairs1[hf][:].rearrange("p u m e -> p u (m e)").bitcast(F32), grouped_tile()))
-        for hf in range(2):
-            quant_page(1, hf, grs[hf])
-        nc.sync.dma_start(
-            out=out_2[1].rearrange("p m t -> p (m t)").bitcast(I32), in_=pq_c[1][:].bitcast(I32)
-        )
+            quant_page(1, hf, weave(1, hf, grouped_tile()))
         for q in range(4):
             nc.sync.dma_start(
                 out=out_3[:, 4 * q : 4 * q + 4, :].bitcast(I32).rearrange("g r m -> r g m"),
                 in_=pq_s[32 * q : 32 * q + 4, :, :].bitcast(I32),
             )
         for nt in range(NT):
-            stage2_pass(1, 0, nt)
+            for which in range(2):
+                stage2_pass(1, 0, nt, which)
         for nt in range(NT):
             finish(0, nt)
-            stage2_pass(0, 1, nt)
-            stage2_pass(1, 1, nt)
+            for which in range(2):
+                for g in range(HG):
+                    stage2_pass(g, 1, nt, which)
         for nt in range(NT):
             finish(1, nt)

@@ -44,14 +44,9 @@ def tile_list_furnace_zone_checkpoint_kernel(
             return keep.tile(shape, dtype, name=name, tag=slot, align_bytes=64)
 
         tab_sc = keep.tile([P, T], U8, name="tab_sc", align_bytes=64)
-        nc.vector.memset(tab_sc[:].bitcast(I32), 0)
+        nc.gpsimd.memset(tab_sc[:].bitcast(I32), 0)
         w3_sc = keep.tile([P, HG, N], U8, name="w3_sc", align_bytes=64)
         nc.vector.memset(w3_sc[:].bitcast(I32), 0)
-        for q in range(4):
-            nc.gpsimd.dma_start(
-                out=tab_sc[32 * q : 32 * q + 4 * KP, :].bitcast(I32),
-                in_=tab_scales[:, 4 * q : 4 * q + 4, :].bitcast(I32),
-            )
         ident = keep.tile([P, P], F32, name="ident")
         make_identity(nc, ident[:])
         amp_t = keep.tile([P, HG, PACK], F32, name="amp_t")
@@ -94,6 +89,11 @@ def tile_list_furnace_zone_checkpoint_kernel(
             w2_raw[g] = t
 
         load_w1(0, 0)
+        for q in range(4):
+            nc.sync.dma_start(
+                out=tab_sc[32 * q : 32 * q + 4 * KP, :].bitcast(I32),
+                in_=tab_scales[:, 4 * q : 4 * q + 4, :].bitcast(I32),
+            )
         nc.sync.dma_start(idx[:], offs)
         nc.sync.dma_start(out=amp_t[:], in_=amp.rearrange("(g p t) -> p g t", g=HG, t=PACK))
         load_tab(0)

@@ -44,9 +44,14 @@ def tile_list_furnace_zone_checkpoint_kernel(
             return keep.tile(shape, dtype, name=name, tag=slot, align_bytes=64)
 
         tab_sc = keep.tile([P, T], U8, name="tab_sc", align_bytes=64)
-        nc.gpsimd.memset(tab_sc[:].bitcast(I32), 0)
+        nc.vector.memset(tab_sc[:].bitcast(I32), 0)
         w3_sc = keep.tile([P, HG, N], U8, name="w3_sc", align_bytes=64)
         nc.vector.memset(w3_sc[:].bitcast(I32), 0)
+        for q in range(4):
+            nc.gpsimd.dma_start(
+                out=tab_sc[32 * q : 32 * q + 4 * KP, :].bitcast(I32),
+                in_=tab_scales[:, 4 * q : 4 * q + 4, :].bitcast(I32),
+            )
         ident = keep.tile([P, P], F32, name="ident")
         make_identity(nc, ident[:])
         amp_t = keep.tile([P, HG, PACK], F32, name="amp_t")
@@ -84,21 +89,16 @@ def tile_list_furnace_zone_checkpoint_kernel(
             page[(g, t)] = tl
 
         def load_w2(g):
-            t = keep.tile([P, PACK, N], F32, name="w2_raw%d" % g)
+            t = slot_tile("w2raw%d" % g, [P, PACK, N], F32, "w2_raw%d" % g)
             nc.sync.dma_start(out=t[:], in_=w2[g * K_PASS : (g + 1) * K_PASS, :].rearrange("(p j) c -> p j c", j=PACK))
             w2_raw[g] = t
 
+        wgs_t = keep.tile([P, S], F32, name="wgs_t")
+        nc.sync.dma_start(out=wgs_t[:], in_=wgs)
         load_w1(0, 0)
-        for q in range(4):
-            nc.sync.dma_start(
-                out=tab_sc[32 * q : 32 * q + 4 * KP, :].bitcast(I32),
-                in_=tab_scales[:, 4 * q : 4 * q + 4, :].bitcast(I32),
-            )
         nc.sync.dma_start(idx[:], offs)
         nc.sync.dma_start(out=amp_t[:], in_=amp.rearrange("(g p t) -> p g t", g=HG, t=PACK))
         load_tab(0)
-        wgs_t = keep.tile([P, S], F32, name="wgs_t")
-        nc.sync.dma_start(out=wgs_t[:], in_=wgs)
         load_w1(0, 1)
         load_tab(1)
         nc.sync.dma_start(idx2[:], offs2)
@@ -111,8 +111,8 @@ def tile_list_furnace_zone_checkpoint_kernel(
         load_page(0, 2)
         load_w1(1, 2)
         load_page(0, 3)
-        load_page(1, 0)
         load_w2(0)
+        load_page(1, 0)
         load_page(1, 1)
         load_w2(1)
         load_page(1, 2)
@@ -140,32 +140,32 @@ def tile_list_furnace_zone_checkpoint_kernel(
                     back[:, jb * P : (jb + 1) * P], dealt[:, jb, t, :, :].rearrange("j q p -> j (q p)"), ident[:]
                 )
             for g in range(HG):
-                wa[(g, t)] = keep.tile([P, S], F32, name="wa%d%d" % (g, t))
+                wa[(g, t)] = slot_tile("wa%d%d" % (g, t), [P, S], F32, "wa%d%d" % (g, t))
                 nc.scalar.activation(out=wa[(g, t)][:], in_=back[:], func=ACT.Copy, scale=amp_t[:, g, t : t + 1])
 
         def copy_on(eng, out, in_):
             if eng == "v":
                 nc.vector.tensor_copy(out=out, in_=in_)
+            elif eng == "g":
+                nc.gpsimd.tensor_scalar(out, in_, 1.0, -0.0, MULT, ADD)
             else:
                 nc.scalar.copy(out=out, in_=in_)
 
         def grouped_tile():
             return keep.tile([P, 4 * 512], BF16, name="grouped", tag="grouped", bufs=3, align_bytes=64)
 
-        def cast_w1(eng, g, a, gr):
-            dst = gr[:].rearrange("p (t m j) -> p m j t", t=PACK, j=PACK)
+        def cast_w1(eng, g, a, gr, ms):
+            dst = gr.rearrange("p (t m j) -> p m j t", t=PACK, j=PACK)
             src = w1_raw[(g, a)][:].rearrange("p j (m t) -> p m j t", t=PACK)
-            copy_on(eng, dst, src)
-            return gr
+            copy_on(eng, dst[:, ms], src[:, ms])
 
-        def cast_w2(eng, g, gr):
+        def cast_w2(eng, g, gr, cs):
             dst = gr[:].rearrange("p (c i j) -> p c j i", i=4, j=PACK)
             src = w2_raw[g][:].rearrange("p j (c i) -> p c j i", i=4)
-            copy_on(eng, dst, src)
-            return gr
+            copy_on(eng, dst[:, cs], src[:, cs])
 
-        def quant(gr, name):
-            codes = keep.tile([P, 512], U32, name=name + "_c", align_bytes=64)
+        def quant(gr, name, slot=None):
+            codes = slot_tile(slot or name, [P, 512], U32, name + "_c")
             scales = keep.tile([P, 512], U8, name=name + "_s", align_bytes=64)
             nc.vector.quantize_mx(out=codes[:].bitcast(FP8X4), scales=scales[:], in_=gr[:])
             return codes, scales
@@ -186,12 +186,13 @@ def tile_list_furnace_zone_checkpoint_kernel(
 
         halves = [slice(0, S // 2), slice(S // 2, S)]
         offs_halves = [slice(0, S // 32), slice(S // 32, S // 16)]
-        acc00 = [bank(0), bank(4)]
 
         def stage1_one(g, a, t, wq):
-            if (g, t) == (0, 0):
+            if t == 0:
+                if a == 0:
+                    acc[(g, t)] = [bank(PACK * g), bank(PACK * (1 - g))]
                 for hf in range(2):
-                    stage1_mm(acc00[hf][:, 0 : S // 2], a, t, wq, halves[hf])
+                    stage1_mm(acc[(g, t)][hf][:, 0 : S // 2], a, t, wq, halves[hf])
                 return
             if a == 0:
                 acc[(g, t)] = bank(PACK * g + t)
@@ -203,126 +204,169 @@ def tile_list_furnace_zone_checkpoint_kernel(
 
         w1q0 = []
         for a in range(KP - 1):
-            w1q0.append(quant(cast_w1("v", 0, a, grouped_tile()), "w1q0%d" % a))
-            if a == 1:
-                v_sc = slot_tile("w1raw01", [P, S], U8, "v_sc")
+            gr = grouped_tile()
+            cast_w1("v", 0, a, gr[:], slice(0, P))
+            w1q0.append(quant(gr, "w1q0%d" % a))
+            if a == 0:
+                v_sc = keep.tile([P, S], U8, name="v_sc", align_bytes=64)
                 nc.vector.tensor_copy(out=v_sc[:], in_=tab_sc[:].indirect(idx[:]))
             v_w.append(keep.tile([P, S], U32, name="v_w%d" % a, align_bytes=64))
             nc.vector.tensor_copy(out=v_w[a][:], in_=tab[a][:].indirect(idx[:]))
         for a in range(KP - 1):
             stage1_pass(0, a, w1q0[a])
         a = KP - 1
-        wq = quant(cast_w1("v", 0, a, slot_tile("w1raw00", [P, 4 * 512], BF16, "gr02")), "w1q0%d" % a)
+        gr = slot_tile("w1raw00", [P, 4 * 512], BF16, "gr02")
+        cast_w1("v", 0, a, gr[:], slice(0, P))
+        wq = quant(gr, "w1q0%d" % a)
         v_w.append(slot_tile("w1raw00", [P, S], U32, "v_w2"))
         for hf in range(2):
             nc.vector.tensor_copy(out=v_w[a][:, halves[hf]], in_=tab[a][:].indirect(idx[:, offs_halves[hf]]))
         stage1_pass(0, a, wq)
 
-        def scratch():
-            return keep.tile([P, S], F32, name="us", tag="us", bufs=1)
-
-        def resonance(src, us, us2, h):
+        def resonance(src, us, h):
             nc.scalar.activation(out=us, in_=src, func=ACT.Square)
-            nc.scalar.activation(out=us2, in_=us, func=ACT.Abs_reciprocal_sqrt, bias=1.0)
-            nc.scalar.activation(out=h, in_=us2, func=ACT.Square)
+            nc.scalar.activation(out=us, in_=us, func=ACT.Abs_reciprocal_sqrt, bias=1.0)
+            nc.scalar.activation(out=h, in_=us, func=ACT.Square)
 
         def store_page(g, t):
             nc.sync.dma_start(out=out1_v[g, t], in_=page[(g, t)][:])
 
-        def scatter(g, t, h):
-            nc.vector.tensor_tensor(page[(g, t)][:].indirect(idx2[:]), h, wa[(g, t)][:], MULT)
+        def weigh(g, t, h, cols):
+            nc.gpsimd.tensor_tensor(wa[(g, t)][:, cols], h, wa[(g, t)][:, cols], MULT)
+
+        def scatter(g, t):
+            nc.vector.tensor_copy(out=page[(g, t)][:].indirect(idx2[:]), in_=wa[(g, t)][:])
             store_page(g, t)
 
-        def scatter_half(g, t, hf, h):
+        def scatter_half(g, t, hf):
+            nc.vector.tensor_copy(out=page[(g, t)][:].indirect(idx2[:, offs_halves[hf]]), in_=wa[(g, t)][:, halves[hf]])
+
+        def scatter_half_fused(g, t, hf, h):
             nc.vector.tensor_tensor(
                 page[(g, t)][:].indirect(idx2[:, offs_halves[hf]]), h, wa[(g, t)][:, halves[hf]], MULT
             )
 
-        h0 = slot_tile("w1raw02", [P, PACK * S], F32, "h0")
-        h1 = slot_tile("dealt", [P, PACK * S], F32, "h1")
+        def respond(g, t, us, h):
+            resonance(acc[(g, t)][:], us, h)
+            weigh(g, t, h, slice(0, S))
+            scatter(g, t)
 
-        def respond(g, t, us, us2):
-            h = (h0, h1)[g][:, t * S : (t + 1) * S]
-            resonance(acc[(g, t)][:], us, us2, h)
-            scatter(g, t, h)
-
-        us00 = scratch()
-        for hf in range(2):
-            resonance(acc00[hf][:, 0 : S // 2], us00[:, halves[hf]], us00[:, halves[hf]], h0[:, halves[hf]])
-            scatter_half(0, 0, hf, h0[:, halves[hf]])
-        store_page(0, 0)
-        gr1 = [grouped_tile() for a in range(KP)]
-        gr1_f = [gr[:].bitcast(F32)[:, 0:S] for gr in gr1]
-        respond(0, 1, gr1_f[0], gr1_f[0])
-        stage1_pass(1, 0, quant(cast_w1("s", 1, 0, gr1[0]), "w1q10"))
-        respond(0, 2, gr1_f[1], gr1_f[2])
-        late = [quant(cast_w1("s", 1, a, gr1[a]), "w1q1%d" % a) for a in (1, 2)]
-        for t in range(PACK):
-            stage1_one(1, 1, t, late[0])
-            stage1_one(1, 2, t, late[1])
-        us03 = slot_tile("w1raw12", [P, S], F32, "us03")
-        respond(0, 3, us03[:], us03[:])
-
-        pairs = {}
-        for g in range(HG):
+        def respond_halves(g, t, us, h):
             for hf in range(2):
-                pairs[(g, hf)] = keep.tile([P, 2 * HALF], F32, name="pairs%d%d" % (g, hf))
-        pq_c = [keep.tile([P, T2], U32, name="pq_c%d" % g, align_bytes=64) for g in range(HG)]
+                resonance(acc[(g, t)][hf][:, 0 : S // 2], us[:, halves[hf]], h[hf])
+                weigh(g, t, h[hf], halves[hf])
+                scatter_half(g, t, hf)
+            store_page(g, t)
+
+        rounded0 = slot_tile("rounded0", [P, PACK * HALF], F32, "rounded0")
+        pairs1 = [keep.tile([P, 2 * HALF], F32, name="pairs1%d" % hf) for hf in range(2)]
         pq_s = keep.tile([P, HG, T2], U8, name="pq_s", align_bytes=64)
+        pq_c = {}
 
-        def words(g, u, hf):
-            return pairs[(g, hf)][:, u * HALF : (u + 1) * HALF]
+        def row0(t):
+            return rounded0[:, t * HALF : (t + 1) * HALF]
 
-        def round_page(eng, g, t, hf):
-            dst = words(g, t // 2, hf).bitcast(BF16).rearrange("p (m e) -> p m e", e=2)
-            copy_on(eng, dst[:, :, t % 2], page[(g, t)][:, hf * HALF : (hf + 1) * HALF])
+        def words1(u, hf):
+            return pairs1[hf][:, u * HALF : (u + 1) * HALF]
 
-        def weave(g, hf, gr):
-            nc.vector.tensor_copy(
-                out=gr[:].bitcast(F32).rearrange("p (m u) -> p m u", u=2),
-                in_=pairs[(g, hf)][:].rearrange("p (u m) -> p m u", u=2),
+        def round0(t):
+            copy_on("g", row0(t).bitcast(BF16), page[(0, t)][:])
+
+        def round1(eng, t, hf):
+            dst = words1(t // 2, hf).bitcast(BF16).rearrange("p (m e) -> p m e", e=2)
+            copy_on(eng, dst[:, :, t % 2], page[(1, t)][:, hf * HALF : (hf + 1) * HALF])
+
+        def interleave0(hf, gr):
+            src = rounded0[:].bitcast(BF16).rearrange("p (t h c i) -> p h c t i", t=PACK, h=2, i=4)
+            nc.scalar.copy(out=gr[:].rearrange("p (c i t) -> p c t i", i=4, t=PACK), in_=src[:, hf])
+            return gr
+
+        def weave1(eng, hf, gr):
+            copy_on(
+                eng,
+                gr[:].bitcast(F32).rearrange("p (m u) -> p m u", u=2),
+                pairs1[hf][:].rearrange("p (u m) -> p m u", u=2),
             )
             return gr
 
-        def quant_page(g, hf, gr):
+        def quant_page(g, hf, gr, codes):
             cols = slice(hf * HALF, (hf + 1) * HALF)
-            nc.vector.quantize_mx(out=pq_c[g][:, cols].bitcast(FP8X4), scales=pq_s[:, g, cols], in_=gr[:])
+            pq_c[(g, hf)] = codes
+            nc.vector.quantize_mx(out=codes[:].bitcast(FP8X4), scales=pq_s[:, g, cols], in_=gr[:])
             nc.sync.dma_start(
-                out=out_2[g].rearrange("p m t -> p (m t)").bitcast(I32)[:, cols], in_=pq_c[g][:, cols].bitcast(I32)
+                out=out_2[g].rearrange("p m t -> p (m t)").bitcast(I32)[:, cols], in_=codes[:].bitcast(I32)
             )
 
-        round_page("s", 0, 0, 1)
-        round_page("s", 0, 1, 1)
-        respond(1, 0, words(0, 0, 0), words(0, 0, 0))
-        respond(1, 1, words(0, 1, 1), words(0, 1, 1))
-        round_page("s", 0, 0, 0)
-        round_page("s", 0, 1, 0)
-        round_page("s", 0, 2, 1)
-        round_page("s", 0, 3, 1)
-        quant_page(0, 1, weave(0, 1, grouped_tile()))
-        grw = [slot_tile("tab%d" % g, [P, 4 * 512], BF16, "grw%d" % g) for g in range(HG)]
-        respond(1, 2, words(0, 1, 0), grw[0][:].bitcast(F32)[:, 0:S])
-        round_page("s", 0, 2, 0)
-        round_page("s", 0, 3, 0)
-        w2q = [quant(cast_w2("s", 0, grw[0]), "w2q0")]
-        round_page("v", 1, 2, 0)
+        def codes_tile(g, hf):
+            return keep.tile([P, HALF], U32, name="pq_c%d%d" % (g, hf), align_bytes=64)
+
+        spare = slot_tile("w1raw02", [P, PACK * S], F32, "spare")
+        respond_halves(0, 0, spare[:, 0:S], [spare[:, S : S + S // 2], spare[:, S + S // 2 : 2 * S]])
+        gr10 = grouped_tile()
+        gr1x = slot_tile("dealt", [P, 2 * 2048], BF16, "gr1x")
+        respond(0, 1, gr10[:].bitcast(F32)[:, 0:S], row0(0))
+        cast_w1("s", 1, 0, gr10[:], slice(0, P // 2))
+        cast_w1("v", 1, 0, gr10[:], slice(P // 2, P))
+        stage1_pass(1, 0, quant(gr10, "w1q10", "wa01"))
+        round0(0)
+        respond(0, 2, gr1x[:].bitcast(F32)[:, 0:S], row0(1))
+        cast_w1("s", 1, 1, gr1x[:, 0:2048], slice(0, P))
+        h03 = spare[:, S : 2 * S]
+        resonance(acc[(0, 3)][:, halves[1]], gr1x[:].bitcast(F32)[:, 2 * S : 2 * S + S // 2], h03[:, halves[1]])
+        round0(1)
+        weigh(0, 3, h03[:, halves[1]], halves[1])
+        cast_w1("s", 1, 2, gr1x[:, 2048:4096], slice(0, P))
+        late_c = keep.tile([P, 1024], U32, name="w1q1x_c", align_bytes=64)
+        late_s = keep.tile([P, 1024], U8, name="w1q1x_s", align_bytes=64)
+        nc.vector.quantize_mx(out=late_c[:].bitcast(FP8X4), scales=late_s[:], in_=gr1x[:])
+        late = [(late_c[:, 512 * i : 512 * (i + 1)], late_s[:, 512 * i : 512 * (i + 1)]) for i in range(2)]
+        us03 = slot_tile("w1raw12", [P, S // 2], F32, "us03")
+        resonance(acc[(0, 3)][:, halves[0]], us03[:], h03[:, halves[0]])
+        scatter_half_fused(0, 3, 0, h03[:, halves[0]])
+        scatter_half(0, 3, 1)
+        store_page(0, 3)
+        for hf in range(2):
+            for a in (1, 2):
+                stage1_mm(acc[(1, 0)][hf][:, 0 : S // 2], a, 0, late[a - 1], halves[hf])
+        for t in range(1, PACK):
+            stage1_one(1, 1, t, late[0])
+            stage1_one(1, 2, t, late[1])
+        grw0 = slot_tile("w1raw12", [P, 4 * 512], BF16, "grw0")
+        cast_w2("s", 0, grw0, slice(0, P // 2))
+        respond_halves(1, 0, spare[:, 2 * S : 3 * S], [row0(2)[:, halves[hf]] for hf in range(2)])
+        round0(2)
+        respond(1, 1, spare[:, 3 * S : 4 * S], row0(3))
+        round0(3)
+        us12 = grw0[:].bitcast(F32)[:, S : 2 * S]
+        nc.scalar.activation(out=us12, in_=acc[(1, 2)][:], func=ACT.Square)
+        nc.scalar.activation(out=words1(0, 1), in_=us12, func=ACT.Abs_reciprocal_sqrt, bias=1.0)
+        nc.scalar.activation(out=words1(0, 0), in_=words1(0, 1), func=ACT.Square)
+        weigh(1, 2, words1(0, 0), slice(0, S))
+        scatter(1, 2)
+        for t in range(2):
+            for hf in range(2):
+                round1("g", t, hf)
+        cast_w2("s", 0, grw0, slice(P // 2, P))
+        w2q = [quant(grw0, "w2q0", "wa12")]
+        round1("v", 2, 0)
+        us13 = spare[:, S : 2 * S]
+        r13 = words1(1, 1)
         h13a = slot_tile("tab2", [P, S // 2], F32, "h13a")
-        us13 = grw[1][:].bitcast(F32)[:, 0:S]
         nc.scalar.activation(out=us13, in_=acc[(1, 3)][:], func=ACT.Square)
-        r13 = h1[:, 3 * S : 4 * S]
         nc.scalar.activation(out=r13, in_=us13, func=ACT.Abs_reciprocal_sqrt, bias=1.0)
         nc.scalar.activation(out=h13a[:], in_=r13[:, halves[0]], func=ACT.Square)
-        scatter_half(1, 3, 0, h13a[:])
-        quant_page(0, 0, weave(0, 0, slot_tile("tab2", [P, 4 * 512], BF16, "gr00")))
-        w2q.append(quant(cast_w2("s", 1, grw[1]), "w2q1"))
-        for t in range(2):
-            round_page("s", 1, t, 0)
-        h13b = slot_tile("tab2", [P, S // 2], F32, "h13b")
+        quant_page(0, 1, interleave0(1, grouped_tile()), codes_tile(0, 1))
+        scatter_half_fused(1, 3, 0, h13a[:])
+        gr00 = interleave0(0, slot_tile("tab0", [P, 4 * 512], BF16, "gr00"))
+        quant_page(0, 0, gr00, slot_tile("tab2", [P, HALF], U32, "pq_c00"))
+        grw1 = slot_tile("rounded0", [P, 4 * 512], BF16, "grw1")
+        cast_w2("s", 1, grw1, slice(0, P))
+        w2q.append(quant(grw1, "w2q1"))
+        h13b = slot_tile("tab0", [P, S // 2], F32, "h13b")
         nc.scalar.activation(out=h13b[:], in_=r13[:, halves[1]], func=ACT.Square)
-        scatter_half(1, 3, 1, h13b[:])
+        scatter_half_fused(1, 3, 1, h13b[:])
         store_page(1, 3)
-        for t in range(3):
-            round_page("s", 1, t, 1)
+        round1("s", 2, 1)
 
         acc2 = {}
 
@@ -340,7 +384,7 @@ def tile_list_furnace_zone_checkpoint_kernel(
                 out=acc2[(hf, nt, which)][:],
                 lhsT=lhsT,
                 lhsT_scale=lhsT_scale,
-                rhs=pq_c[g][:, cols].bitcast(FP8X4),
+                rhs=pq_c[(g, hf)][:].bitcast(FP8X4),
                 rhs_scale=pq_s[:, g, cols],
                 start=(g == 0),
                 stop=(g == HG - 1),
@@ -360,10 +404,26 @@ def tile_list_furnace_zone_checkpoint_kernel(
         for nt in range(NT):
             for which in range(2):
                 stage2_pass(0, 0, nt, which)
-        round_page("v", 1, 3, 0)
-        round_page("s", 1, 3, 1)
-        for hf in range(2):
-            quant_page(1, hf, weave(1, hf, grouped_tile()))
+        quarters = [slice(0, HALF // 2), slice(HALF // 2, HALF)]
+        last0 = words1(1, 0).bitcast(BF16).rearrange("p (m e) -> p m e", e=2)
+        for qs in quarters:
+            nc.vector.tensor_copy(out=last0[:, qs, 1], in_=page[(1, 3)][:, qs])
+        round1("s", 3, 1)
+        gr = grouped_tile()
+        for qs in quarters:
+            nc.vector.tensor_copy(
+                out=gr[:].bitcast(F32).rearrange("p (m u) -> p m u", u=2)[:, qs],
+                in_=pairs1[0][:].rearrange("p (u m) -> p m u", u=2)[:, qs],
+            )
+        pq_c[(1, 0)] = codes_tile(1, 0)
+        for i, qs in enumerate(quarters):
+            nc.vector.quantize_mx(
+                out=pq_c[(1, 0)][:, qs].bitcast(FP8X4), scales=pq_s[:, 1, qs], in_=gr[:, i * 1024 : (i + 1) * 1024]
+            )
+        nc.sync.dma_start(
+            out=out_2[1].rearrange("p m t -> p (m t)").bitcast(I32)[:, 0:HALF], in_=pq_c[(1, 0)][:].bitcast(I32)
+        )
+        quant_page(1, 1, weave1("v", 1, grouped_tile()), codes_tile(1, 1))
         for q in range(4):
             nc.sync.dma_start(
                 out=out_3[:, 4 * q : 4 * q + 4, :].bitcast(I32).rearrange("g r m -> r g m"),
@@ -374,8 +434,32 @@ def tile_list_furnace_zone_checkpoint_kernel(
                 stage2_pass(1, 0, nt, which)
         for nt in range(NT):
             finish(0, nt)
-            for which in range(2):
+            for which in range(2 if nt < NT - 1 else 1):
                 for g in range(HG):
                     stage2_pass(g, 1, nt, which)
-        for nt in range(NT):
-            finish(1, nt)
+        nt = NT - 1
+        last_b = []
+        for i, qs in enumerate(quarters):
+            last_b.append(bank(2 * nt + 1 - 7 * i))
+            for g in range(HG):
+                nc.tensor.matmul_mx(
+                    out=last_b[i][:, 0 : HALF // 2],
+                    lhsT=w2q[g][0][:, nt * P : (nt + 1) * P].bitcast(FP8X4),
+                    lhsT_scale=w2q[g][1][:, nt * P : (nt + 1) * P],
+                    rhs=pq_c[(g, 1)][:, qs].bitcast(FP8X4),
+                    rhs_scale=pq_s[:, g, HALF + i * (HALF // 2) : HALF + (i + 1) * (HALF // 2)],
+                    start=(g == 0),
+                    stop=(g == HG - 1),
+                )
+            if i == 0:
+                finish(1, 0)
+        for k in range(1, NT - 1):
+            finish(1, k)
+        th = th_all[1][:, nt * HALF : (nt + 1) * HALF]
+        nc.scalar.activation(out=th, in_=acc2[(1, nt, 0)][:], func=ACT.Tanh)
+        for i, qs in enumerate(quarters):
+            nc.vector.tensor_tensor(th[:, qs], last_b[i][:, 0 : HALF // 2], th[:, qs], MULT)
+        for i, qs in enumerate(quarters):
+            cols = slice(HALF + i * (HALF // 2), HALF + (i + 1) * (HALF // 2))
+            nc.vector.tensor_tensor(base_t[nt][:, cols], th[:, qs], base_t[nt][:, cols], ADD)
+            nc.sync.dma_start(out=out_0[nt * P : (nt + 1) * P, cols], in_=base_t[nt][:, cols])

@@ -305,8 +305,7 @@ def tile_list_furnace_zone_checkpoint_kernel(
         gr10 = grouped_tile()
         gr1x = slot_tile("dealt", [P, 2 * 2048], BF16, "gr1x")
         respond(0, 1, gr10[:].bitcast(F32)[:, 0:S], row0(0))
-        cast_w1("s", 1, 0, gr10[:], slice(0, P // 2))
-        cast_w1("v", 1, 0, gr10[:], slice(P // 2, P))
+        cast_w1("s", 1, 0, gr10[:], slice(0, P))
         stage1_pass(1, 0, quant(gr10, "w1q10", "wa01"))
         round0(0)
         respond(0, 2, gr1x[:].bitcast(F32)[:, 0:S], row0(1))
@@ -392,14 +391,18 @@ def tile_list_furnace_zone_checkpoint_kernel(
 
         th_all = [slot_tile("w1raw1%d" % hf, [P, NT * HALF], F32, "th%d" % hf) for hf in range(2)]
 
+        products = {}
+
         def finish(hf, nt):
-            cols = slice(hf * HALF, (hf + 1) * HALF)
             th = th_all[hf][:, nt * HALF : (nt + 1) * HALF]
             nc.scalar.activation(out=th, in_=acc2[(hf, nt, 0)][:], func=ACT.Tanh)
-            nc.vector.tensor_tensor(th, acc2[(hf, nt, 1)][:], th, MULT)
-            adder = nc.gpsimd if (NT * hf + nt) in (0, 1, 2, 4) else nc.vector
-            adder.tensor_tensor(base_t[nt][:, cols], th, base_t[nt][:, cols], ADD)
-            nc.sync.dma_start(out=out_0[nt * P : (nt + 1) * P, cols], in_=base_t[nt][:, cols])
+            products[(hf, nt)] = spare[:, S : 2 * S] if (hf, nt) == (1, 1) else th
+            nc.vector.tensor_tensor(products[(hf, nt)], acc2[(hf, nt, 1)][:], th, MULT)
+
+        def add_base(adder, hf, nt, out):
+            cols = slice(hf * HALF, (hf + 1) * HALF)
+            adder.tensor_tensor(out, products[(hf, nt)], base_t[nt][:, cols], ADD)
+            nc.sync.dma_start(out=out_0[nt * P : (nt + 1) * P, cols], in_=out)
 
         for nt in range(NT):
             for which in range(2):
@@ -434,6 +437,8 @@ def tile_list_furnace_zone_checkpoint_kernel(
                 stage2_pass(1, 0, nt, which)
         for nt in range(NT):
             finish(0, nt)
+            if nt < NT - 1:
+                add_base(nc.gpsimd, 0, nt, base_t[nt][:, 0:HALF])
             for which in range(2 if nt < NT - 1 else 1):
                 for g in range(HG):
                     stage2_pass(g, 1, nt, which)
@@ -453,12 +458,16 @@ def tile_list_furnace_zone_checkpoint_kernel(
                 )
             if i == 0:
                 finish(1, 0)
-        for k in range(1, NT - 1):
-            finish(1, k)
+        finish(1, 1)
+        add_base(nc.vector, 0, NT - 1, th_all[1][:, HALF : 2 * HALF])
+        add_base(nc.vector, 1, 0, products[(0, NT - 1)])
+        finish(1, 2)
+        add_base(nc.vector, 1, 1, base_t[1][:, HALF:T2])
         th = th_all[1][:, nt * HALF : (nt + 1) * HALF]
         nc.scalar.activation(out=th, in_=acc2[(1, nt, 0)][:], func=ACT.Tanh)
         for i, qs in enumerate(quarters):
             nc.vector.tensor_tensor(th[:, qs], last_b[i][:, 0 : HALF // 2], th[:, qs], MULT)
+        add_base(nc.vector, 1, 2, base_t[2][:, HALF:T2])
         for i, qs in enumerate(quarters):
             cols = slice(HALF + i * (HALF // 2), HALF + (i + 1) * (HALF // 2))
             nc.vector.tensor_tensor(base_t[nt][:, cols], th[:, qs], base_t[nt][:, cols], ADD)

@@ -104,21 +104,16 @@ def tile_list_furnace_zone_checkpoint_kernel(
         nc.sync.dma_start(idx2[:], offs2)
         load_w1(0, 2)
         load_tab(2)
-        load_page(0, 0)
-        load_w1(1, 0)
-        load_page(0, 1)
-        load_w1(1, 1)
-        load_page(0, 2)
-        load_w1(1, 2)
+        for t in range(KP):
+            load_page(0, t)
+            load_w1(1, t)
         load_page(0, 3)
+        for t in (2, 0, 1, 3):
+            load_page(1, t)
         load_w2(0)
-        load_page(1, 0)
-        load_page(1, 1)
-        load_w2(1)
-        load_page(1, 2)
-        load_page(1, 3)
         w3_w = keep.tile([P, HG, 2 * N], U8, name="w3_w", align_bytes=64)
         nc.sync.dma_start(out=w3_w[:].bitcast(I32), in_=w3_words.bitcast(I32).rearrange("g p c -> p g c"))
+        load_w2(1)
         for nt in range(NT):
             base_t[nt] = keep.tile([P, T2], F32, name="base%d" % nt)
             nc.sync.dma_start(out=base_t[nt][:], in_=base[nt * P : (nt + 1) * P, :])
@@ -140,42 +135,39 @@ def tile_list_furnace_zone_checkpoint_kernel(
                     back[:, jb * P : (jb + 1) * P], dealt[:, jb, t, :, :].rearrange("j q p -> j (q p)"), ident[:]
                 )
             for g in range(HG):
-                wa[(g, t)] = slot_tile("wa%d%d" % (g, t), [P, S], F32, "wa%d%d" % (g, t))
+                wa[(g, t)] = keep.tile([P, S], F32, name="wa%d%d" % (g, t))
                 nc.scalar.activation(out=wa[(g, t)][:], in_=back[:], func=ACT.Copy, scale=amp_t[:, g, t : t + 1])
-
-        def copy_on(eng, out, in_):
-            if eng == "v":
-                nc.vector.tensor_copy(out=out, in_=in_)
-            elif eng == "g":
-                nc.gpsimd.tensor_scalar(out, in_, 1.0, -0.0, MULT, ADD)
-            else:
-                nc.scalar.copy(out=out, in_=in_)
 
         def grouped_tile():
             return keep.tile([P, 4 * 512], BF16, name="grouped", tag="grouped", bufs=3, align_bytes=64)
 
-        def cast_w1(eng, g, a, gr, ms):
+        def cast_views(g, a, gr):
             dst = gr.rearrange("p (t m j) -> p m j t", t=PACK, j=PACK)
             src = w1_raw[(g, a)][:].rearrange("p j (m t) -> p m j t", t=PACK)
-            copy_on(eng, dst[:, ms], src[:, ms])
+            return dst, src
 
-        def cast_w2(eng, g, gr, cs):
-            dst = gr[:].rearrange("p (c i j) -> p c j i", i=4, j=PACK)
+        def cast_w2(g, gr):
+            dst = gr.rearrange("p (c i j) -> p c j i", i=4, j=PACK)
             src = w2_raw[g][:].rearrange("p j (c i) -> p c j i", i=4)
-            copy_on(eng, dst[:, cs], src[:, cs])
+            nc.scalar.copy(out=dst, in_=src)
 
-        def quant(gr, name, slot=None):
-            codes = slot_tile(slot or name, [P, 512], U32, name + "_c")
+        def quant(gr, name):
+            codes = keep.tile([P, 512], U32, name=name + "_c", align_bytes=64)
             scales = keep.tile([P, 512], U8, name=name + "_s", align_bytes=64)
-            nc.vector.quantize_mx(out=codes[:].bitcast(FP8X4), scales=scales[:], in_=gr[:])
+            nc.vector.quantize_mx(out=codes[:].bitcast(FP8X4), scales=scales[:], in_=gr)
             return codes, scales
 
         v_w = []
+        w1q = {}
+        whole = [slice(0, S)]
+        pieces = [slice(0, 128), slice(128, 256), slice(256, S)]
+        piece_banks = (0, 4, 6)
         acc = {}
 
-        def stage1_mm(out, a, t, wq, cols):
+        def stage1_mm(g, t, a, i, cols):
+            wq = w1q[(g, a)]
             nc.tensor.matmul_mx(
-                out=out,
+                out=acc[(g, t)][i][:, 0 : cols.stop - cols.start],
                 lhsT=wq[0][:, t * P : (t + 1) * P].bitcast(FP8X4),
                 lhsT_scale=wq[1][:, t * P : (t + 1) * P],
                 rhs=v_w[a][:, cols].bitcast(FP8X4),
@@ -184,188 +176,173 @@ def tile_list_furnace_zone_checkpoint_kernel(
                 stop=(a == KP - 1),
             )
 
-        halves = [slice(0, S // 2), slice(S // 2, S)]
-        offs_halves = [slice(0, S // 32), slice(S // 32, S // 16)]
+        def acc_cols(g, t, cols):
+            if len(acc[(g, t)]) == 1:
+                return acc[(g, t)][0][:, cols]
+            i = pieces.index(cols)
+            return acc[(g, t)][i][:, 0 : cols.stop - cols.start]
 
-        def stage1_one(g, a, t, wq):
-            if t == 0:
-                if a == 0:
-                    acc[(g, t)] = [bank(PACK * g), bank(PACK * (1 - g))]
-                for hf in range(2):
-                    stage1_mm(acc[(g, t)][hf][:, 0 : S // 2], a, t, wq, halves[hf])
-                return
-            if a == 0:
-                acc[(g, t)] = bank(PACK * g + t)
-            stage1_mm(acc[(g, t)][:], a, t, wq, slice(0, S))
-
-        def stage1_pass(g, a, wq):
-            for t in range(PACK):
-                stage1_one(g, a, t, wq)
-
-        w1q0 = []
-        for a in range(KP - 1):
+        for a in range(KP):
             gr = grouped_tile()
-            cast_w1("v", 0, a, gr[:], slice(0, P))
-            w1q0.append(quant(gr, "w1q0%d" % a))
+            dst, src = cast_views(0, a, gr[:])
+            nc.vector.tensor_copy(out=dst, in_=src)
+            w1q[(0, a)] = quant(gr[:], "w1q0%d" % a)
             if a == 0:
                 v_sc = keep.tile([P, S], U8, name="v_sc", align_bytes=64)
                 nc.vector.tensor_copy(out=v_sc[:], in_=tab_sc[:].indirect(idx[:]))
+                acc[(0, 0)] = [bank(b) for b in piece_banks]
+                for t in range(1, PACK):
+                    acc[(0, t)] = [bank(t)]
             v_w.append(keep.tile([P, S], U32, name="v_w%d" % a, align_bytes=64))
-            nc.vector.tensor_copy(out=v_w[a][:], in_=tab[a][:].indirect(idx[:]))
-        for a in range(KP - 1):
-            stage1_pass(0, a, w1q0[a])
-        a = KP - 1
-        gr = slot_tile("w1raw00", [P, 4 * 512], BF16, "gr02")
-        cast_w1("v", 0, a, gr[:], slice(0, P))
-        wq = quant(gr, "w1q0%d" % a)
-        v_w.append(slot_tile("w1raw00", [P, S], U32, "v_w2"))
-        for hf in range(2):
-            nc.vector.tensor_copy(out=v_w[a][:, halves[hf]], in_=tab[a][:].indirect(idx[:, offs_halves[hf]]))
-        stage1_pass(0, a, wq)
+            for cols in pieces if a == KP - 1 else whole:
+                nc.vector.tensor_copy(
+                    out=v_w[a][:, cols], in_=tab[a][:].indirect(idx[:, cols.start // 16 : cols.stop // 16])
+                )
+            for i, cols in enumerate(pieces):
+                stage1_mm(0, 0, a, i, cols)
+            for t in range(1, PACK):
+                stage1_mm(0, t, a, 0, whole[0])
 
-        def resonance(src, us, h):
-            nc.scalar.activation(out=us, in_=src, func=ACT.Square)
-            nc.scalar.activation(out=us, in_=us, func=ACT.Abs_reciprocal_sqrt, bias=1.0)
-            nc.scalar.activation(out=h, in_=us, func=ACT.Square)
+        def resonance(g, t, parts, us, h):
+            for cols in parts:
+                nc.scalar.activation(out=us[:, cols], in_=acc_cols(g, t, cols), func=ACT.Square)
+            for cols in parts:
+                nc.scalar.activation(out=us[:, cols], in_=us[:, cols], func=ACT.Abs_reciprocal_sqrt, bias=1.0)
+            for cols in parts:
+                nc.scalar.activation(out=h[:, cols], in_=us[:, cols], func=ACT.Square)
+
+        def weigh(g, t, h, cols):
+            nc.gpsimd.tensor_tensor(wa[(g, t)][:, cols], h[:, cols], wa[(g, t)][:, cols], MULT)
+
+        def window(g, t, cols):
+            return page[(g, t)][:].indirect(idx2[:, cols.start // 16 : cols.stop // 16])
+
+        def scatter(g, t, cols):
+            nc.vector.tensor_copy(out=window(g, t, cols), in_=wa[(g, t)][:, cols])
+
+        def scatter_fused(g, t, cols, h):
+            nc.vector.tensor_tensor(window(g, t, cols), h, wa[(g, t)][:, cols], MULT)
 
         def store_page(g, t):
             nc.sync.dma_start(out=out1_v[g, t], in_=page[(g, t)][:])
 
-        def weigh(g, t, h, cols):
-            nc.gpsimd.tensor_tensor(wa[(g, t)][:, cols], h, wa[(g, t)][:, cols], MULT)
-
-        def scatter(g, t):
-            nc.vector.tensor_copy(out=page[(g, t)][:].indirect(idx2[:]), in_=wa[(g, t)][:])
-            store_page(g, t)
-
-        def scatter_half(g, t, hf):
-            nc.vector.tensor_copy(out=page[(g, t)][:].indirect(idx2[:, offs_halves[hf]]), in_=wa[(g, t)][:, halves[hf]])
-
-        def scatter_half_fused(g, t, hf, h):
-            nc.vector.tensor_tensor(
-                page[(g, t)][:].indirect(idx2[:, offs_halves[hf]]), h, wa[(g, t)][:, halves[hf]], MULT
-            )
+        halves = [slice(0, S // 2), slice(S // 2, S)]
 
         def respond(g, t, us, h):
-            resonance(acc[(g, t)][:], us, h)
-            weigh(g, t, h, slice(0, S))
-            scatter(g, t)
-
-        def respond_halves(g, t, us, h):
-            for hf in range(2):
-                resonance(acc[(g, t)][hf][:, 0 : S // 2], us[:, halves[hf]], h[hf])
-                weigh(g, t, h[hf], halves[hf])
-                scatter_half(g, t, hf)
+            resonance(g, t, halves, us, h)
+            weigh(g, t, h, whole[0])
+            scatter(g, t, whole[0])
             store_page(g, t)
 
+        def respond_first(g, t, us, h):
+            resonance(g, t, pieces[0:2], us, h)
+            weigh(g, t, h, pieces[0])
+            scatter(g, t, pieces[0])
+            resonance(g, t, pieces[2:3], us, h)
+            weigh(g, t, h, slice(128, S))
+            scatter(g, t, slice(128, S))
+            store_page(g, t)
+
+        def round_on_gpsimd(out, in_):
+            nc.gpsimd.tensor_scalar(out, in_, 1.0, -0.0, MULT, ADD)
+
         rounded0 = slot_tile("rounded0", [P, PACK * HALF], F32, "rounded0")
-        pairs1 = [keep.tile([P, 2 * HALF], F32, name="pairs1%d" % hf) for hf in range(2)]
+        pairs = keep.tile([P, 2 * T2], F32, name="pairs")
         pq_s = keep.tile([P, HG, T2], U8, name="pq_s", align_bytes=64)
-        pq_c = {}
 
         def row0(t):
             return rounded0[:, t * HALF : (t + 1) * HALF]
 
-        def words1(u, hf):
-            return pairs1[hf][:, u * HALF : (u + 1) * HALF]
+        def pair_lane(t):
+            words = pairs[:, (t // 2) * T2 : (t // 2 + 1) * T2]
+            return words.bitcast(BF16).rearrange("p (m e) -> p m e", e=2)[:, :, t % 2]
 
         def round0(t):
-            copy_on("g", row0(t).bitcast(BF16), page[(0, t)][:])
+            round_on_gpsimd(row0(t).bitcast(BF16), page[(0, t)][:])
 
-        def round1(eng, t, hf):
-            dst = words1(t // 2, hf).bitcast(BF16).rearrange("p (m e) -> p m e", e=2)
-            copy_on(eng, dst[:, :, t % 2], page[(1, t)][:, hf * HALF : (hf + 1) * HALF])
+        def round1(t):
+            round_on_gpsimd(pair_lane(t), page[(1, t)][:])
 
-        def interleave0(hf, gr):
-            src = rounded0[:].bitcast(BF16).rearrange("p (t h c i) -> p h c t i", t=PACK, h=2, i=4)
-            nc.scalar.copy(out=gr[:].rearrange("p (c i t) -> p c t i", i=4, t=PACK), in_=src[:, hf])
-            return gr
+        def cast1(a, gr):
+            dst, src = cast_views(1, a, gr)
+            nc.scalar.copy(out=dst, in_=src)
+            w1q[(1, a)] = quant(gr, "w1q1%d" % a)
+            if a == 0:
+                acc[(1, 2)] = [bank(b) for b in piece_banks]
+            for i, cols in enumerate(pieces):
+                stage1_mm(1, 2, a, i, cols)
 
-        def weave1(eng, hf, gr):
-            copy_on(
-                eng,
-                gr[:].bitcast(F32).rearrange("p (m u) -> p m u", u=2),
-                pairs1[hf][:].rearrange("p (u m) -> p m u", u=2),
-            )
-            return gr
+        spare_a = slot_tile("w1raw00", [P, PACK * S], F32, "spare_a")
+        spare_b = slot_tile("w1raw01", [P, PACK * S], F32, "spare_b")
 
-        def quant_page(g, hf, gr, codes):
-            cols = slice(hf * HALF, (hf + 1) * HALF)
-            pq_c[(g, hf)] = codes
-            nc.vector.quantize_mx(out=codes[:].bitcast(FP8X4), scales=pq_s[:, g, cols], in_=gr[:])
-            nc.sync.dma_start(
-                out=out_2[g].rearrange("p m t -> p (m t)").bitcast(I32)[:, cols], in_=codes[:].bitcast(I32)
-            )
+        def part(tl, i):
+            return tl[:, i * S : (i + 1) * S]
 
-        def codes_tile(g, hf):
-            return keep.tile([P, HALF], U32, name="pq_c%d%d" % (g, hf), align_bytes=64)
-
-        spare = slot_tile("w1raw02", [P, PACK * S], F32, "spare")
-        respond_halves(0, 0, spare[:, 0:S], [spare[:, S : S + S // 2], spare[:, S + S // 2 : 2 * S]])
-        gr10 = grouped_tile()
         gr1x = slot_tile("dealt", [P, 2 * 2048], BF16, "gr1x")
-        respond(0, 1, gr10[:].bitcast(F32)[:, 0:S], row0(0))
-        cast_w1("s", 1, 0, gr10[:], slice(0, P))
-        stage1_pass(1, 0, quant(gr10, "w1q10", "wa01"))
+        gr1x_f = gr1x[:].bitcast(F32)
+        early = [slice(0, 192), slice(192, 384)]
+        late = slice(384, S)
+
+        respond_first(0, 0, part(spare_a, 0), part(spare_a, 1))
+        respond(0, 1, part(spare_a, 2), row0(0))
         round0(0)
-        respond(0, 2, gr1x[:].bitcast(F32)[:, 0:S], row0(1))
-        cast_w1("s", 1, 1, gr1x[:, 0:2048], slice(0, P))
-        h03 = spare[:, S : 2 * S]
-        resonance(acc[(0, 3)][:, halves[1]], gr1x[:].bitcast(F32)[:, 2 * S : 2 * S + S // 2], h03[:, halves[1]])
+        respond(0, 2, gr1x_f[:, 0:S], row0(1))
+        cast1(0, gr1x[:, 0:2048])
         round0(1)
-        weigh(0, 3, h03[:, halves[1]], halves[1])
-        cast_w1("s", 1, 2, gr1x[:, 2048:4096], slice(0, P))
-        late_c = keep.tile([P, 1024], U32, name="w1q1x_c", align_bytes=64)
-        late_s = keep.tile([P, 1024], U8, name="w1q1x_s", align_bytes=64)
-        nc.vector.quantize_mx(out=late_c[:].bitcast(FP8X4), scales=late_s[:], in_=gr1x[:])
-        late = [(late_c[:, 512 * i : 512 * (i + 1)], late_s[:, 512 * i : 512 * (i + 1)]) for i in range(2)]
-        us03 = slot_tile("w1raw12", [P, S // 2], F32, "us03")
-        resonance(acc[(0, 3)][:, halves[0]], us03[:], h03[:, halves[0]])
-        scatter_half_fused(0, 3, 0, h03[:, halves[0]])
-        scatter_half(0, 3, 1)
-        store_page(0, 3)
-        for hf in range(2):
-            for a in (1, 2):
-                stage1_mm(acc[(1, 0)][hf][:, 0 : S // 2], a, 0, late[a - 1], halves[hf])
-        for t in range(1, PACK):
-            stage1_one(1, 1, t, late[0])
-            stage1_one(1, 2, t, late[1])
-        grw0 = slot_tile("w1raw12", [P, 4 * 512], BF16, "grw0")
-        cast_w2("s", 0, grw0, slice(0, P // 2))
-        respond_halves(1, 0, spare[:, 2 * S : 3 * S], [row0(2)[:, halves[hf]] for hf in range(2)])
+        resonance(0, 3, early, gr1x_f[:, 2 * S : 3 * S], row0(2))
+        weigh(0, 3, row0(2), slice(0, 384))
+        scatter(0, 3, early[0])
         round0(2)
-        respond(1, 1, spare[:, 3 * S : 4 * S], row0(3))
+        cast1(1, gr1x[:, 2048:4096])
+        cast1(2, grouped_tile()[:])
+        late3 = slot_tile("w1raw12", [P, 2 * S], F32, "late3")
+        resonance(0, 3, [late], part(late3, 0), part(late3, 1))
+        scatter_fused(0, 3, late, part(late3, 1)[:, late])
+        scatter(0, 3, early[1])
+        store_page(0, 3)
+
+        def stage1_tile(t, b):
+            acc[(1, t)] = [bank(b)]
+            for a in range(KP):
+                stage1_mm(1, t, a, 0, whole[0])
+
+        respond_first(1, 2, part(spare_b, 0), part(spare_b, 1))
+        stage1_tile(0, piece_banks[0])
+        respond(1, 0, part(spare_b, 2), row0(3))
         round0(3)
-        us12 = grw0[:].bitcast(F32)[:, S : 2 * S]
-        nc.scalar.activation(out=us12, in_=acc[(1, 2)][:], func=ACT.Square)
-        nc.scalar.activation(out=words1(0, 1), in_=us12, func=ACT.Abs_reciprocal_sqrt, bias=1.0)
-        nc.scalar.activation(out=words1(0, 0), in_=words1(0, 1), func=ACT.Square)
-        weigh(1, 2, words1(0, 0), slice(0, S))
-        scatter(1, 2)
-        for t in range(2):
-            for hf in range(2):
-                round1("g", t, hf)
-        cast_w2("s", 0, grw0, slice(P // 2, P))
-        w2q = [quant(grw0, "w2q0", "wa12")]
-        round1("v", 2, 0)
-        us13 = spare[:, S : 2 * S]
-        r13 = words1(1, 1)
-        h13a = slot_tile("tab2", [P, S // 2], F32, "h13a")
-        nc.scalar.activation(out=us13, in_=acc[(1, 3)][:], func=ACT.Square)
-        nc.scalar.activation(out=r13, in_=us13, func=ACT.Abs_reciprocal_sqrt, bias=1.0)
-        nc.scalar.activation(out=h13a[:], in_=r13[:, halves[0]], func=ACT.Square)
-        quant_page(0, 1, interleave0(1, grouped_tile()), codes_tile(0, 1))
-        scatter_half_fused(1, 3, 0, h13a[:])
-        gr00 = interleave0(0, slot_tile("tab0", [P, 4 * 512], BF16, "gr00"))
-        quant_page(0, 0, gr00, slot_tile("tab2", [P, HALF], U32, "pq_c00"))
-        grw1 = slot_tile("rounded0", [P, 4 * 512], BF16, "grw1")
-        cast_w2("s", 1, grw1, slice(0, P))
-        w2q.append(quant(grw1, "w2q1"))
-        h13b = slot_tile("tab0", [P, S // 2], F32, "h13b")
-        nc.scalar.activation(out=h13b[:], in_=r13[:, halves[1]], func=ACT.Square)
-        scatter_half_fused(1, 3, 1, h13b[:])
+        stage1_tile(1, piece_banks[1])
+        respond(1, 1, part(spare_b, 3), pairs[:, T2 : T2 + S])
+        round1(2)
+        stage1_tile(3, piece_banks[2])
+        gr0 = slot_tile("w1raw02", [P, 2 * 2048], BF16, "gr0")
+        grw1 = slot_tile("tab2", [P, 2048], BF16, "grw1")
+        r_late = grw1[:].bitcast(F32)[:, 0:S]
+        nc.scalar.activation(out=r_late[:, late], in_=acc_cols(1, 3, late), func=ACT.Square)
+        resonance(1, 3, early, gr0[:].bitcast(F32)[:, 0:S], pairs[:, 0:S])
+        nc.scalar.activation(out=r_late[:, late], in_=r_late[:, late], func=ACT.Abs_reciprocal_sqrt, bias=1.0)
+        weigh(1, 3, pairs[:, 0:S], slice(0, 384))
+        scatter(1, 3, slice(0, 384))
+        round1(0)
+        round1(1)
+        nc.scalar.copy(
+            out=gr0[:].rearrange("p (c i t) -> p c t i", i=4, t=PACK),
+            in_=rounded0[:].bitcast(BF16).rearrange("p (t c i) -> p c t i", t=PACK, i=4),
+        )
+        pq_c = [slot_tile("tab%d" % g, [P, T2], U32, "pq_c%d" % g) for g in range(HG)]
+
+        def store_codes(g):
+            nc.sync.dma_start(out=out_2[g].rearrange("p m t -> p (m t)").bitcast(I32), in_=pq_c[g][:].bitcast(I32))
+
+        nc.vector.quantize_mx(out=pq_c[0][:].bitcast(FP8X4), scales=pq_s[:, 0, :], in_=gr0[:])
+        store_codes(0)
+        grw0 = slot_tile("rounded0", [P, 2048], BF16, "grw0")
+        cast_w2(0, grw0[:])
+        w2q = [quant(grw0[:], "w2q0")]
+        h_late = slot_tile("w2raw0", [P, S], F32, "h_late")
+        nc.scalar.activation(out=h_late[:, late], in_=r_late[:, late], func=ACT.Square)
+        scatter_fused(1, 3, late, h_late[:, late])
         store_page(1, 3)
-        round1("s", 2, 1)
+        cast_w2(1, grw1[:])
 
         acc2 = {}
 
@@ -383,20 +360,19 @@ def tile_list_furnace_zone_checkpoint_kernel(
                 out=acc2[(hf, nt, which)][:],
                 lhsT=lhsT,
                 lhsT_scale=lhsT_scale,
-                rhs=pq_c[(g, hf)][:].bitcast(FP8X4),
+                rhs=pq_c[g][:, cols].bitcast(FP8X4),
                 rhs_scale=pq_s[:, g, cols],
                 start=(g == 0),
                 stop=(g == HG - 1),
             )
 
         th_all = [slot_tile("w1raw1%d" % hf, [P, NT * HALF], F32, "th%d" % hf) for hf in range(2)]
-
         products = {}
 
         def finish(hf, nt):
             th = th_all[hf][:, nt * HALF : (nt + 1) * HALF]
             nc.scalar.activation(out=th, in_=acc2[(hf, nt, 0)][:], func=ACT.Tanh)
-            products[(hf, nt)] = spare[:, S : 2 * S] if (hf, nt) == (1, 1) else th
+            products[(hf, nt)] = part(spare_a, 0) if (hf, nt) == (1, 1) else th
             nc.vector.tensor_tensor(products[(hf, nt)], acc2[(hf, nt, 1)][:], th, MULT)
 
         def add_base(adder, hf, nt, out):
@@ -404,37 +380,48 @@ def tile_list_furnace_zone_checkpoint_kernel(
             adder.tensor_tensor(out, products[(hf, nt)], base_t[nt][:, cols], ADD)
             nc.sync.dma_start(out=out_0[nt * P : (nt + 1) * P, cols], in_=out)
 
-        for nt in range(NT):
-            for which in range(2):
+        for which in range(2):
+            for nt in range(NT):
                 stage2_pass(0, 0, nt, which)
+
+        def weave(gr, cols):
+            first = cols.start % HALF
+            nc.vector.tensor_copy(
+                out=gr[:].bitcast(F32).rearrange("p (m u) -> p m u", u=2)[:, first : first + cols.stop - cols.start],
+                in_=pairs[:].rearrange("p (u m) -> p m u", u=2)[:, cols],
+            )
+
+        def quant_page1(gr, cols):
+            first = PACK * (cols.start % HALF)
+            nc.vector.quantize_mx(
+                out=pq_c[1][:, cols].bitcast(FP8X4),
+                scales=pq_s[:, 1, cols],
+                in_=gr[:, first : first + PACK * (cols.stop - cols.start)],
+            )
+
         quarters = [slice(0, HALF // 2), slice(HALF // 2, HALF)]
-        last0 = words1(1, 0).bitcast(BF16).rearrange("p (m e) -> p m e", e=2)
+        second = slice(HALF, T2)
         for qs in quarters:
-            nc.vector.tensor_copy(out=last0[:, qs, 1], in_=page[(1, 3)][:, qs])
-        round1("s", 3, 1)
+            nc.vector.tensor_copy(out=pair_lane(3)[:, qs], in_=page[(1, 3)][:, qs])
         gr = grouped_tile()
         for qs in quarters:
-            nc.vector.tensor_copy(
-                out=gr[:].bitcast(F32).rearrange("p (m u) -> p m u", u=2)[:, qs],
-                in_=pairs1[0][:].rearrange("p (u m) -> p m u", u=2)[:, qs],
-            )
-        pq_c[(1, 0)] = codes_tile(1, 0)
-        for i, qs in enumerate(quarters):
-            nc.vector.quantize_mx(
-                out=pq_c[(1, 0)][:, qs].bitcast(FP8X4), scales=pq_s[:, 1, qs], in_=gr[:, i * 1024 : (i + 1) * 1024]
-            )
-        nc.sync.dma_start(
-            out=out_2[1].rearrange("p m t -> p (m t)").bitcast(I32)[:, 0:HALF], in_=pq_c[(1, 0)][:].bitcast(I32)
-        )
-        quant_page(1, 1, weave1("v", 1, grouped_tile()), codes_tile(1, 1))
+            weave(gr, qs)
+        for qs in quarters:
+            quant_page1(gr, qs)
+        nc.vector.tensor_copy(out=pair_lane(3)[:, second], in_=page[(1, 3)][:, second])
+        w2q.append(quant(grw1[:], "w2q1"))
+        gr = grouped_tile()
+        weave(gr, second)
+        for which in range(2):
+            for nt in range(NT):
+                stage2_pass(1, 0, nt, which)
+        quant_page1(gr, second)
+        store_codes(1)
         for q in range(4):
             nc.sync.dma_start(
                 out=out_3[:, 4 * q : 4 * q + 4, :].bitcast(I32).rearrange("g r m -> r g m"),
                 in_=pq_s[32 * q : 32 * q + 4, :, :].bitcast(I32),
             )
-        for nt in range(NT):
-            for which in range(2):
-                stage2_pass(1, 0, nt, which)
         for nt in range(NT):
             finish(0, nt)
             if nt < NT - 1:
@@ -451,8 +438,8 @@ def tile_list_furnace_zone_checkpoint_kernel(
                     out=last_b[i][:, 0 : HALF // 2],
                     lhsT=w2q[g][0][:, nt * P : (nt + 1) * P].bitcast(FP8X4),
                     lhsT_scale=w2q[g][1][:, nt * P : (nt + 1) * P],
-                    rhs=pq_c[(g, 1)][:, qs].bitcast(FP8X4),
-                    rhs_scale=pq_s[:, g, HALF + i * (HALF // 2) : HALF + (i + 1) * (HALF // 2)],
+                    rhs=pq_c[g][:, HALF + qs.start : HALF + qs.stop].bitcast(FP8X4),
+                    rhs_scale=pq_s[:, g, HALF + qs.start : HALF + qs.stop],
                     start=(g == 0),
                     stop=(g == HG - 1),
                 )

@@ -43,7 +43,7 @@ def tile_list_furnace_zone_checkpoint_kernel(
         def slot_tile(slot, shape, dtype, name):
             return keep.tile(shape, dtype, name=name, tag=slot, align_bytes=64)
 
-        tab_sc = keep.tile([P, T], U8, name="tab_sc", align_bytes=64)
+        tab_sc = slot_tile("chain", [P, T], U8, "tab_sc")
         nc.vector.memset(tab_sc[:].bitcast(I32), 0)
         w3_sc = keep.tile([P, HG, N], U8, name="w3_sc", align_bytes=64)
         nc.vector.memset(w3_sc[:].bitcast(I32), 0)
@@ -139,7 +139,7 @@ def tile_list_furnace_zone_checkpoint_kernel(
                 nc.scalar.activation(out=wa[(g, t)][:], in_=back[:], func=ACT.Copy, scale=amp_t[:, g, t : t + 1])
 
         def grouped_tile():
-            return keep.tile([P, 4 * 512], BF16, name="grouped", tag="grouped", bufs=3, align_bytes=64)
+            return keep.tile([P, 4 * 512], BF16, name="grouped", tag="grouped", bufs=2, align_bytes=64)
 
         def cast_views(g, a, gr):
             dst = gr.rearrange("p (t m j) -> p m j t", t=PACK, j=PACK)
@@ -182,10 +182,15 @@ def tile_list_furnace_zone_checkpoint_kernel(
             i = pieces.index(cols)
             return acc[(g, t)][i][:, 0 : cols.stop - cols.start]
 
+        head_slots = ("grouped0", "chain", "w1raw01")
         for a in range(KP):
-            gr = grouped_tile()
+            gr = slot_tile(head_slots[a], [P, 2048], BF16, "gr0%d" % a)
             dst, src = cast_views(0, a, gr[:])
-            nc.vector.tensor_copy(out=dst, in_=src)
+            if a == KP - 1:
+                nc.scalar.copy(out=dst[:, 0:40], in_=src[:, 0:40])
+                nc.vector.tensor_copy(out=dst[:, 40:P], in_=src[:, 40:P])
+            else:
+                nc.vector.tensor_copy(out=dst, in_=src)
             w1q[(0, a)] = quant(gr[:], "w1q0%d" % a)
             if a == 0:
                 v_sc = keep.tile([P, S], U8, name="v_sc", align_bytes=64)
@@ -193,7 +198,7 @@ def tile_list_furnace_zone_checkpoint_kernel(
                 acc[(0, 0)] = [bank(b) for b in piece_banks]
                 for t in range(1, PACK):
                     acc[(0, t)] = [bank(t)]
-            v_w.append(keep.tile([P, S], U32, name="v_w%d" % a, align_bytes=64))
+            v_w.append(slot_tile("v_w0" if a == 0 else head_slots[a], [P, S], U32, "v_w%d" % a))
             for cols in pieces if a == KP - 1 else whole:
                 nc.vector.tensor_copy(
                     out=v_w[a][:, cols], in_=tab[a][:].indirect(idx[:, cols.start // 16 : cols.stop // 16])
@@ -273,7 +278,6 @@ def tile_list_furnace_zone_checkpoint_kernel(
                 stage1_mm(1, 2, a, i, cols)
 
         spare_a = slot_tile("w1raw00", [P, PACK * S], F32, "spare_a")
-        spare_b = slot_tile("w1raw01", [P, PACK * S], F32, "spare_b")
 
         def part(tl, i):
             return tl[:, i * S : (i + 1) * S]
@@ -294,7 +298,8 @@ def tile_list_furnace_zone_checkpoint_kernel(
         scatter(0, 3, early[0])
         round0(2)
         cast1(1, gr1x[:, 2048:4096])
-        cast1(2, grouped_tile()[:])
+        cast1(2, slot_tile("w1raw11", [P, 2048], BF16, "gr12")[:])
+        spare_b = slot_tile("w1raw10", [P, PACK * S], F32, "spare_b")
         late3 = slot_tile("w1raw12", [P, 2 * S], F32, "late3")
         resonance(0, 3, [late], part(late3, 0), part(late3, 1))
         scatter_fused(0, 3, late, part(late3, 1)[:, late])

@@ -55,11 +55,6 @@ def tile_list_furnace_zone_checkpoint_kernel(
         ident = keep.tile([P, P], F32, name="ident")
         make_identity(nc, ident[:])
         amp_t = keep.tile([P, HG, PACK], F32, name="amp_t")
-        for q in range(4):
-            nc.gpsimd.dma_start(
-                out=w3_sc[32 * q : 32 * q + 4, :, :].bitcast(I32),
-                in_=w3_scales[:, 4 * q : 4 * q + 4, :].bitcast(I32).rearrange("g r c -> r g c"),
-            )
 
         idx = lists.tile([P, S // 16], U16, name="idx")
         idx2 = lists.tile([P, S // 16], U16, name="idx2")
@@ -105,14 +100,19 @@ def tile_list_furnace_zone_checkpoint_kernel(
         load_w1(0, 2)
         load_tab(2)
         for t in range(KP):
-            load_page(0, t)
+            load_page(0, (0, 2, 1)[t])
             load_w1(1, t)
         load_page(0, 3)
-        for t in (2, 0, 1, 3):
+        for t in (0, 2, 3, 1):
             load_page(1, t)
         load_w2(0)
         w3_w = keep.tile([P, HG, 2 * N], U8, name="w3_w", align_bytes=64)
         nc.sync.dma_start(out=w3_w[:].bitcast(I32), in_=w3_words.bitcast(I32).rearrange("g p c -> p g c"))
+        for q in range(4):
+            nc.sync.dma_start(
+                out=w3_sc[32 * q : 32 * q + 4, :, :].bitcast(I32),
+                in_=w3_scales[:, 4 * q : 4 * q + 4, :].bitcast(I32).rearrange("g r c -> r g c"),
+            )
         load_w2(1)
         for nt in range(NT):
             base_t[nt] = keep.tile([P, T2], F32, name="base%d" % nt)
@@ -121,22 +121,30 @@ def tile_list_furnace_zone_checkpoint_kernel(
         warm = keep.tile([P, 1], F32, name="warm")
         nc.scalar.activation(out=warm[:], in_=ident[:, 0:1], func=ACT.Abs_reciprocal_sqrt, bias=1.0)
 
-        wgs_T = bank(5)
-        for jb in range(4):
-            nc.tensor.transpose(wgs_T[:, jb * P : (jb + 1) * P], wgs_t[:, jb * P : (jb + 1) * P], ident[:])
-        dealt = slot_tile("dealt", [P, 4, PACK, 4, 32], F32, "dealt")
-        for q in range(4):
-            nc.scalar.copy(out=dealt[:, :, :, q, :], in_=wgs_T[:].rearrange("j (b p t) -> j b t p", b=4, t=PACK))
+        dealt = [slot_tile("dealt%d" % i, [P, 2, PACK, 4, 32], F32, "dealt%d" % i) for i in range(2)]
+        for jb, b in enumerate((0, 1, 4, 5)):
+            wgs_T = bank(b)
+            nc.tensor.transpose(wgs_T[:, 0:P], wgs_t[:, jb * P : (jb + 1) * P], ident[:])
+            rows = wgs_T[:, 0:P].rearrange("j (p t) -> j t p", t=PACK)
+            nc.scalar.copy(out=dealt[jb // 2][:, jb % 2], in_=rows.unsqueeze(2).to_broadcast([P, PACK, 4, 32]))
         wa = {}
-        for t in range(PACK):
-            back = bank(5 + (t + 1) % 3)
+        back = []
+        for t, b in enumerate((2, 3, 6, 7)):
+            back.append(bank(b))
             for jb in range(4):
                 nc.tensor.transpose(
-                    back[:, jb * P : (jb + 1) * P], dealt[:, jb, t, :, :].rearrange("j q p -> j (q p)"), ident[:]
+                    back[t][:, jb * P : (jb + 1) * P],
+                    dealt[jb // 2][:, jb % 2, t, :, :].rearrange("j q p -> j (q p)"),
+                    ident[:],
                 )
-            for g in range(HG):
-                wa[(g, t)] = keep.tile([P, S], F32, name="wa%d%d" % (g, t))
-                nc.scalar.activation(out=wa[(g, t)][:], in_=back[:], func=ACT.Copy, scale=amp_t[:, g, t : t + 1])
+
+        def weights(g, tile):
+            for t in range(PACK):
+                wa[(g, t)] = tile[:, t * S : (t + 1) * S]
+                nc.scalar.activation(out=wa[(g, t)], in_=back[t][:], func=ACT.Copy, scale=amp_t[:, g, t : t + 1])
+
+        for g in range(HG):
+            weights(g, keep.tile([P, PACK * S], F32, name="wa%d" % g))
 
         def grouped_tile():
             return keep.tile([P, 4 * 512], BF16, name="grouped", tag="grouped", bufs=2, align_bytes=64)
@@ -151,9 +159,9 @@ def tile_list_furnace_zone_checkpoint_kernel(
             src = w2_raw[g][:].rearrange("p j (c i) -> p c j i", i=4)
             nc.scalar.copy(out=dst, in_=src)
 
-        def quant(gr, name):
-            codes = keep.tile([P, 512], U32, name=name + "_c", align_bytes=64)
-            scales = keep.tile([P, 512], U8, name=name + "_s", align_bytes=64)
+        def quant(gr, name, words=512, slot=None):
+            codes = slot_tile(slot or name, [P, words], U32, name + "_c")
+            scales = keep.tile([P, words], U8, name=name + "_s", align_bytes=64)
             nc.vector.quantize_mx(out=codes[:].bitcast(FP8X4), scales=scales[:], in_=gr)
             return codes, scales
 
@@ -161,20 +169,28 @@ def tile_list_furnace_zone_checkpoint_kernel(
         w1q = {}
         whole = [slice(0, S)]
         pieces = [slice(0, 128), slice(128, 256), slice(256, S)]
-        piece_banks = (0, 4, 6)
+        piece_banks = ((0, 4, 5), (2, 3, 6))
         acc = {}
 
         def stage1_mm(g, t, a, i, cols):
-            wq = w1q[(g, a)]
+            if a == KP - 1:
+                wq, place = w1q[(g, a, t % 2)], t // 2
+            else:
+                wq, place = w1q[(g, a)], t
             nc.tensor.matmul_mx(
                 out=acc[(g, t)][i][:, 0 : cols.stop - cols.start],
-                lhsT=wq[0][:, t * P : (t + 1) * P].bitcast(FP8X4),
-                lhsT_scale=wq[1][:, t * P : (t + 1) * P],
+                lhsT=wq[0][:, place * P : (place + 1) * P].bitcast(FP8X4),
+                lhsT_scale=wq[1][:, place * P : (place + 1) * P],
                 rhs=v_w[a][:, cols].bitcast(FP8X4),
                 rhs_scale=v_sc[4 * a : P, cols],
                 start=(a == 0),
                 stop=(a == KP - 1),
             )
+
+        def stage1_tile(g, t, b):
+            acc[(g, t)] = [bank(b)]
+            for a in range(KP):
+                stage1_mm(g, t, a, 0, whole[0])
 
         def acc_cols(g, t, cols):
             if len(acc[(g, t)]) == 1:
@@ -182,39 +198,57 @@ def tile_list_furnace_zone_checkpoint_kernel(
             i = pieces.index(cols)
             return acc[(g, t)][i][:, 0 : cols.stop - cols.start]
 
-        head_slots = ("grouped0", "chain", "w1raw01")
-        for a in range(KP):
-            gr = slot_tile(head_slots[a], [P, 2048], BF16, "gr0%d" % a)
+        def cast0(a, slot):
+            gr = slot_tile(slot, [P, 2048], BF16, "gr0%d" % a)
             dst, src = cast_views(0, a, gr[:])
-            if a == KP - 1:
-                nc.scalar.copy(out=dst[:, 0:40], in_=src[:, 0:40])
-                nc.vector.tensor_copy(out=dst[:, 40:P], in_=src[:, 40:P])
-            else:
-                nc.vector.tensor_copy(out=dst, in_=src)
+            nc.vector.tensor_copy(out=dst, in_=src)
             w1q[(0, a)] = quant(gr[:], "w1q0%d" % a)
-            if a == 0:
-                v_sc = keep.tile([P, S], U8, name="v_sc", align_bytes=64)
-                nc.vector.tensor_copy(out=v_sc[:], in_=tab_sc[:].indirect(idx[:]))
-                acc[(0, 0)] = [bank(b) for b in piece_banks]
-                for t in range(1, PACK):
-                    acc[(0, t)] = [bank(t)]
-            v_w.append(slot_tile("v_w0" if a == 0 else head_slots[a], [P, S], U32, "v_w%d" % a))
-            for cols in pieces if a == KP - 1 else whole:
+
+        def cast_parity(copy, g, e, gr):
+            src = w1_raw[(g, KP - 1)][:].rearrange("p j (m u e) -> p e m j u", u=2, e=2)[:, e]
+            copy(out=gr.rearrange("p (u m j) -> p m j u", u=2, j=PACK), in_=src)
+
+        def gather(a, slot, parts):
+            v_w.append(slot_tile(slot, [P, S], U32, "v_w%d" % a))
+            for cols in parts:
                 nc.vector.tensor_copy(
                     out=v_w[a][:, cols], in_=tab[a][:].indirect(idx[:, cols.start // 16 : cols.stop // 16])
                 )
+
+        def first_tile_pass(a):
             for i, cols in enumerate(pieces):
                 stage1_mm(0, 0, a, i, cols)
-            for t in range(1, PACK):
-                stage1_mm(0, t, a, 0, whole[0])
+
+        cast0(0, "grouped0")
+        gather(0, "v_w0", whole)
+        cast0(1, "grouped1")
+        gather(1, "v_w1", whole)
+        v_sc = keep.tile([P, S], U8, name="v_sc", align_bytes=64)
+        nc.vector.tensor_copy(out=v_sc[:], in_=tab_sc[:].indirect(idx[:]))
+        acc[(0, 0)] = [bank(b) for b in piece_banks[0]]
+        acc[(0, 2)] = [bank(1)]
+        for a in range(KP - 1):
+            first_tile_pass(a)
+            stage1_mm(0, 2, a, 0, whole[0])
+        gr02 = [slot_tile(slot, [P, 1024], BF16, "gr02" + slot) for slot in ("chain", "dealt0")]
+        cast_parity(nc.vector.tensor_copy, 0, 0, gr02[0][:])
+        cast_parity(nc.scalar.copy, 0, 1, gr02[1][:])
+        w1q[(0, 2, 0)] = quant(gr02[0][:], "w1q020", 2 * P)
+        gather(2, "chain", pieces)
+        first_tile_pass(2)
+        stage1_mm(0, 2, 2, 0, whole[0])
+        w1q[(0, 2, 1)] = quant(gr02[1][:], "w1q021", 2 * P, slot="tab2")
+
+        def resonance_in(g, t, parts, scratch, h):
+            for cols, us in zip(parts, scratch):
+                nc.scalar.activation(out=us, in_=acc_cols(g, t, cols), func=ACT.Square)
+            for us in scratch:
+                nc.scalar.activation(out=us, in_=us, func=ACT.Abs_reciprocal_sqrt, bias=1.0)
+            for cols, us in zip(parts, scratch):
+                nc.scalar.activation(out=h[:, cols], in_=us, func=ACT.Square)
 
         def resonance(g, t, parts, us, h):
-            for cols in parts:
-                nc.scalar.activation(out=us[:, cols], in_=acc_cols(g, t, cols), func=ACT.Square)
-            for cols in parts:
-                nc.scalar.activation(out=us[:, cols], in_=us[:, cols], func=ACT.Abs_reciprocal_sqrt, bias=1.0)
-            for cols in parts:
-                nc.scalar.activation(out=h[:, cols], in_=us[:, cols], func=ACT.Square)
+            resonance_in(g, t, parts, [us[:, cols] for cols in parts], h)
 
         def weigh(g, t, h, cols):
             nc.gpsimd.tensor_tensor(wa[(g, t)][:, cols], h[:, cols], wa[(g, t)][:, cols], MULT)
@@ -241,11 +275,22 @@ def tile_list_furnace_zone_checkpoint_kernel(
 
         def respond_first(g, t, us, h):
             resonance(g, t, pieces[0:2], us, h)
-            weigh(g, t, h, pieces[0])
-            scatter(g, t, pieces[0])
+            scatter_fused(g, t, pieces[0], h[:, pieces[0]])
             resonance(g, t, pieces[2:3], us, h)
             weigh(g, t, h, slice(128, S))
             scatter(g, t, slice(128, S))
+            store_page(g, t)
+
+        def respond_very_first(g, t, spare, h):
+            resonance_in(g, t, pieces[0:2], [spare[:, 0:128], spare[:, 448:576]], h)
+            first = pieces[0]
+            nc.vector.tensor_tensor(wa[(g, t)][:, first], h[:, first], wa[(g, t)][:, first], MULT)
+            weigh(g, t, h, pieces[1])
+            for cols in pieces[0:2]:
+                scatter(g, t, cols)
+            resonance_in(g, t, pieces[2:3], [spare[:, 0:256]], h)
+            weigh(g, t, h, pieces[2])
+            scatter(g, t, pieces[2])
             store_page(g, t)
 
         def round_on_gpsimd(out, in_):
@@ -273,62 +318,70 @@ def tile_list_furnace_zone_checkpoint_kernel(
             nc.scalar.copy(out=dst, in_=src)
             w1q[(1, a)] = quant(gr, "w1q1%d" % a)
             if a == 0:
-                acc[(1, 2)] = [bank(b) for b in piece_banks]
+                acc[(1, 0)] = [bank(b) for b in piece_banks[1]]
             for i, cols in enumerate(pieces):
-                stage1_mm(1, 2, a, i, cols)
+                stage1_mm(1, 0, a, i, cols)
+
+        def cast1_last(e, gr):
+            cast_parity(nc.scalar.copy, 1, e, gr)
+            w1q[(1, KP - 1, e)] = quant(gr, "w1q12%d" % e, 2 * P)
 
         spare_a = slot_tile("w1raw00", [P, PACK * S], F32, "spare_a")
 
         def part(tl, i):
             return tl[:, i * S : (i + 1) * S]
 
-        gr1x = slot_tile("dealt", [P, 2 * 2048], BF16, "gr1x")
+        gr1x = slot_tile("w1raw01", [P, 2 * 2048], BF16, "gr1x")
         gr1x_f = gr1x[:].bitcast(F32)
         early = [slice(0, 192), slice(192, 384)]
         late = slice(384, S)
 
-        respond_first(0, 0, part(spare_a, 0), part(spare_a, 1))
-        respond(0, 1, part(spare_a, 2), row0(0))
+        respond_very_first(0, 0, spare_a, part(spare_a, 2))
+        stage1_tile(0, 1, piece_banks[0][0])
+        stage1_tile(0, 3, piece_banks[0][1])
+        respond(0, 2, spare_a[:, 256:768], row0(0))
         round0(0)
-        respond(0, 2, gr1x_f[:, 0:S], row0(1))
+        respond(0, 1, gr1x_f[:, 0:S], row0(2))
         cast1(0, gr1x[:, 0:2048])
-        round0(1)
-        resonance(0, 3, early, gr1x_f[:, 2 * S : 3 * S], row0(2))
-        weigh(0, 3, row0(2), slice(0, 384))
-        scatter(0, 3, early[0])
         round0(2)
+        r3_late = part(spare_a, 3)
+        nc.scalar.activation(out=r3_late[:, late], in_=acc_cols(0, 3, late), func=ACT.Square)
+        resonance(0, 3, early, gr1x_f[:, 2 * S : 3 * S], row0(1))
+        nc.scalar.activation(out=r3_late[:, late], in_=r3_late[:, late], func=ACT.Abs_reciprocal_sqrt, bias=1.0)
+        weigh(0, 3, row0(1), slice(0, 384))
+        scatter(0, 3, early[0])
+        round0(1)
         cast1(1, gr1x[:, 2048:4096])
-        cast1(2, slot_tile("w1raw11", [P, 2048], BF16, "gr12")[:])
-        spare_b = slot_tile("w1raw10", [P, PACK * S], F32, "spare_b")
-        late3 = slot_tile("w1raw12", [P, 2 * S], F32, "late3")
-        resonance(0, 3, [late], part(late3, 0), part(late3, 1))
-        scatter_fused(0, 3, late, part(late3, 1)[:, late])
+        gr12 = slot_tile("w1raw11", [P, 2 * 2048], BF16, "gr12")
+        cast1_last(0, gr12[:, 0:1024])
+        for i, cols in enumerate(pieces):
+            stage1_mm(1, 0, KP - 1, i, cols)
+        h3_late = gr12[:].bitcast(F32)[:, 2 * S : 2 * S + 128]
+        nc.scalar.activation(out=h3_late, in_=r3_late[:, late], func=ACT.Square)
+        scatter_fused(0, 3, late, h3_late)
         scatter(0, 3, early[1])
         store_page(0, 3)
+        cast1_last(1, gr12[:, 1024:2048])
+        spare_b = slot_tile("w1raw10", [P, PACK * S], F32, "spare_b")
 
-        def stage1_tile(t, b):
-            acc[(1, t)] = [bank(b)]
-            for a in range(KP):
-                stage1_mm(1, t, a, 0, whole[0])
-
-        respond_first(1, 2, part(spare_b, 0), part(spare_b, 1))
-        stage1_tile(0, piece_banks[0])
-        respond(1, 0, part(spare_b, 2), row0(3))
+        respond_first(1, 0, part(spare_b, 0), part(spare_b, 1))
+        stage1_tile(1, 2, 7)
+        respond(1, 2, part(spare_b, 2), row0(3))
         round0(3)
-        stage1_tile(1, piece_banks[1])
-        respond(1, 1, part(spare_b, 3), pairs[:, T2 : T2 + S])
-        round1(2)
-        stage1_tile(3, piece_banks[2])
-        gr0 = slot_tile("w1raw02", [P, 2 * 2048], BF16, "gr0")
+        stage1_tile(1, 3, piece_banks[1][0])
+        respond(1, 3, part(spare_b, 3), pairs[:, 0:S])
+        round1(0)
+        stage1_tile(1, 1, piece_banks[1][1])
+        gr0 = slot_tile("w1raw12", [P, 2 * 2048], BF16, "gr0")
         grw1 = slot_tile("tab2", [P, 2048], BF16, "grw1")
         r_late = grw1[:].bitcast(F32)[:, 0:S]
-        nc.scalar.activation(out=r_late[:, late], in_=acc_cols(1, 3, late), func=ACT.Square)
-        resonance(1, 3, early, gr0[:].bitcast(F32)[:, 0:S], pairs[:, 0:S])
+        nc.scalar.activation(out=r_late[:, late], in_=acc_cols(1, 1, late), func=ACT.Square)
+        resonance(1, 1, early, gr0[:].bitcast(F32)[:, 0:S], pairs[:, T2 : T2 + S])
         nc.scalar.activation(out=r_late[:, late], in_=r_late[:, late], func=ACT.Abs_reciprocal_sqrt, bias=1.0)
-        weigh(1, 3, pairs[:, 0:S], slice(0, 384))
-        scatter(1, 3, slice(0, 384))
-        round1(0)
-        round1(1)
+        weigh(1, 1, pairs[:, T2 : T2 + S], slice(0, 384))
+        scatter(1, 1, slice(0, 384))
+        round1(2)
+        round1(3)
         nc.scalar.copy(
             out=gr0[:].rearrange("p (c i t) -> p c t i", i=4, t=PACK),
             in_=rounded0[:].bitcast(BF16).rearrange("p (t c i) -> p c t i", t=PACK, i=4),
@@ -345,8 +398,8 @@ def tile_list_furnace_zone_checkpoint_kernel(
         w2q = [quant(grw0[:], "w2q0")]
         h_late = slot_tile("w2raw0", [P, S], F32, "h_late")
         nc.scalar.activation(out=h_late[:, late], in_=r_late[:, late], func=ACT.Square)
-        scatter_fused(1, 3, late, h_late[:, late])
-        store_page(1, 3)
+        scatter_fused(1, 1, late, h_late[:, late])
+        store_page(1, 1)
         cast_w2(1, grw1[:])
 
         acc2 = {}
@@ -407,13 +460,13 @@ def tile_list_furnace_zone_checkpoint_kernel(
         quarters = [slice(0, HALF // 2), slice(HALF // 2, HALF)]
         second = slice(HALF, T2)
         for qs in quarters:
-            nc.vector.tensor_copy(out=pair_lane(3)[:, qs], in_=page[(1, 3)][:, qs])
+            nc.vector.tensor_copy(out=pair_lane(1)[:, qs], in_=page[(1, 1)][:, qs])
         gr = grouped_tile()
         for qs in quarters:
             weave(gr, qs)
         for qs in quarters:
             quant_page1(gr, qs)
-        nc.vector.tensor_copy(out=pair_lane(3)[:, second], in_=page[(1, 3)][:, second])
+        nc.vector.tensor_copy(out=pair_lane(1)[:, second], in_=page[(1, 1)][:, second])
         w2q.append(quant(grw1[:], "w2q1"))
         gr = grouped_tile()
         weave(gr, second)

@@ -25,6 +25,7 @@ KP = K // K_PASS
 HG = H // K_PASS
 HALF = T2 // 2
 NT = N // P
+W2_SHARE = 160
 
 
 def tile_list_furnace_zone_checkpoint_kernel(
@@ -64,10 +65,14 @@ def tile_list_furnace_zone_checkpoint_kernel(
         w2_raw = {}
         base_t = {}
 
+        def load_part_rows(dst, src):
+            for j in range(PACK):
+                nc.sync.dma_start(out=dst[:, j], in_=src[:, j])
+
         def load_w1(g, a):
             t = slot_tile("w1raw%d%d" % (g, a), [P, PACK, K_PASS], F32, "w1_raw%d%d" % (g, a))
             rows = w1[a * K_PASS : (a + 1) * K_PASS, g * K_PASS : (g + 1) * K_PASS]
-            nc.sync.dma_start(out=t[:], in_=rows.rearrange("(p j) c -> p j c", j=PACK))
+            load_part_rows(t[:], rows.rearrange("(p j) c -> p j c", j=PACK))
             w1_raw[(g, a)] = t
 
         def load_tab(a):
@@ -99,13 +104,22 @@ def tile_list_furnace_zone_checkpoint_kernel(
         nc.sync.dma_start(idx2[:], offs2)
         load_w1(0, 2)
         load_tab(2)
+        rounded0 = slot_tile("rounded0", [P, PACK * HALF], F32, "rounded0")
+        w2_rows0 = w2[0:K_PASS, :].rearrange("(p j) c -> p j c", j=PACK)
+        w2_early = rounded0[:, T2 : 2 * T2].rearrange("p (j c) -> p j c", j=PACK)
         for t in range(KP):
             load_page(0, (0, 2, 1)[t])
+            if t == KP - 1:
+                load_part_rows(w2_early, w2_rows0[:, :, 0 : N // 2])
             load_w1(1, t)
         load_page(0, 3)
-        for t in (0, 2, 3, 1):
-            load_page(1, t)
-        load_w2(0)
+        load_page(1, 0)
+        load_page(1, 2)
+        load_w2(1)
+        load_page(1, 3)
+        load_page(1, 1)
+        w2_late = slot_tile("w2raw0", [P, PACK, N // 2], F32, "w2_late")
+        load_part_rows(w2_late[:], w2_rows0[:, :, N // 2 : N])
         w3_w = keep.tile([P, HG, 2 * N], U8, name="w3_w", align_bytes=64)
         nc.sync.dma_start(out=w3_w[:].bitcast(I32), in_=w3_words.bitcast(I32).rearrange("g p c -> p g c"))
         for q in range(4):
@@ -113,7 +127,6 @@ def tile_list_furnace_zone_checkpoint_kernel(
                 out=w3_sc[32 * q : 32 * q + 4, :, :].bitcast(I32),
                 in_=w3_scales[:, 4 * q : 4 * q + 4, :].bitcast(I32).rearrange("g r c -> r g c"),
             )
-        load_w2(1)
         for nt in range(NT):
             base_t[nt] = keep.tile([P, T2], F32, name="base%d" % nt)
             nc.sync.dma_start(out=base_t[nt][:], in_=base[nt * P : (nt + 1) * P, :])
@@ -154,10 +167,9 @@ def tile_list_furnace_zone_checkpoint_kernel(
             src = w1_raw[(g, a)][:].rearrange("p j (m t) -> p m j t", t=PACK)
             return dst, src
 
-        def cast_w2(g, gr):
+        def cast_w2(raw, gr):
             dst = gr.rearrange("p (c i j) -> p c j i", i=4, j=PACK)
-            src = w2_raw[g][:].rearrange("p j (c i) -> p c j i", i=4)
-            nc.scalar.copy(out=dst, in_=src)
+            nc.scalar.copy(out=dst, in_=raw.rearrange("p j (c i) -> p c j i", i=4))
 
         def quant(gr, name, words=512, slot=None):
             codes = slot_tile(slot or name, [P, words], U32, name + "_c")
@@ -296,12 +308,15 @@ def tile_list_furnace_zone_checkpoint_kernel(
         def round_on_gpsimd(out, in_):
             nc.gpsimd.tensor_scalar(out, in_, 1.0, -0.0, MULT, ADD)
 
-        rounded0 = slot_tile("rounded0", [P, PACK * HALF], F32, "rounded0")
         pairs = keep.tile([P, 2 * T2], F32, name="pairs")
         pq_s = keep.tile([P, HG, T2], U8, name="pq_s", align_bytes=64)
 
+        def cast_w2_gpsimd(raw, gr):
+            round_on_gpsimd(gr.rearrange("p (c j) -> p c j", j=PACK), raw.rearrange("p j c -> p c j"))
+
         def row0(t):
-            return rounded0[:, t * HALF : (t + 1) * HALF]
+            place = t // 2 + 2 * (t % 2)
+            return rounded0[:, place * HALF : (place + 1) * HALF]
 
         def pair_lane(t):
             words = pairs[:, (t // 2) * T2 : (t // 2 + 1) * T2]
@@ -346,10 +361,14 @@ def tile_list_furnace_zone_checkpoint_kernel(
         round0(2)
         r3_late = part(spare_a, 3)
         nc.scalar.activation(out=r3_late[:, late], in_=acc_cols(0, 3, late), func=ACT.Square)
-        resonance(0, 3, early, gr1x_f[:, 2 * S : 3 * S], row0(1))
+        grw0 = slot_tile("tab2", [P, 2048], BF16, "grw0")
+        h03 = grw0[:].bitcast(F32)[:, 0:S]
+        resonance(0, 3, early, gr1x_f[:, 2 * S : 3 * S], h03)
         nc.scalar.activation(out=r3_late[:, late], in_=r3_late[:, late], func=ACT.Abs_reciprocal_sqrt, bias=1.0)
-        weigh(0, 3, row0(1), slice(0, 384))
+        weigh(0, 3, h03, slice(0, 384))
         scatter(0, 3, early[0])
+        for c in range(0, N // 2, 128):
+            cast_w2_gpsimd(w2_early[:, :, c : c + 128], grw0[:, PACK * c : PACK * (c + 128)])
         round0(1)
         cast1(1, gr1x[:, 2048:4096])
         gr12 = slot_tile("w1raw11", [P, 2 * 2048], BF16, "gr12")
@@ -364,7 +383,10 @@ def tile_list_furnace_zone_checkpoint_kernel(
         cast1_last(1, gr12[:, 1024:2048])
         spare_b = slot_tile("w1raw10", [P, PACK * S], F32, "spare_b")
 
-        respond_first(1, 0, part(spare_b, 0), part(spare_b, 1))
+        grw1 = slot_tile("grw1", [P, 2048], BF16, "grw1")
+        grw1_f = grw1[:].bitcast(F32)
+        respond_first(1, 0, part(spare_b, 0), grw1_f[:, 0:S])
+        cast_w2_gpsimd(w2_raw[1][:, :, 0:W2_SHARE], grw1[:, 0 : PACK * W2_SHARE])
         stage1_tile(1, 2, 7)
         respond(1, 2, part(spare_b, 2), row0(3))
         round0(3)
@@ -373,34 +395,46 @@ def tile_list_furnace_zone_checkpoint_kernel(
         round1(0)
         stage1_tile(1, 1, piece_banks[1][1])
         gr0 = slot_tile("w1raw12", [P, 2 * 2048], BF16, "gr0")
-        grw1 = slot_tile("tab2", [P, 2048], BF16, "grw1")
-        r_late = grw1[:].bitcast(F32)[:, 0:S]
-        nc.scalar.activation(out=r_late[:, late], in_=acc_cols(1, 1, late), func=ACT.Square)
-        resonance(1, 1, early, gr0[:].bitcast(F32)[:, 0:S], pairs[:, T2 : T2 + S])
-        nc.scalar.activation(out=r_late[:, late], in_=r_late[:, late], func=ACT.Abs_reciprocal_sqrt, bias=1.0)
+        gr0_f = gr0[:].bitcast(F32)
+        r_late = gr0_f[:, 1024 : 1024 + 128]
+        u_late = grw1_f[:, 896:1024]
+        nc.scalar.activation(out=u_late, in_=acc_cols(1, 1, late), func=ACT.Square)
+        resonance_in(1, 1, early, [gr0_f[:, 0:192], grw0[:].bitcast(F32)[:, 512:704]], pairs[:, T2 : T2 + S])
+        nc.scalar.activation(out=r_late, in_=u_late, func=ACT.Abs_reciprocal_sqrt, bias=1.0)
         weigh(1, 1, pairs[:, T2 : T2 + S], slice(0, 384))
         scatter(1, 1, slice(0, 384))
         round1(2)
         round1(3)
-        nc.scalar.copy(
-            out=gr0[:].rearrange("p (c i t) -> p c t i", i=4, t=PACK),
-            in_=rounded0[:].bitcast(BF16).rearrange("p (t c i) -> p c t i", t=PACK, i=4),
-        )
         pq_c = [slot_tile("tab%d" % g, [P, T2], U32, "pq_c%d" % g) for g in range(HG)]
+
+        def interleave0(hf):
+            rows = rounded0[:].bitcast(BF16).rearrange("p (e u c i) -> p c u e i", e=2, u=2, i=4)
+            nc.scalar.copy(
+                out=gr0[:, hf * 2048 : (hf + 1) * 2048].rearrange("p (c i u e) -> p c u e i", i=4, u=2, e=2),
+                in_=rows[:, hf * 128 : (hf + 1) * 128],
+            )
+
+        def quant_page0(hf):
+            cols = slice(hf * HALF, (hf + 1) * HALF)
+            nc.vector.quantize_mx(
+                out=pq_c[0][:, cols].bitcast(FP8X4), scales=pq_s[:, 0, cols], in_=gr0[:, hf * 2048 : (hf + 1) * 2048]
+            )
 
         def store_codes(g):
             nc.sync.dma_start(out=out_2[g].rearrange("p m t -> p (m t)").bitcast(I32), in_=pq_c[g][:].bitcast(I32))
 
-        nc.vector.quantize_mx(out=pq_c[0][:].bitcast(FP8X4), scales=pq_s[:, 0, :], in_=gr0[:])
-        store_codes(0)
-        grw0 = slot_tile("rounded0", [P, 2048], BF16, "grw0")
-        cast_w2(0, grw0[:])
+        interleave0(0)
+        quant_page0(0)
+        cast_w2(w2_late[:], grw0[:, 1024:2048])
         w2q = [quant(grw0[:], "w2q0")]
         h_late = slot_tile("w2raw0", [P, S], F32, "h_late")
-        nc.scalar.activation(out=h_late[:, late], in_=r_late[:, late], func=ACT.Square)
+        nc.scalar.activation(out=h_late[:, late], in_=r_late, func=ACT.Square)
         scatter_fused(1, 1, late, h_late[:, late])
         store_page(1, 1)
-        cast_w2(1, grw1[:])
+        interleave0(1)
+        cast_w2(w2_raw[1][:, :, W2_SHARE:N], grw1[:, PACK * W2_SHARE : PACK * N])
+        tanh_warm = keep.tile([P, 1], F32, name="tanh_warm")
+        nc.scalar.activation(out=tanh_warm[:], in_=grw1[:, 2047:2048], func=ACT.Tanh)
 
         acc2 = {}
 
@@ -442,9 +476,9 @@ def tile_list_furnace_zone_checkpoint_kernel(
             for nt in range(NT):
                 stage2_pass(0, 0, nt, which)
 
-        def weave(gr, cols):
+        def weave(gr, cols, copy=nc.vector.tensor_copy):
             first = cols.start % HALF
-            nc.vector.tensor_copy(
+            copy(
                 out=gr[:].bitcast(F32).rearrange("p (m u) -> p m u", u=2)[:, first : first + cols.stop - cols.start],
                 in_=pairs[:].rearrange("p (u m) -> p m u", u=2)[:, cols],
             )
@@ -462,18 +496,20 @@ def tile_list_furnace_zone_checkpoint_kernel(
         for qs in quarters:
             nc.vector.tensor_copy(out=pair_lane(1)[:, qs], in_=page[(1, 1)][:, qs])
         gr = grouped_tile()
-        for qs in quarters:
-            weave(gr, qs)
+        weave(gr, quarters[0])
+        nc.vector.tensor_copy(out=pair_lane(1)[:, second], in_=page[(1, 1)][:, second])
+        weave(gr, quarters[1])
+        gr_second = grouped_tile()
+        weave(gr_second, second, nc.scalar.copy)
         for qs in quarters:
             quant_page1(gr, qs)
-        nc.vector.tensor_copy(out=pair_lane(1)[:, second], in_=page[(1, 1)][:, second])
-        w2q.append(quant(grw1[:], "w2q1"))
-        gr = grouped_tile()
-        weave(gr, second)
+        w2q.append(quant(grw1[:], "w2q1", slot="w2raw0"))
         for which in range(2):
             for nt in range(NT):
                 stage2_pass(1, 0, nt, which)
-        quant_page1(gr, second)
+        quant_page0(1)
+        store_codes(0)
+        quant_page1(gr_second, second)
         store_codes(1)
         for q in range(4):
             nc.sync.dma_start(

@@ -318,15 +318,14 @@ def tile_list_furnace_zone_checkpoint_kernel(
             place = t // 2 + 2 * (t % 2)
             return rounded0[:, place * HALF : (place + 1) * HALF]
 
-        def pair_lane(t):
-            words = pairs[:, (t // 2) * T2 : (t // 2 + 1) * T2]
-            return words.bitcast(BF16).rearrange("p (m e) -> p m e", e=2)[:, :, t % 2]
+        def row1(t):
+            return pairs[:, t * HALF : (t + 1) * HALF].bitcast(BF16)
 
         def round0(t):
             round_on_gpsimd(row0(t).bitcast(BF16), page[(0, t)][:])
 
         def round1(t):
-            round_on_gpsimd(pair_lane(t), page[(1, t)][:])
+            round_on_gpsimd(row1(t), page[(1, t)][:])
 
         def cast1(a, gr):
             dst, src = cast_views(1, a, gr)
@@ -399,9 +398,9 @@ def tile_list_furnace_zone_checkpoint_kernel(
         r_late = gr0_f[:, 1024 : 1024 + 128]
         u_late = grw1_f[:, 896:1024]
         nc.scalar.activation(out=u_late, in_=acc_cols(1, 1, late), func=ACT.Square)
-        resonance_in(1, 1, early, [gr0_f[:, 0:192], grw0[:].bitcast(F32)[:, 512:704]], pairs[:, T2 : T2 + S])
+        resonance_in(1, 1, early, [gr0_f[:, 0:192], grw0[:].bitcast(F32)[:, 512:704]], pairs[:, 1280 : 1280 + S])
         nc.scalar.activation(out=r_late, in_=u_late, func=ACT.Abs_reciprocal_sqrt, bias=1.0)
-        weigh(1, 1, pairs[:, T2 : T2 + S], slice(0, 384))
+        weigh(1, 1, pairs[:, 1280 : 1280 + S], slice(0, 384))
         scatter(1, 1, slice(0, 384))
         round1(2)
         round1(3)
@@ -477,10 +476,11 @@ def tile_list_furnace_zone_checkpoint_kernel(
                 stage2_pass(0, 0, nt, which)
 
         def weave(gr, cols, copy=nc.vector.tensor_copy):
-            first = cols.start % HALF
+            first = PACK * (cols.start % HALF)
+            rows = pairs[:].bitcast(BF16).rearrange("p (t c i) -> p c t i", t=PACK, i=4)
             copy(
-                out=gr[:].bitcast(F32).rearrange("p (m u) -> p m u", u=2)[:, first : first + cols.stop - cols.start],
-                in_=pairs[:].rearrange("p (u m) -> p m u", u=2)[:, cols],
+                out=gr[:, first : first + PACK * (cols.stop - cols.start)].rearrange("p (c i t) -> p c t i", i=4, t=PACK),
+                in_=rows[:, cols.start // 4 : cols.stop // 4],
             )
 
         def quant_page1(gr, cols):
@@ -494,10 +494,10 @@ def tile_list_furnace_zone_checkpoint_kernel(
         quarters = [slice(0, HALF // 2), slice(HALF // 2, HALF)]
         second = slice(HALF, T2)
         for qs in quarters:
-            nc.vector.tensor_copy(out=pair_lane(1)[:, qs], in_=page[(1, 1)][:, qs])
+            nc.vector.tensor_copy(out=row1(1)[:, qs], in_=page[(1, 1)][:, qs])
+        nc.scalar.copy(out=row1(1)[:, second], in_=page[(1, 1)][:, second])
         gr = grouped_tile()
         weave(gr, quarters[0])
-        nc.vector.tensor_copy(out=pair_lane(1)[:, second], in_=page[(1, 1)][:, second])
         weave(gr, quarters[1])
         gr_second = grouped_tile()
         weave(gr_second, second, nc.scalar.copy)

@@ -116,8 +116,8 @@ def tile_list_furnace_zone_checkpoint_kernel(
         load_page(1, 0)
         load_page(1, 2)
         load_w2(1)
-        load_page(1, 3)
         load_page(1, 1)
+        load_page(1, 3)
         w2_late = slot_tile("w2raw0", [P, PACK, N // 2], F32, "w2_late")
         load_part_rows(w2_late[:], w2_rows0[:, :, N // 2 : N])
         w3_w = keep.tile([P, HG, 2 * N], U8, name="w3_w", align_bytes=64)
@@ -389,21 +389,21 @@ def tile_list_furnace_zone_checkpoint_kernel(
         stage1_tile(1, 2, 7)
         respond(1, 2, part(spare_b, 2), row0(3))
         round0(3)
-        stage1_tile(1, 3, piece_banks[1][0])
-        respond(1, 3, part(spare_b, 3), pairs[:, 0:S])
+        stage1_tile(1, 1, piece_banks[1][0])
+        respond(1, 1, part(spare_b, 3), pairs[:, 0:S])
         round1(0)
-        stage1_tile(1, 1, piece_banks[1][1])
+        stage1_tile(1, 3, piece_banks[1][1])
         gr0 = slot_tile("w1raw12", [P, 2 * 2048], BF16, "gr0")
         gr0_f = gr0[:].bitcast(F32)
         r_late = gr0_f[:, 1024 : 1024 + 128]
         u_late = grw1_f[:, 896:1024]
-        nc.scalar.activation(out=u_late, in_=acc_cols(1, 1, late), func=ACT.Square)
-        resonance_in(1, 1, early, [gr0_f[:, 0:192], grw0[:].bitcast(F32)[:, 512:704]], pairs[:, 1280 : 1280 + S])
+        nc.scalar.activation(out=u_late, in_=acc_cols(1, 3, late), func=ACT.Square)
+        resonance_in(1, 3, early, [gr0_f[:, 0:192], grw0[:].bitcast(F32)[:, 512:704]], pairs[:, 768 : 768 + S])
         nc.scalar.activation(out=r_late, in_=u_late, func=ACT.Abs_reciprocal_sqrt, bias=1.0)
-        weigh(1, 1, pairs[:, 1280 : 1280 + S], slice(0, 384))
-        scatter(1, 1, slice(0, 384))
+        weigh(1, 3, pairs[:, 768 : 768 + S], slice(0, 384))
+        scatter(1, 3, slice(0, 384))
         round1(2)
-        round1(3)
+        round1(1)
         pq_c = [slot_tile("tab%d" % g, [P, T2], U32, "pq_c%d" % g) for g in range(HG)]
 
         def interleave0(hf):
@@ -428,8 +428,8 @@ def tile_list_furnace_zone_checkpoint_kernel(
         w2q = [quant(grw0[:], "w2q0")]
         h_late = slot_tile("w2raw0", [P, S], F32, "h_late")
         nc.scalar.activation(out=h_late[:, late], in_=r_late, func=ACT.Square)
-        scatter_fused(1, 1, late, h_late[:, late])
-        store_page(1, 1)
+        scatter_fused(1, 3, late, h_late[:, late])
+        store_page(1, 3)
         interleave0(1)
         cast_w2(w2_raw[1][:, :, W2_SHARE:N], grw1[:, PACK * W2_SHARE : PACK * N])
         tanh_warm = keep.tile([P, 1], F32, name="tanh_warm")
@@ -437,8 +437,8 @@ def tile_list_furnace_zone_checkpoint_kernel(
 
         acc2 = {}
 
-        def stage2_pass(g, hf, nt, which):
-            cols = slice(hf * HALF, (hf + 1) * HALF)
+        def stage2_pass(g, hf, nt, which, part=slice(0, HALF)):
+            cols = slice(hf * HALF + part.start, hf * HALF + part.stop)
             if g == 0:
                 acc2[(hf, nt, which)] = bank(2 * nt + which)
             if which == 0:
@@ -448,13 +448,13 @@ def tile_list_furnace_zone_checkpoint_kernel(
                 lhsT = w2q[g][0][:, nt * P : (nt + 1) * P].bitcast(FP8X4)
                 lhsT_scale = w2q[g][1][:, nt * P : (nt + 1) * P]
             nc.tensor.matmul_mx(
-                out=acc2[(hf, nt, which)][:],
+                out=acc2[(hf, nt, which)][:, part],
                 lhsT=lhsT,
                 lhsT_scale=lhsT_scale,
                 rhs=pq_c[g][:, cols].bitcast(FP8X4),
                 rhs_scale=pq_s[:, g, cols],
                 start=(g == 0),
-                stop=(g == HG - 1),
+                stop=(g == HG - 1 and part.stop == HALF),
             )
 
         th_all = [slot_tile("w1raw1%d" % hf, [P, NT * HALF], F32, "th%d" % hf) for hf in range(2)]
@@ -494,8 +494,8 @@ def tile_list_furnace_zone_checkpoint_kernel(
         quarters = [slice(0, HALF // 2), slice(HALF // 2, HALF)]
         second = slice(HALF, T2)
         for qs in quarters:
-            nc.vector.tensor_copy(out=row1(1)[:, qs], in_=page[(1, 1)][:, qs])
-        nc.scalar.copy(out=row1(1)[:, second], in_=page[(1, 1)][:, second])
+            nc.vector.tensor_copy(out=row1(3)[:, qs], in_=page[(1, 3)][:, qs])
+        nc.scalar.copy(out=row1(3)[:, second], in_=page[(1, 3)][:, second])
         gr = grouped_tile()
         weave(gr, quarters[0])
         weave(gr, quarters[1])
@@ -503,10 +503,11 @@ def tile_list_furnace_zone_checkpoint_kernel(
         weave(gr_second, second, nc.scalar.copy)
         for qs in quarters:
             quant_page1(gr, qs)
-        w2q.append(quant(grw1[:], "w2q1", slot="w2raw0"))
-        for which in range(2):
             for nt in range(NT):
-                stage2_pass(1, 0, nt, which)
+                stage2_pass(1, 0, nt, 0, qs)
+        w2q.append(quant(grw1[:], "w2q1", slot="w2raw0"))
+        for nt in range(NT):
+            stage2_pass(1, 0, nt, 1)
         quant_page0(1)
         store_codes(0)
         quant_page1(gr_second, second)

@@ -385,13 +385,13 @@ def tile_list_furnace_zone_checkpoint_kernel(
         grw1 = slot_tile("grw1", [P, 2048], BF16, "grw1")
         grw1_f = grw1[:].bitcast(F32)
         respond_first(1, 0, part(spare_b, 0), grw1_f[:, 0:S])
-        cast_w2_gpsimd(w2_raw[1][:, :, 0:W2_SHARE], grw1[:, 0 : PACK * W2_SHARE])
         stage1_tile(1, 2, 7)
         respond(1, 2, part(spare_b, 2), row0(3))
         round0(3)
         stage1_tile(1, 1, piece_banks[1][0])
-        respond(1, 1, part(spare_b, 3), pairs[:, 0:S])
+        respond(1, 1, grw1_f[:, 0:S], pairs[:, 0:S])
         round1(0)
+        cast_w2_gpsimd(w2_raw[1][:, :, 0:W2_SHARE], grw1[:, 0 : PACK * W2_SHARE])
         stage1_tile(1, 3, piece_banks[1][1])
         gr0 = slot_tile("w1raw12", [P, 2 * 2048], BF16, "gr0")
         gr0_f = gr0[:].bitcast(F32)

from contextlib import ExitStack

import concourse.mybir as mybir
from concourse.masks import make_identity

K, T, S, T2, H, N = 1536, 2048, 512, 1024, 1024, 512
FLOPS = 2 * K * H * S + 2 * 2 * H * N * T2

F32 = mybir.dt.float32
BF16 = mybir.dt.bfloat16
I32 = mybir.dt.int32
U32 = mybir.dt.uint32
U16 = mybir.dt.uint16
U8 = mybir.dt.uint8
FP8X4 = mybir.dt.float8_e4m3fn_x4
FP4X4 = mybir.dt.float4_e2m1fn_x4
ACT = mybir.ActivationFunctionType
MULT = mybir.AluOpType.mult
ADD = mybir.AluOpType.add

P = 128
PACK = 4
K_PASS = P * PACK
KP = K // K_PASS
HG = H // K_PASS
HALF = T2 // 2
NT = N // P
W2_SHARE = 160


def tile_list_furnace_zone_checkpoint_kernel(
    tc, tab_words, tab_scales, offs, offs2, w1, amp, wgs, page0, w2, w3_words, w3_scales, base,
    out_0, out_1, out_2, out_3,
):
    nc = tc.nc
    with ExitStack() as ctx:
        lists = ctx.enter_context(tc.tile_pool(name="lists", bufs=1))
        keep = ctx.enter_context(tc.tile_pool(name="keep", bufs=1))
        psum = ctx.enter_context(tc.psum_pool(name="psum", bufs=1))

        def bank(b):
            return psum.tile([P, 512], F32, name="bank%d" % b, tag="bank%d" % b)

        def slot_tile(slot, shape, dtype, name):
            return keep.tile(shape, dtype, name=name, tag=slot, align_bytes=64)

        tab_sc = slot_tile("chain", [P, T], U8, "tab_sc")
        nc.vector.memset(tab_sc[:].bitcast(I32), 0)
        w3_sc = keep.tile([P, HG, N], U8, name="w3_sc", align_bytes=64)
        nc.vector.memset(w3_sc[:].bitcast(I32), 0)
        for q in range(4):
            nc.gpsimd.dma_start(
                out=tab_sc[32 * q : 32 * q + 4 * KP, :].bitcast(I32),
                in_=tab_scales[:, 4 * q : 4 * q + 4, :].bitcast(I32),
            )
        ident = keep.tile([P, P], F32, name="ident")
        make_identity(nc, ident[:])
        amp_t = keep.tile([P, HG, PACK], F32, name="amp_t")

        idx = lists.tile([P, S // 16], U16, name="idx")
        idx2 = lists.tile([P, S // 16], U16, name="idx2")
        w1_raw = {}
        tab = {}
        page = {}
        w2_raw = {}
        base_t = {}

        def load_part_rows(dst, src):
            for j in range(PACK):
                nc.sync.dma_start(out=dst[:, j], in_=src[:, j])

        def load_w1(g, a):
            t = slot_tile("w1raw%d%d" % (g, a), [P, PACK, K_PASS], F32, "w1_raw%d%d" % (g, a))
            rows = w1[a * K_PASS : (a + 1) * K_PASS, g * K_PASS : (g + 1) * K_PASS]
            load_part_rows(t[:], rows.rearrange("(p j) c -> p j c", j=PACK))
            w1_raw[(g, a)] = t

        def load_tab(a):
            t = slot_tile("tab%d" % a, [P, T], U32, "tab%d" % a)
            nc.sync.dma_start(out=t[:].bitcast(I32), in_=tab_words[a].rearrange("p n t -> p (n t)").bitcast(I32))
            tab[a] = t

        page0_v = page0.rearrange("(g p t) m -> g t p m", g=HG, t=PACK)
        out1_v = out_1.rearrange("(g p t) m -> g t p m", g=HG, t=PACK)

        def load_page(g, t):
            tl = keep.tile([P, T2], F32, name="page%d%d" % (g, t))
            nc.sync.dma_start(out=tl[:], in_=page0_v[g, t])
            page[(g, t)] = tl

        def load_w2(g):
            t = slot_tile("w2raw%d" % g, [P, PACK, N], F32, "w2_raw%d" % g)
            nc.sync.dma_start(out=t[:], in_=w2[g * K_PASS : (g + 1) * K_PASS, :].rearrange("(p j) c -> p j c", j=PACK))
            w2_raw[g] = t

        wgs_t = keep.tile([P, S], F32, name="wgs_t")
        nc.sync.dma_start(out=wgs_t[:], in_=wgs)
        load_w1(0, 0)
        nc.sync.dma_start(idx[:], offs)
        nc.sync.dma_start(out=amp_t[:], in_=amp.rearrange("(g p t) -> p g t", g=HG, t=PACK))
        load_tab(0)
        load_w1(0, 1)
        load_tab(1)
        nc.sync.dma_start(idx2[:], offs2)
        load_w1(0, 2)
        load_tab(2)
        rounded0 = slot_tile("rounded0", [P, PACK * HALF], F32, "rounded0")
        w2_rows0 = w2[0:K_PASS, :].rearrange("(p j) c -> p j c", j=PACK)
        w2_early = rounded0[:, T2 : 2 * T2].rearrange("p (j c) -> p j c", j=PACK)
        for t in range(KP):
            load_page(0, (0, 2, 1)[t])
            if t == KP - 1:
                load_part_rows(w2_early, w2_rows0[:, :, 0 : N // 2])
            load_w1(1, t)
        load_page(0, 3)
        load_page(1, 0)
        load_page(1, 2)
        load_w2(1)
        load_page(1, 1)
        load_page(1, 3)
        w2_late = slot_tile("w2raw0", [P, PACK, N // 2], F32, "w2_late")
        load_part_rows(w2_late[:], w2_rows0[:, :, N // 2 : N])
        w3_w = keep.tile([P, HG, 2 * N], U8, name="w3_w", align_bytes=64)
        nc.sync.dma_start(out=w3_w[:].bitcast(I32), in_=w3_words.bitcast(I32).rearrange("g p c -> p g c"))
        for q in range(4):
            nc.sync.dma_start(
                out=w3_sc[32 * q : 32 * q + 4, :, :].bitcast(I32),
                in_=w3_scales[:, 4 * q : 4 * q + 4, :].bitcast(I32).rearrange("g r c -> r g c"),
            )
        for nt in range(NT):
            base_t[nt] = keep.tile([P, T2], F32, name="base%d" % nt)
            nc.sync.dma_start(out=base_t[nt][:], in_=base[nt * P : (nt + 1) * P, :])

        warm = keep.tile([P, 1], F32, name="warm")
        nc.scalar.activation(out=warm[:], in_=ident[:, 0:1], func=ACT.Abs_reciprocal_sqrt, bias=1.0)

        dealt = [slot_tile("dealt%d" % i, [P, 2, PACK, 4, 32], F32, "dealt%d" % i) for i in range(2)]
        for jb, b in enumerate((0, 1, 4, 5)):
            wgs_T = bank(b)
            nc.tensor.transpose(wgs_T[:, 0:P], wgs_t[:, jb * P : (jb + 1) * P], ident[:])
            rows = wgs_T[:, 0:P].rearrange("j (p t) -> j t p", t=PACK)
            nc.scalar.copy(out=dealt[jb // 2][:, jb % 2], in_=rows.unsqueeze(2).to_broadcast([P, PACK, 4, 32]))
        wa = {}
        back = []
        for t, b in enumerate((2, 3, 6, 7)):
            back.append(bank(b))
            for jb in range(4):
                nc.tensor.transpose(
                    back[t][:, jb * P : (jb + 1) * P],
                    dealt[jb // 2][:, jb % 2, t, :, :].rearrange("j q p -> j (q p)"),
                    ident[:],
                )

        def weights(g, tile):
            for t in range(PACK):
                wa[(g, t)] = tile[:, t * S : (t + 1) * S]
                nc.scalar.activation(out=wa[(g, t)], in_=back[t][:], func=ACT.Copy, scale=amp_t[:, g, t : t + 1])

        for g in range(HG):
            weights(g, keep.tile([P, PACK * S], F32, name="wa%d" % g))

        def grouped_tile():
            return keep.tile([P, 4 * 512], BF16, name="grouped", tag="grouped", bufs=2, align_bytes=64)

        def cast_views(g, a, gr):
            dst = gr.rearrange("p (t m j) -> p m j t", t=PACK, j=PACK)
            src = w1_raw[(g, a)][:].rearrange("p j (m t) -> p m j t", t=PACK)
            return dst, src

        def cast_w2(raw, gr):
            dst = gr.rearrange("p (c i j) -> p c j i", i=4, j=PACK)
            nc.scalar.copy(out=dst, in_=raw.rearrange("p j (c i) -> p c j i", i=4))

        def quant(gr, name, words=512, slot=None):
            codes = slot_tile(slot or name, [P, words], U32, name + "_c")
            scales = keep.tile([P, words], U8, name=name + "_s", align_bytes=64)
            nc.vector.quantize_mx(out=codes[:].bitcast(FP8X4), scales=scales[:], in_=gr)
            return codes, scales

        v_w = []
        w1q = {}
        whole = [slice(0, S)]
        pieces = [slice(0, 128), slice(128, 256), slice(256, S)]
        piece_banks = ((0, 4, 5), (2, 3, 6))
        acc = {}

        def stage1_mm(g, t, a, i, cols):
            if a == KP - 1:
                wq, place = w1q[(g, a, t % 2)], t // 2
            else:
                wq, place = w1q[(g, a)], t
            nc.tensor.matmul_mx(
                out=acc[(g, t)][i][:, 0 : cols.stop - cols.start],
                lhsT=wq[0][:, place * P : (place + 1) * P].bitcast(FP8X4),
                lhsT_scale=wq[1][:, place * P : (place + 1) * P],
                rhs=v_w[a][:, cols].bitcast(FP8X4),
                rhs_scale=v_sc[4 * a : P, cols],
                start=(a == 0),
                stop=(a == KP - 1),
            )

        def stage1_tile(g, t, b):
            acc[(g, t)] = [bank(b)]
            for a in range(KP):
                stage1_mm(g, t, a, 0, whole[0])

        def acc_cols(g, t, cols):
            if len(acc[(g, t)]) == 1:
                return acc[(g, t)][0][:, cols]
            i = pieces.index(cols)
            return acc[(g, t)][i][:, 0 : cols.stop - cols.start]

        def cast0(a, slot):
            gr = slot_tile(slot, [P, 2048], BF16, "gr0%d" % a)
            dst, src = cast_views(0, a, gr[:])
            nc.vector.tensor_copy(out=dst, in_=src)
            w1q[(0, a)] = quant(gr[:], "w1q0%d" % a)

        def cast_parity(copy, g, e, gr):
            src = w1_raw[(g, KP - 1)][:].rearrange("p j (m u e) -> p e m j u", u=2, e=2)[:, e]
            copy(out=gr.rearrange("p (u m j) -> p m j u", u=2, j=PACK), in_=src)

        def gather(a, slot, parts):
            v_w.append(slot_tile(slot, [P, S], U32, "v_w%d" % a))
            for cols in parts:
                nc.vector.tensor_copy(
                    out=v_w[a][:, cols], in_=tab[a][:].indirect(idx[:, cols.start // 16 : cols.stop // 16])
                )

        def first_tile_pass(a):
            for i, cols in enumerate(pieces):
                stage1_mm(0, 0, a, i, cols)

        cast0(0, "grouped0")
        gather(0, "v_w0", whole)
        cast0(1, "grouped1")
        gather(1, "v_w1", whole)
        v_sc = keep.tile([P, S], U8, name="v_sc", align_bytes=64)
        nc.vector.tensor_copy(out=v_sc[:], in_=tab_sc[:].indirect(idx[:]))
        acc[(0, 0)] = [bank(b) for b in piece_banks[0]]
        acc[(0, 2)] = [bank(1)]
        for a in range(KP - 1):
            first_tile_pass(a)
            stage1_mm(0, 2, a, 0, whole[0])
        gr02 = [slot_tile(slot, [P, 1024], BF16, "gr02" + slot) for slot in ("chain", "dealt0")]
        cast_parity(nc.vector.tensor_copy, 0, 0, gr02[0][:])
        cast_parity(nc.scalar.copy, 0, 1, gr02[1][:])
        w1q[(0, 2, 0)] = quant(gr02[0][:], "w1q020", 2 * P)
        gather(2, "chain", pieces)
        first_tile_pass(2)
        stage1_mm(0, 2, 2, 0, whole[0])
        w1q[(0, 2, 1)] = quant(gr02[1][:], "w1q021", 2 * P, slot="tab2")

        def resonance_in(g, t, parts, scratch, h):
            for cols, us in zip(parts, scratch):
                nc.scalar.activation(out=us, in_=acc_cols(g, t, cols), func=ACT.Square)
            for us in scratch:
                nc.scalar.activation(out=us, in_=us, func=ACT.Abs_reciprocal_sqrt, bias=1.0)
            for cols, us in zip(parts, scratch):
                nc.scalar.activation(out=h[:, cols], in_=us, func=ACT.Square)

        def resonance(g, t, parts, us, h):
            resonance_in(g, t, parts, [us[:, cols] for cols in parts], h)

        def weigh(g, t, h, cols):
            nc.gpsimd.tensor_tensor(wa[(g, t)][:, cols], h[:, cols], wa[(g, t)][:, cols], MULT)

        def window(g, t, cols):
            return page[(g, t)][:].indirect(idx2[:, cols.start // 16 : cols.stop // 16])

        def scatter(g, t, cols):
            nc.vector.tensor_copy(out=window(g, t, cols), in_=wa[(g, t)][:, cols])

        def scatter_fused(g, t, cols, h):
            nc.vector.tensor_tensor(window(g, t, cols), h, wa[(g, t)][:, cols], MULT)

        def store_page(g, t):
            nc.sync.dma_start(out=out1_v[g, t], in_=page[(g, t)][:])

        halves = [slice(0, S // 2), slice(S // 2, S)]

        def respond(g, t, us, h):
            resonance(g, t, halves, us, h)
            weigh(g, t, h, whole[0])
            scatter(g, t, whole[0])
            store_page(g, t)

        def respond_first(g, t, us, h):
            resonance(g, t, pieces[0:2], us, h)
            scatter_fused(g, t, pieces[0], h[:, pieces[0]])
            resonance(g, t, pieces[2:3], us, h)
            weigh(g, t, h, slice(128, S))
            scatter(g, t, slice(128, S))
            store_page(g, t)

        def respond_very_first(g, t, spare, h):
            resonance_in(g, t, pieces[0:2], [spare[:, 0:128], spare[:, 448:576]], h)
            first = pieces[0]
            nc.vector.tensor_tensor(wa[(g, t)][:, first], h[:, first], wa[(g, t)][:, first], MULT)
            weigh(g, t, h, pieces[1])
            for cols in pieces[0:2]:
                scatter(g, t, cols)
            resonance_in(g, t, pieces[2:3], [spare[:, 0:256]], h)
            weigh(g, t, h, pieces[2])
            scatter(g, t, pieces[2])
            store_page(g, t)

        def round_on_gpsimd(out, in_):
            nc.gpsimd.tensor_scalar(out, in_, 1.0, -0.0, MULT, ADD)

        pairs = keep.tile([P, 2 * T2], F32, name="pairs")
        pq_s = keep.tile([P, HG, T2], U8, name="pq_s", align_bytes=64)

        def cast_w2_gpsimd(raw, gr):
            round_on_gpsimd(gr.rearrange("p (c j) -> p c j", j=PACK), raw.rearrange("p j c -> p c j"))

        def row0(t):
            place = t // 2 + 2 * (t % 2)
            return rounded0[:, place * HALF : (place + 1) * HALF]

        def row1(t):
            return pairs[:, t * HALF : (t + 1) * HALF].bitcast(BF16)

        def round0(t):
            round_on_gpsimd(row0(t).bitcast(BF16), page[(0, t)][:])

        def round1(t):
            round_on_gpsimd(row1(t), page[(1, t)][:])

        def cast1(a, gr):
            dst, src = cast_views(1, a, gr)
            nc.scalar.copy(out=dst, in_=src)
            w1q[(1, a)] = quant(gr, "w1q1%d" % a)
            if a == 0:
                acc[(1, 0)] = [bank(b) for b in piece_banks[1]]
            for i, cols in enumerate(pieces):
                stage1_mm(1, 0, a, i, cols)

        def cast1_last(e, gr):
            cast_parity(nc.scalar.copy, 1, e, gr)
            w1q[(1, KP - 1, e)] = quant(gr, "w1q12%d" % e, 2 * P)

        spare_a = slot_tile("w1raw00", [P, PACK * S], F32, "spare_a")

        def part(tl, i):
            return tl[:, i * S : (i + 1) * S]

        gr1x = slot_tile("w1raw01", [P, 2 * 2048], BF16, "gr1x")
        gr1x_f = gr1x[:].bitcast(F32)
        early = [slice(0, 192), slice(192, 384)]
        late = slice(384, S)

        respond_very_first(0, 0, spare_a, part(spare_a, 2))
        stage1_tile(0, 1, piece_banks[0][0])
        stage1_tile(0, 3, piece_banks[0][1])
        respond(0, 2, spare_a[:, 256:768], row0(0))
        round0(0)
        respond(0, 1, gr1x_f[:, 0:S], row0(2))
        cast1(0, gr1x[:, 0:2048])
        round0(2)
        r3_late = part(spare_a, 3)
        nc.scalar.activation(out=r3_late[:, late], in_=acc_cols(0, 3, late), func=ACT.Square)
        grw0 = slot_tile("tab2", [P, 2048], BF16, "grw0")
        h03 = grw0[:].bitcast(F32)[:, 0:S]
        resonance(0, 3, early, gr1x_f[:, 2 * S : 3 * S], h03)
        nc.scalar.activation(out=r3_late[:, late], in_=r3_late[:, late], func=ACT.Abs_reciprocal_sqrt, bias=1.0)
        weigh(0, 3, h03, slice(0, 384))
        scatter(0, 3, early[0])
        for c in range(0, N // 2, 128):
            cast_w2_gpsimd(w2_early[:, :, c : c + 128], grw0[:, PACK * c : PACK * (c + 128)])
        round0(1)
        cast1(1, gr1x[:, 2048:4096])
        gr12 = slot_tile("w1raw11", [P, 2 * 2048], BF16, "gr12")
        cast1_last(0, gr12[:, 0:1024])
        for i, cols in enumerate(pieces):
            stage1_mm(1, 0, KP - 1, i, cols)
        h3_late = gr12[:].bitcast(F32)[:, 2 * S : 2 * S + 128]
        nc.scalar.activation(out=h3_late, in_=r3_late[:, late], func=ACT.Square)
        scatter_fused(0, 3, late, h3_late)
        scatter(0, 3, early[1])
        store_page(0, 3)
        cast1_last(1, gr12[:, 1024:2048])
        spare_b = slot_tile("w1raw10", [P, PACK * S], F32, "spare_b")

        grw1 = slot_tile("grw1", [P, 2048], BF16, "grw1")
        grw1_f = grw1[:].bitcast(F32)
        respond_first(1, 0, part(spare_b, 0), grw1_f[:, 0:S])
        stage1_tile(1, 2, 7)
        respond(1, 2, part(spare_b, 2), row0(3))
        round0(3)
        stage1_tile(1, 1, piece_banks[1][0])
        respond(1, 1, grw1_f[:, 0:S], pairs[:, 0:S])
        round1(0)
        cast_w2_gpsimd(w2_raw[1][:, :, 0:W2_SHARE], grw1[:, 0 : PACK * W2_SHARE])
        stage1_tile(1, 3, piece_banks[1][1])
        gr0 = slot_tile("w1raw12", [P, 2 * 2048], BF16, "gr0")
        gr0_f = gr0[:].bitcast(F32)
        r_late = gr0_f[:, 1024 : 1024 + 128]
        u_late = grw1_f[:, 896:1024]
        nc.scalar.activation(out=u_late, in_=acc_cols(1, 3, late), func=ACT.Square)
        resonance_in(1, 3, early, [gr0_f[:, 0:192], grw0[:].bitcast(F32)[:, 512:704]], pairs[:, 768 : 768 + S])
        nc.scalar.activation(out=r_late, in_=u_late, func=ACT.Abs_reciprocal_sqrt, bias=1.0)
        weigh(1, 3, pairs[:, 768 : 768 + S], slice(0, 384))
        scatter(1, 3, slice(0, 384))
        round1(2)
        round1(1)
        pq_c = [slot_tile("tab%d" % g, [P, T2], U32, "pq_c%d" % g) for g in range(HG)]

        def interleave0(hf):
            rows = rounded0[:].bitcast(BF16).rearrange("p (e u c i) -> p c u e i", e=2, u=2, i=4)
            nc.scalar.copy(
                out=gr0[:, hf * 2048 : (hf + 1) * 2048].rearrange("p (c i u e) -> p c u e i", i=4, u=2, e=2),
                in_=rows[:, hf * 128 : (hf + 1) * 128],
            )

        def quant_page0(hf):
            cols = slice(hf * HALF, (hf + 1) * HALF)
            nc.vector.quantize_mx(
                out=pq_c[0][:, cols].bitcast(FP8X4), scales=pq_s[:, 0, cols], in_=gr0[:, hf * 2048 : (hf + 1) * 2048]
            )

        def store_codes(g):
            nc.sync.dma_start(out=out_2[g].rearrange("p m t -> p (m t)").bitcast(I32), in_=pq_c[g][:].bitcast(I32))

        interleave0(0)
        quant_page0(0)
        cast_w2(w2_late[:], grw0[:, 1024:2048])
        w2q = [quant(grw0[:], "w2q0")]
        h_late = slot_tile("w2raw0", [P, S], F32, "h_late")
        nc.scalar.activation(out=h_late[:, late], in_=r_late, func=ACT.Square)
        scatter_fused(1, 3, late, h_late[:, late])
        store_page(1, 3)
        interleave0(1)
        cast_w2(w2_raw[1][:, :, W2_SHARE:N], grw1[:, PACK * W2_SHARE : PACK * N])
        tanh_warm = keep.tile([P, 1], F32, name="tanh_warm")
        nc.scalar.activation(out=tanh_warm[:], in_=grw1[:, 2047:2048], func=ACT.Tanh)

        acc2 = {}

        def stage2_pass(g, hf, nt, which, part=slice(0, HALF)):
            cols = slice(hf * HALF + part.start, hf * HALF + part.stop)
            if g == 0:
                acc2[(hf, nt, which)] = bank(2 * nt + which)
            if which == 0:
                lhsT = w3_w[:, g, 2 * nt * P : 2 * (nt + 1) * P].bitcast(FP4X4)
                lhsT_scale = w3_sc[:, g, nt * P : (nt + 1) * P]
            else:
                lhsT = w2q[g][0][:, nt * P : (nt + 1) * P].bitcast(FP8X4)
                lhsT_scale = w2q[g][1][:, nt * P : (nt + 1) * P]
            nc.tensor.matmul_mx(
                out=acc2[(hf, nt, which)][:, part],
                lhsT=lhsT,
                lhsT_scale=lhsT_scale,
                rhs=pq_c[g][:, cols].bitcast(FP8X4),
                rhs_scale=pq_s[:, g, cols],
                start=(g == 0),
                stop=(g == HG - 1 and part.stop == HALF),
            )

        th_all = [slot_tile("w1raw1%d" % hf, [P, NT * HALF], F32, "th%d" % hf) for hf in range(2)]
        products = {}

        def finish(hf, nt):
            th = th_all[hf][:, nt * HALF : (nt + 1) * HALF]
            nc.scalar.activation(out=th, in_=acc2[(hf, nt, 0)][:], func=ACT.Tanh)
            products[(hf, nt)] = part(spare_a, 0) if (hf, nt) == (1, 1) else th
            nc.vector.tensor_tensor(products[(hf, nt)], acc2[(hf, nt, 1)][:], th, MULT)

        def add_base(adder, hf, nt, out):
            cols = slice(hf * HALF, (hf + 1) * HALF)
            adder.tensor_tensor(out, products[(hf, nt)], base_t[nt][:, cols], ADD)
            nc.sync.dma_start(out=out_0[nt * P : (nt + 1) * P, cols], in_=out)

        for which in range(2):
            for nt in range(NT):
                stage2_pass(0, 0, nt, which)

        def weave(gr, cols, copy=nc.vector.tensor_copy):
            first = PACK * (cols.start % HALF)
            rows = pairs[:].bitcast(BF16).rearrange("p (t c i) -> p c t i", t=PACK, i=4)
            copy(
                out=gr[:, first : first + PACK * (cols.stop - cols.start)].rearrange("p (c i t) -> p c t i", i=4, t=PACK),
                in_=rows[:, cols.start // 4 : cols.stop // 4],
            )

        def quant_page1(gr, cols):
            first = PACK * (cols.start % HALF)
            nc.vector.quantize_mx(
                out=pq_c[1][:, cols].bitcast(FP8X4),
                scales=pq_s[:, 1, cols],
                in_=gr[:, first : first + PACK * (cols.stop - cols.start)],
            )

        quarters = [slice(0, HALF // 2), slice(HALF // 2, HALF)]
        second = slice(HALF, T2)
        for qs in quarters:
            nc.vector.tensor_copy(out=row1(3)[:, qs], in_=page[(1, 3)][:, qs])
        nc.scalar.copy(out=row1(3)[:, second], in_=page[(1, 3)][:, second])
        gr = grouped_tile()
        weave(gr, quarters[0])
        weave(gr, quarters[1])
        gr_second = grouped_tile()
        weave(gr_second, second, nc.scalar.copy)
        for qs in quarters:
            quant_page1(gr, qs)
            for nt in range(NT):
                stage2_pass(1, 0, nt, 0, qs)
        w2q.append(quant(grw1[:], "w2q1", slot="w2raw0"))
        for nt in range(NT):
            stage2_pass(1, 0, nt, 1)
        quant_page0(1)
        store_codes(0)
        quant_page1(gr_second, second)
        store_codes(1)
        for q in range(4):
            nc.sync.dma_start(
                out=out_3[:, 4 * q : 4 * q + 4, :].bitcast(I32).rearrange("g r m -> r g m"),
                in_=pq_s[32 * q : 32 * q + 4, :, :].bitcast(I32),
            )
        for nt in range(NT):
            finish(0, nt)
            if nt < NT - 1:
                add_base(nc.gpsimd, 0, nt, base_t[nt][:, 0:HALF])
            for which in range(2 if nt < NT - 1 else 1):
                for g in range(HG):
                    stage2_pass(g, 1, nt, which)
        nt = NT - 1
        last_b = []
        for i, qs in enumerate(quarters):
            last_b.append(bank(2 * nt + 1 - 7 * i))
            for g in range(HG):
                nc.tensor.matmul_mx(
                    out=last_b[i][:, 0 : HALF // 2],
                    lhsT=w2q[g][0][:, nt * P : (nt + 1) * P].bitcast(FP8X4),
                    lhsT_scale=w2q[g][1][:, nt * P : (nt + 1) * P],
                    rhs=pq_c[g][:, HALF + qs.start : HALF + qs.stop].bitcast(FP8X4),
                    rhs_scale=pq_s[:, g, HALF + qs.start : HALF + qs.stop],
                    start=(g == 0),
                    stop=(g == HG - 1),
                )
            if i == 0:
                finish(1, 0)
        finish(1, 1)
        add_base(nc.vector, 0, NT - 1, th_all[1][:, HALF : 2 * HALF])
        add_base(nc.vector, 1, 0, products[(0, NT - 1)])
        finish(1, 2)
        add_base(nc.vector, 1, 1, base_t[1][:, HALF:T2])
        th = th_all[1][:, nt * HALF : (nt + 1) * HALF]
        nc.scalar.activation(out=th, in_=acc2[(1, nt, 0)][:], func=ACT.Tanh)
        for i, qs in enumerate(quarters):
            nc.vector.tensor_tensor(th[:, qs], last_b[i][:, 0 : HALF // 2], th[:, qs], MULT)
        add_base(nc.vector, 1, 2, base_t[2][:, HALF:T2])
        for i, qs in enumerate(quarters):
            cols = slice(HALF + i * (HALF // 2), HALF + (i + 1) * (HALF // 2))
            nc.vector.tensor_tensor(base_t[nt][:, cols], th[:, qs], base_t[nt][:, cols], ADD)
            nc.sync.dma_start(out=out_0[nt * P : (nt + 1) * P, cols], in_=base_t[nt][:, cols])
